import numpy as np, ml_dtypes
CORES = [2,3,42,43,82,83,122,123]
N = 8
import mx_ref
BF = ml_dtypes.bfloat16
def pick(q, e):
    c = np.concatenate([q[0].reshape(128, -1, 4), np.zeros((128, 1, 4), np.uint8)], axis=1); s = np.concatenate([q[1], np.ones((16, 1), np.uint8)], axis=1)
    return (np.ascontiguousarray(c[:, e].reshape(128, -1)), np.ascontiguousarray(s[:, e]))
def join(*qs):
    return (np.concatenate([q[0] for q in qs], axis=1), np.concatenate([q[1] for q in qs], axis=1))
def put(q, e, v):
    c, s = q[0].reshape(128, -1, 4).copy(), q[1].copy(); c[:, e] = v[0].reshape(128, -1, 4); s[:, e] = v[1]
    return (c.reshape(128, -1), s)
def pk(c, s):
    return (np.ascontiguousarray(c), mx_ref.live(s))
def emit(q):
    return q[0], q[1]
def packed(v, rng):
    q = [mx_ref.quantize(np.ascontiguousarray(v[r])) for r in range(N)]
    return np.stack([a for a, b in q]), np.stack([mx_ref.plane(b, rng) for a, b in q])
def tile(rs):
    return np.stack(rs, axis=2).reshape(128, -1).astype(BF)
def f(rng, *shape):
    return mx_ref.flush((rng.standard_normal(shape, dtype=np.float32) * np.exp2(rng.integers(-2, 3, shape[:-1] + (1,)))).astype(BF))
def wide(rng, *shape, cols=0):
    v = rng.standard_normal(shape, dtype=np.float32) * np.exp2(rng.integers(-12, 13, shape)).astype(np.float32)
    if cols: v *= np.repeat(np.exp2(rng.integers(-cols, cols + 1, shape[:-2] + (1, shape[-1] // 4))) * (rng.random(shape[:-2] + (1, shape[-1] // 4)) > 0.0625), 4, axis=-1).astype(np.float32)
    return mx_ref.flush(v.astype(BF))
P, CAPP, LAST = 192, 64, 4
def times(t, v):
    return mx_ref.flush((t.astype(np.float32) * np.asarray(v, np.float32)).astype(BF))
def weights(rng, v):
    c, p = packed(times(f(rng, N, 128, 4096), v), rng)
    return {"wc": c, "ws": p}
def plain(rng):
    return {"x": f(rng, N, 128, 4 * P), "u": np.stack([f(rng, 128, 512)] * N), **weights(rng, 0.25)}
def tagged(rng, al, be, lo):
    d = plain(rng)
    x, u = np.array(d["x"]), np.array(d["u"])
    x[:, :24] = 0
    for p, v in ((0, al), (8, be), (16, lo)): x[:, p, ::4] = np.asarray(v, np.float32).astype(BF)
    u[:, :, :8] = 0
    u[:, 0, 0] = 2.0 ** 21
    u[:, 8, 4] = 2.0 ** 21
    u[:, 16, 4] = 1.0
    keep = ~np.isin(np.arange(1024) % 128, (0, 8, 16))
    return {"x": x, "u": u, **weights(rng, 0.25 * np.repeat(keep, 4))}
def setup_inputs(rng):
    return plain(rng)
def setup_inputs_ties(rng):
    return tagged(rng, rng.integers(-1, 1, (N, P)), rng.integers(-1, 1, (N, P)), np.zeros((N, P)))
def setup_inputs_near(rng):
    place = np.zeros((N, P), int) + np.arange(P)
    early = place < CAPP
    al = np.where(early, -((place + int(rng.integers(0, 2))) % 2), 4 * rng.integers(0, 2, (N, P)))
    lo = rng.integers(0, 8, (N, P))
    lo[0] = np.minimum(lo[0], 6)
    lo[1] = 7
    return tagged(rng, al, np.where(early, 0, 4), np.where(early, 0, lo))
def setup_inputs_crowd(rng):
    b = np.concatenate([[N - 1], rng.permutation(N - 2) + 1, [N]])
    a = np.where(np.roll(b, -1) > np.roll(b, -2), 16, -16)
    one = np.ones((1, P), int)
    a, b = a[:, None] * one, b[:, None] * one
    a[N - 3] = 16
    a[N - 2, P - 1] = -16
    a[N - 1, :CAPP - 1] = -16
    a[N - 1, P - 1] = -16
    b[N - 1, P - 1] = -16
    return tagged(rng, a, b, 0 * b)
def setup_inputs_huge(rng):
    d = plain(rng)
    sign = np.repeat(np.where(rng.random((N, 1, P)) < 0.25, -1.0, 1.0), 4, axis=2)
    u = np.array(d["u"])
    u[:, :, :8] = (-(1 + rng.random((128, 8))) * 2.0 ** 29).astype(np.float32).astype(BF)
    x = ((1 + rng.random((N, 128, 4 * P))) * 2.0 ** 27 * sign).astype(np.float32).astype(BF)
    return {"x": x, "u": u, **weights(rng, 0.125)}
def setup_inputs_spread(rng):
    return {**plain(rng), "x": wide(rng, N, 128, 4 * P, cols=6)}
def check_inputs(d):
    b = []
    for k in ("x", "u"):
        v = np.abs(d[k].astype(np.float32))
        if not (np.isfinite(v).all() and ((v == 0) | (v >= 2.0 ** -30) & (v <= 2.0 ** 30)).all()): b.append("a value of " + k)
    v = d["u"].astype(np.float32)
    if (v != v[:1]).any(): b.append("u isn't the same on every rank")
    return b
def reference(x, u, wc, ws):
    y, sp = np.zeros((N, 128, (LAST - 1) * P), np.float32), np.zeros((N, 1, (LAST - 1) * P), np.float32)
    oc, osc = np.zeros((N, 128, 4 * P), np.uint8), np.zeros((N, 16, P), np.uint8)
    tu = [mx_ref.quantize(np.ascontiguousarray(u[r])) for r in range(N)]
    wt = [[pick(pk(wc[r], ws[r]), np.arange(128 * m, 128 * m + 128)) for m in range(8)] for r in range(N)]
    cell = {1: [mx_ref.quantize(np.ascontiguousarray(x[r])) for r in range(N)]}
    got = {1: [mx_ref.matmul(tu[r], cell[1][r]) for r in range(N)]}
    for w in range(2, LAST + 1):
        cell[w], got[w] = [], []
        for r in range(N):
            home = [(r + k) % N for k in range(w)]
            at = [(np.arange(P) + (r + k) // N) % P for k in range(w)]
            score = np.stack([got[k][r][0] + got[w - k][home[k]][1][at[k]] for k in range(1, w)]) + np.float32(0)
            best = 1 + np.argmax(score, axis=0)
            slots, left, right = [], [], []
            for k in range(1, w):
                e = np.flatnonzero(best == k)[:CAPP]
                sp[r, 0, (w - 2) * P + e] = k
                fill = np.full(CAPP - len(e), -1)
                slots.append(np.concatenate([e, fill]))
                left.append(pick(cell[k][r], slots[-1]))
                right.append(pick(cell[w - k][home[k]], np.concatenate([at[k][e], fill])))
            a, b = join(*left), join(*right)
            z = [np.maximum(mx_ref.matmul(wt[r][t], a) + mx_ref.matmul(wt[r][4 + t], b), np.float32(0)) * np.float32(0.05) for t in range(4)]
            new = mx_ref.quantize(np.ascontiguousarray(tile(z)))
            e = np.concatenate(slots)
            used = np.flatnonzero(e >= 0)
            cell[w].append(put(cell[w - 1][r], e[used], pick(new, used)))
            got[w].append(mx_ref.matmul(tu[r], cell[w][r]))
            y[r, :, (w - 2) * P:(w - 1) * P] = got[w][r]
    for r in range(N): oc[r], osc[r] = emit(cell[LAST][r])
    return {"y": y, "oc": oc, "osc": osc, "sp": sp}

@@ -1,0 +1,492 @@
+import numpy as np
+from concourse.mybir import dt, AluOpType, AxisListType, ActivationFunctionType
+
+N, P, CAP = 8, 192, 64
+CODE = "float8_e4m3fn_x4"
+JUNK, NEW2, BDUP, C1, RA, R1B, N2, L7, LATE, K2, K1B, R2, QEND = (
+    0, 64, 128, 256, 512, 576, 704, 768, 896, 1024, 1216, 1344, 1536)
+K4 = 256
+
+SCRATCH = {}
+PART = {}
+
+
+def _buf(name, cols, dtype="float32", where="sbuf"):
+    SCRATCH[name] = (where, [128, cols], dtype)
+
+
+def _parts(buf, items):
+    at = 0
+    for name, cols in items:
+        PART[name] = (buf, at)
+        at += cols
+    _buf(buf, at)
+
+
+for _n, _c in (("A", QEND), ("K", 448), ("W", 1024), ("U", 128), ("UA", 128), ("UB", 128), ("L", P), ("S", P),
+               ("R", P), ("O", P)):
+    _buf("Q" + _n, _c, CODE)
+    _buf("S" + _n, _c, "uint8")
+for _n, _c in (("XT", 1024), ("UT", 512), ("TL", 768), ("TK", 1280), ("T4", 768)):
+    _buf(_n, _c, "bfloat16")
+for _n in range(8):
+    _buf("P%d" % _n, 512, where="psum")
+for _n, _c in (("IM", P), ("IM2", P), ("IQ", 2), ("IQ2", 2), ("QI", 12), ("QI2", 12)):
+    _buf(_n, _c, "int32")
+for _n, _c in (("O0", 8), ("O1", 8), ("O3", 12), ("OS", 12), ("OL", 12), ("OF", 12)):
+    _buf(_n, _c, "uint16")
+_parts("ROWS", [(_n, P) for _n in ("MASK", "A1R", "S2R", "WM", "WC", "WM3", "WC3")]
+       + [("RST", 3 * P), ("WMX", 3 * P), ("WCX", 3 * P), ("MD", 64), ("S1B", 128), ("MC", 128),
+          ("MCM", 128), ("MCS", 128), ("WG", 128), ("WG0", 128), ("J16", 128), ("A2R", 64), ("AL", 64), ("S2L", 80),
+          ("S1A", 80), ("MA", 80), ("MK", 64), ("SC", 64), ("WM1", 64), ("WC1", 64)])
+_parts("LISTS", [(_n, 16) for _n in (
+    "PW0", "PW", "C2B", "K2W", "C1W", "D21", "R12W", "PF", "CW", "EW", "EW2", "MW", "CUW", "AB", "AB2",
+    "OB", "O3F", "O3D", "S3D", "S3", "F0", "F1", "X1", "X2", "L0", "V0", "V1", "V2", "V3", "INV", "Q0", "Q1", "T4W",
+    "Z0", "Z2", "Z3", "Z4", "Z5", "Z6", "Z7", "Z8", "Z9", "KI", "OF0", "ONE", "CU4")]
+    + [(_n, 32) for _n in ("DW", "TD", "F12", "X3", "LP", "LS", "VT", "SH")]
+    + [("PR", 64), ("PT", 64), ("ST", 64)])
+_parts("ZERO", [("INJ", 64), ("TW", 32), ("K3D", 32), ("K3", 32), ("VAL", 32), ("SPW", 32), ("SI", 64), ("EX", 16),
+                ("CUM", 144)])
+for _n, _c in (("Y", 3 * P), ("SP2", P), ("SPT", 32), ("UP1", 24), ("LUP1", 36), ("DN2", 60), ("LDN2", 36),
+               ("UP2", 12), ("LUP2", 12)):
+    _buf(_n, _c)
+ARRIVE = ["h1c", "h1s", "r1c", "r2c", "r2s", "h2c", "h2s", "up1", "up2", "dn2", "f4c", "f4s"]
+POOL = ["s%d" % _n for _n in range(100)]
+SEMAPHORES = ARRIVE + ["sent", "st"] + POOL
+
+
+def V(name, lo, hi, step=1, rows=None):
+    name, at = PART.get(name, (name, 0))
+    return (name, at + lo, at + hi, step, rows)
+
+
+def _bank(a):
+    return a[0][0] == "P" and a[0][1:].isdigit()
+
+
+def _meet(a, b):
+    if a[0] != b[0]:
+        return False
+    if _bank(a):
+        return True
+    if a[2] <= b[1] or b[2] <= a[1]:
+        return False
+    return not (a[3] == b[3] and a[3] > 1 and (a[1] - b[1]) % a[3] != 0)
+
+
+def _emit(g, T, ops):
+    queues = {"g": g, "v": g.vector, "s": g.scalar, "t": g.tensor, "y": g.sync}
+    known = {q: set() for q in queues}
+    for i, o in enumerate(ops):
+        if o["q"] == "arr":
+            o["known"] = set()
+            continue
+        deps = []
+        for j in range(i - 1, -1, -1):
+            p = ops[j]
+            if j in known[o["q"]]:
+                continue
+            hit = any(_meet(a, b) for a in o["r"] + o["w"] for b in p["w"]) or any(_meet(a, b) for a in o["w"] for b in p["r"])
+            if o.get("acc") and p["q"] == "t":
+                hit = False
+            if not hit and p["q"] != o["q"]:
+                hit = any(_bank(a) and _meet(a, b) for a in o["r"] for b in p["r"])
+            if hit:
+                deps.append(j)
+                known[o["q"]] |= {j} | p["known"]
+        o["deps"] = deps[::-1]
+        o["known"] = set(known[o["q"]])
+        for j in deps:
+            ops[j]["used"] = True
+    last, count, total = {}, {}, {"st": 0, "sent": 0}
+    for i, o in enumerate(ops):
+        if o["q"] == "arr":
+            continue
+        q = queues[o["q"]]
+        for j in o["deps"]:
+            q.wait_ge(T.sem[ops[j]["sem"]], ops[j]["val"])
+        ins = o["fn"](q)
+        if o.get("sent"):
+            total["sent"] += o["sent"]
+        elif o.get("store"):
+            ins.then_inc(T.sem["st"], 16)
+            total["st"] += 16
+        elif o.get("used"):
+            s = [s for s in POOL if s not in last or last[s] in o["known"]][0]
+            step = 16 if o.get("dma") else 1
+            last[s] = i
+            count[s] = count.get(s, 0) + step
+            o["sem"], o["val"] = s, count[s]
+            ins.then_inc(T.sem[s], step)
+    g.wait_ge(T.sem["sent"], total["sent"])
+    g.sync.wait_ge(T.sem["st"], total["st"])
+
+
+def rank_program(g, core, T, topo):
+    r = T.rank_of(core)
+    if r is None:
+        return
+    A, ACT = AluOpType, ActivationFunctionType
+    ops = []
+    up, down, up2, down2 = [T.cores[(r + k) % N] for k in (1, -1, 2, -2)]
+    last = int(r == N - 1)
+    sh = int(r == 0)
+
+    def ap(v):
+        rows = slice(None) if v[4] is None else slice(v[4][0], v[4][1])
+        return T[v[0]][rows, v[1]:v[2]] if v[3] == 1 else T[v[0]][rows, v[1]:v[2]:v[3]]
+
+    def op(q, fn, r_, w, **k):
+        ops.append(dict(q=q, fn=fn, r=[v for v in r_ if isinstance(v, tuple)], w=w, **k))
+
+    def val(s):
+        return ap(s) if isinstance(s, tuple) else s
+
+    def tt(o, a, b, f):
+        op("v", lambda q: q.tensor_tensor(ap(o), ap(a), ap(b), f), [a, b], [o])
+
+    def ts(o, a, s1, f1, s2=None, f2=None):
+        if f2 is None:
+            op("v", lambda q: q.tensor_scalar(ap(o), ap(a), val(s1), None, f1), [a, s1], [o])
+        else:
+            op("v", lambda q: q.tensor_scalar(ap(o), ap(a), val(s1), val(s2), f1, f2), [a, s1, s2], [o])
+
+    def cp(o, a, q="v"):
+        if q == "v":
+            op("v", lambda e: e.tensor_copy(ap(o), ap(a)), [a], [o])
+        else:
+            op("s", lambda e: e.activation(ap(o), ap(a), ACT.Copy), [a], [o])
+
+    def fill(o, c):
+        op("v", lambda q: q.memset(ap(o), c), [], [o])
+
+    def scan(o, a, b, f0, f1):
+        op("v", lambda q: q.tensor_tensor_scan(ap(o), ap(a), ap(b), 0.0, f0, f1), [a, b], [o])
+
+    def flip(o, a):
+        op("v", lambda q: q.transpose(ap(o), ap(a)), [a], [o])
+
+    def iota(o, pat, base, cm, small):
+        if small:
+            op("g", lambda q: q.iota(ap(o), pat, base, cm, allow_small_or_imprecise_dtypes=True), [], [o])
+        else:
+            op("g", lambda q: q.iota(ap(o), pat, base, cm), [], [o])
+
+    def quant(b, lo, hi, tile):
+        op("v", lambda q: q.quantize_mx(ap(V("Q" + b, lo, hi)), ap(V("S" + b, lo, hi)), ap(tile)), [tile],
+           [V("Q" + b, lo, hi), V("S" + b, lo, hi)])
+
+    def mm(bank, sb, slo, mb, lo, hi, start=True, stop=True):
+        sides = [V("Q" + sb, slo, slo + 128), V("S" + sb, slo, slo + 128), V("Q" + mb, lo, hi), V("S" + mb, lo, hi)]
+        o = V("P%d" % bank, 0, hi - lo)
+        op("t", lambda q: q.matmul_mx(ap(o), ap(sides[0]), ap(sides[1]), ap(sides[2]), ap(sides[3]), start, stop),
+           sides, [o], acc=not start)
+
+    def half(right, mb, lo, hi):
+        for t in range(4):
+            mm(t, "W", 128 * t + (512 if right else 0), mb, lo, hi, start=not right, stop=right)
+
+    c05 = float(np.float32(0.05))
+
+    def relu(tile, col, lo, hi, on_v=()):
+        for t in range(4):
+            o, a = V(tile, 4 * col + t, 4 * (col + hi - lo), 4), V("P%d" % t, lo, hi)
+            if t in on_v:
+                ts(o, a, 0.0, A.max, c05, A.mult)
+            else:
+                op("s", lambda q, o=o, a=a: q.activation(ap(o), ap(a), ACT.Relu, scale=c05), [a], [o])
+
+    def pick(ob, olo, wb, wlo, whi, off):
+        n = 16 * (off[2] - off[1])
+        oq, wq, os_, ws_ = V("Q" + ob, olo, olo + n), V("Q" + wb, wlo, whi), V("S" + ob, olo, olo + n), V("S" + wb, wlo, whi)
+        op("v", lambda q: q.tensor_copy(ap(oq).bitcast(dt.uint32), ap(wq).bitcast(dt.uint32).indirect(ap(off))), [wq, off], [oq])
+        op("s", lambda q: q.activation(ap(os_), ap(ws_).indirect(ap(off)), ACT.Copy), [ws_, off], [os_])
+
+    def engines(src, dst, kind):
+        es = topo.engines(src, dst)
+        return es[-8:] if kind == "hi" else es[:8] if kind == "lo" else es
+
+    def send(dst, o, a, sem, kind):
+        rid, pid, _ = topo.addr(dst)
+        es = engines(core, dst, kind)
+        cast = (lambda v: ap(v).bitcast(dt.uint8)) if a[0][0] == "Q" else ap
+        op("g", lambda q: q.remote_dma(cast(o), cast(a), T.sem[sem], T.sem["sent"], pid, rid, sum(1 << e for e in es)),
+           [a], [], sent=len(es))
+
+    def send2(dst, ob, olo, ab, alo, n, sem, kind):
+        send(dst, V("Q" + ob, olo, olo + n), V("Q" + ab, alo, alo + n), sem + "c", kind)
+        send(dst, V("S" + ob, olo, olo + n), V("S" + ab, alo, alo + n), sem + "s", kind)
+
+    def dma(q, o, a, r_, w, store=False):
+        op(q, lambda e: e.dma_start(o, a), r_, w, dma=True, store=store)
+
+    def mask(m, at, b, lo, n):
+        tt(V(m, at, at + n), V(b, lo, lo + n), V("MASK", at % P, at % P + n), A.mult)
+
+    def turn(m, at, b, shift):
+        mask(m, at, b, shift, P - shift)
+        if shift:
+            mask(m, at + P - 1, b, 0, 1)
+
+    def fold(c, m, n):
+        scan(V(c, 0, n), V("RST", 0, n), V(m, 0, n), A.mult, A.add)
+        return V(c, 15, n, 16)
+
+    def W(name, lo=0, hi=12):
+        return V(name, lo, hi)
+
+    for b, lo, n, s, src, kind in (("QA", RA, 64, "h1c", up, "hi"), ("SA", RA, P, "h1s", up, "hi"), ("QA", R1B, 128, "r1c", up, "hi"),
+                                   ("QA", R2, P, "r2c", up2, "lo"), ("SA", R2, P, "r2s", up2, "lo"),
+                                   ("QA", N2, 64, "h2c", up, "all"), ("SA", N2, 64, "h2s", up, "all"),
+                                   ("QR", 0, P, "f4c", up, "all"), ("SR", 0, P, "f4s", up, "all"),
+                                   ("LUP1", 0, 24, "up1", down, "all"), ("LUP2", 0, 12, "up2", down, "all"),
+                                   ("LDN2", 0, 36, "dn2", up, "all")):
+        ops.append(dict(q="arr", r=[], w=[V(b, lo, lo + n)], sem=s, val=len(engines(src, core, kind))))
+
+    dma("y", T.XT[:, 0:512], T.x[:, 0:512], [], [V("XT", 0, 512)])
+    dma("s", T.XT[:, 512:768], T.x[:, 512:768], [], [V("XT", 512, 768)])
+    dma("y", T.XT[:, 768:1024], T.x[:, 0:256], [], [V("XT", 768, 1024)])
+    dma("s", T.UT[:], T.u[:], [], [V("UT", 0, 512)])
+    dma("y", T.QW[:, 0:512].bitcast(dt.uint8), T.wc[:, 0:2048], [], [V("QW", 0, 512)])
+    dma("s", T.SW[:], T.ws[:], [], [V("SW", 0, 1024)])
+    dma("y", T.QW[:, 512:1024].bitcast(dt.uint8), T.wc[:, 2048:4096], [], [V("QW", 512, 1024)])
+    iota(V("IM", 0, P), [[0, 12], [1, 16]], 128, -1, False)
+    iota(V("IQ", 0, 2), [[0, 2]], 0, 1, False)
+    iota(W("PW0"), [[16, 12]], 0, 0, True)
+    iota(V("J16", 0, 128), [[0, 8], [1, 16]], 0, 0, True)
+    fill(V("O0", 0, 8), 0)
+    fill(V("O1", 0, 8), 1)
+    fill(V("RST", 0, 3 * P), 1.0)
+    fill(V("ZERO", 0, 320), 0.0)
+    fill(V("RST", 0, 3 * P, 16), 0.0)
+    quant("A", C1, C1 + 128, V("XT", 0, 512))
+    send(down, V("QA", RA, RA + 64), V("QA", C1 + sh, C1 + sh + 64), "h1c", "hi")
+    quant("A", C1 + 128, C1 + 256, V("XT", 512, 1024))
+    send(down, V("SA", RA, RA + P), V("SA", C1 + sh, C1 + sh + P), "h1s", "hi")
+    send(down, V("QA", R1B, R1B + 128), V("QA", C1 + sh + 64, C1 + sh + P), "r1c", "hi")
+    send2(down2, "A", R2, "A", C1 + int(r < 2), P, "r2", "lo")
+    quant("A", BDUP, BDUP + 128, V("XT", 256, 768))
+    ts(V("IM2", 0, P), V("IM", 0, P), 15, A.bitwise_and)
+    ts(V("IQ2", 0, 2), V("IQ", 0, 2), 15, A.bitwise_and)
+    quant("U", 0, 128, V("UT", 0, 512))
+    cp(V("Z0", 0, 2), V("IQ2", 0, 2))
+    pick("UA", 0, "U", 0, 128, V("O0", 0, 8))
+    pick("UB", 0, "U", 0, 128, V("O1", 0, 8))
+    if last:
+        quant("A", L7, L7 + 128, V("XT", 508, 1020))
+    mm(4, "UA", 0, "A", C1, C1 + P)
+    half(False, "A", C1 - 64, C1 + 64)
+    ts(V("MASK", 0, P), V("IM2", 0, P), 0, A.is_equal)
+    cp(V("A1R", 0, P), V("P4", 0, P), "s")
+    fill(V("TL", 256, 512), 0.0)
+    ts(W("PW"), W("PW0"), V("Z0", 0, 1), A.add)
+    ts(V("WG0", 0, 128), V("J16", 0, 128), V("Z0", 0, 1), A.is_le)
+    ts(V("WG", 0, 128), V("MASK", 0, 128), 32.0, A.mult)
+    turn("WM", 0, "A1R", 0)
+    tt(V("WG", 0, 128), V("WG", 0, 128), V("WG0", 0, 128), A.add)
+    a1w = fold("WC", "WM", P)
+    ts(V("INJ", 0, 64, 16), W("PW", 0, 4), float(K2), A.add)
+    ts(W("EW"), W("PW"), float(P - 1), A.is_equal)
+    cp(W("UP1"), a1w)
+    cp(W("UP1", 16, 24), V("WC", 79, P, 16))
+    ts(W("CW", 0, 8), W("PW", 4, 12), float(1 - CAP), A.add)
+    ts(V("DW", 16, 32, 2), W("PW", 4, 12), float(K2), A.add)
+    for h in (1, 17):
+        ts(V("DW", h, h + 15, 2), W("PW", 4, 12), float(NEW2), A.add)
+    if last:
+        ts(V("MD", 0, 63), V("MASK", 0, 63), float(LATE + 1 - K2), A.mult)
+        ts(V("MD", 63, 64), V("MASK", 63, 64), float(NEW2 - K2), A.mult)
+        cp(V("AL", 0, 1), V("A1R", P - 1, P))
+        cp(V("AL", 1, 64), V("A1R", 0, 63))
+        ts(W("Z2", 0, 8), W("EW", 4, 12), float(LATE - (P - 1) - (K1B - 64)), A.mult, float(K1B - 64), A.add)
+        tt(V("DW", 0, 16, 2), W("Z2", 0, 8), W("PW", 4, 12), A.add)
+        for h in (0, 8):
+            ts(W("EW2", h, h + 8), W("EW", 4, 12), -199.0, A.mult)
+        fill(V("MC", 127, 128), 0.0)
+    else:
+        ts(V("MD", 0, 64), V("MASK", 0, 64), float(LATE - K2), A.mult)
+        ts(V("DW", 0, 16, 2), W("PW", 4, 12), float(K1B - 64), A.add)
+    pd = W("PW")
+    if sh:
+        ts(W("Z7"), W("EW"), float(-P), A.mult, 1.0, A.add)
+        tt(W("Z8"), W("Z7"), W("PW"), A.add)
+        pd = W("Z8")
+
+    half(True, "A", RA - 64, RA + 64)
+    relu("TL", 128, 64, 128, on_v=(1, 3))
+    quant("A", JUNK, JUNK + 128, V("TL", 256, 768))
+    send2(down, "A", N2, "A", NEW2, 64, "h2", "all")
+
+    mm(7, "UA", 0, "A", NEW2, NEW2 + 128)
+    mm(4, "U", 0, "A", NEW2, NEW2 + P)
+    half(False, "A", C1 + 64, C1 + P)
+    ts(W("Z3"), pd, 64.0 - last, A.is_lt, float(N2 + last - RA), A.mult)
+    ts(W("Z4"), pd, float(RA), A.add)
+    mask("WM1", 0, "P7", 0, 64)
+    cp(V("A2R", 0, 64), V("P7", 0, 64))
+    cp(W("UP1", 12, 16), fold("WC1", "WM1", 64))
+    send(up, W("LUP1", 0, 24), W("UP1", 0, 24), "up1", "all")
+    cp(V("Y", 0, P), V("P4", 0, P), "s")
+    mm(5, "UB", 0, "A", R1B, R1B + 128)
+    half(True, "A", R1B, R1B + 128)
+    tt(V("S1B", 0, 128), V("P5", 0, 128), V("A1R", 64, P), A.add)
+    mask("WMX", P + 64 - sh, "P5", 0, 128 - last)
+    relu("TK", P, 0, 128)
+    if last:
+        mm(7, "UB", 0, "A", RA, RA + 128)
+        mask("WMX", P + 63, "P7", 63, 1)
+        tt(V("S1A", 64, 65), V("P7", 63, 64), V("A1R", 63, 64), A.add)
+    half(False, "A", NEW2, NEW2 + P)
+    quant("A", K1B, K1B + 128, V("TK", 4 * P, 1280))
+    mm(6, "UB", 0, "A", R2, R2 + P)
+    half(True, "A", R2, R2 + P)
+    tt(V("S2R", 64, P), V("P6", 64, P), V("A1R", 64, P), A.add)
+    tt(V("S2L", last, 64 + last), V("P6", 0, 64), V("A2R", 0, 64), A.add)
+    tt(V("MC", 0, 128 - last), V("S1B", 0, 128 - last), V("S2R", 64, P - last), A.is_ge)
+    relu("TK", 0, 0, P)
+    if last:
+        cp(V("S2L", 0, 1), V("S2R", P - 1, P))
+    tt(V("MCM", 0, 128), V("MC", 0, 128), V("WG", 0, 128), A.mult)
+    scan(V("CUM", 16, 144), V("MC", 0, 128), V("MC", 0, 128), A.add, A.max)
+    mcs = fold("MCS", "MCM", 128)
+    ts(W("MW", 0, 8), mcs, 32.0, A.is_ge, 232.0, A.mult)
+    tt(W("CUW", 0, 8), mcs, V("CUM", 15, 128, 16), A.add)
+    quant("A", K2, K2 + P, V("TK", 0, 4 * P))
+    tt(W("AB", 0, 8), W("CUW", 0, 8), W("MW", 0, 8), A.subtract)
+    tt(W("AB", 8, 16), W("AB", 0, 8), W("CW", 0, 8), A.subtract)
+    left = L7 if last else C1 - 64
+    half(False, "A", left, left + 128)
+
+    mm(5, "UB", 0, "A", N2 - 64, N2 + 64)
+    half(True, "A", N2 - 64, N2 + 64)
+    tt(V("S1A", 0, 64), V("P5", 64, 128), V("AL" if last else "A1R", 0, 64), A.add)
+    tt(V("MA", 0, 64 + last), V("S1A", 0, 64 + last), V("S2L", 0, 64 + last), A.is_ge)
+    ma, n1, ab = V("MA", last, 64 + last), V("ONE", 8, 9), "AB"
+    op("v", lambda q: q.tensor_reduce(ap(n1), ap(ma), AxisListType.X, A.add), [ma], [n1])
+    if last:
+        ts(W("Z9", 0, 16), W("EW2", 0, 16), V("MA", 0, 1), A.mult)
+    tt(V("MK", 0, 64), ma, V("MD", 0, 64), A.mult)
+    if last:
+        tt(W("AB2", 0, 16), W("AB", 0, 16), W("Z9", 0, 16), A.add)
+        ab = "AB2"
+    ts(V("TW", 1, 16, 2), W(ab, 0, 8), n1, A.add, float(CAP - 200), A.is_le)
+    ts(V("TW", 17, 32, 2), W(ab, 8, 16), n1, A.add, 0.0, A.is_ge)
+    scan(V("SC", 0, 64), V("INJ", 0, 64), V("MK", 0, 64), A.max, A.add)
+    relu("TL", 0, 64, 128)
+    scan(V("TD", 0, 32), V("TW", 0, 32), V("DW", 0, 32), A.mult, A.max)
+    cp(W("O3", 0, 4), V("SC", 15, 64, 16))
+    tt(W("OB", 0, 8), V("TD", 1, 16, 2), V("TD", 17, 32, 2), A.max)
+    quant("A", LATE, LATE + 128, V("TL", 0, 512))
+    cp(W("O3", 4, 12), W("OB", 0, 8))
+    pick("K", 0, "A", 0, QEND, W("O3"))
+    mm(4, "UA", 0, "K", 0, P)
+    mm(7, "UB", 0, "K", 0, P)
+    mm(0, "U", 0, "K", 0, P)
+
+    o3 = W("O3F")
+    turn("WMX", 2 * P, "P6", sh)
+    turn("WM3", 0, "P4", 0)
+    fill(V("LUP1", 24, 36), 0.0)
+    cp(W("UP2"), fold("WC3", "WM3", P))
+    send(up, W("LUP2"), W("UP2"), "up2", "all")
+    turn("WMX", 0, "P7", sh)
+    if sh or last:
+        mask("WMX", P, "P5", 65, 63)
+        mask("WMX", 2 * P - 1, "P5", 64, 1)
+    else:
+        mask("WMX", P, "P5", 64, 64)
+    tt(W("DN2", 0, 36), fold("WCX", "WMX", 3 * P), W("LUP1", 0, 36), A.add)
+    m12, kd = W("DN2", 36, 48), W("DN2", 48, 60)
+    tt(m12, W("DN2"), W("DN2", 12, 24), A.max)
+    tt(kd, W("DN2", 12, 24), W("DN2"), A.is_gt)
+    send(down, W("LDN2", 0, 36), W("DN2", 24, 60), "dn2", "all")
+    cp(V("Y", P, 2 * P), V("P0", 0, P), "s")
+    o3d = o3
+    if sh:
+        cp(W("SI"), W("O3"))
+        cp(W("SI", 32, 43), W("O3", 1, 12))
+        cp(W("SI", 43, 44), W("O3", 0, 1))
+        flip(V("ST", 0, 64), V("SI", 0, 64))
+        cp(V("SH", 0, 31), V("ST", 1, 32))
+        cp(V("SH", 15, 32, 16), V("ST", 32, 64, 16))
+        flip(V("SI", 0, 32), V("SH", 0, 32))
+        o3d = W("SI")
+    cp(o3, W("O3"))
+    if last:
+        ts(W("Z5"), W("EW"), float(N2 - RA - (P - 1)), A.mult)
+        tt(W("Z6"), W("Z3"), W("Z4"), A.add)
+        tt(W("R12W"), W("Z6"), W("Z5"), A.add)
+    else:
+        tt(W("R12W"), W("Z3"), W("Z4"), A.add)
+    ts(V("F12", 0, 24, 2), pd, float(R2), A.add)
+    tt(W("F0"), W("R12W"), o3d, A.subtract)
+    ts(W("C1W"), W("PW"), float(C1), A.add)
+    tt(W("F1"), W("F0"), kd, A.mult)
+    ts(W("K2W"), W("PW"), float(K2), A.add)
+    tt(V("F12", 1, 24, 2), W("F1"), o3d, A.add)
+    dma("y", T.y[:, 0:2 * P], T.Y[:, 0:2 * P], [V("Y", 0, 2 * P), W("F0")], [], store=True)
+    tt(W("S3D"), W("LUP2"), W("DN2", 24, 36), A.add)
+    tt(V("K3D", 1, 24, 2), W("S3D"), m12, A.is_gt)
+    scan(V("X3", 0, 24), V("K3D", 0, 24), V("F12", 0, 24), A.mult, A.max)
+    cp(W("OS"), V("X3", 1, 24, 2))
+    pick("S", 0, "A", 0, QEND, W("OS"))
+    send2(down, "R", 0, "S", 0, P, "f4", "all")
+    kap, k3, l12 = W("LDN2", 24, 36), V("K3", 1, 24, 2), V("LP", 1, 24, 2)
+    ts(W("L0"), kap, float(NEW2 - C1), A.mult)
+    tt(W("S3"), W("UP2"), W("LDN2"), A.add)
+    tt(l12, W("L0"), W("C1W"), A.add)
+    tt(k3, W("S3"), W("LDN2", 12, 24), A.is_gt)
+    tt(V("LP", 0, 24, 2), o3, l12, A.subtract)
+    ts(W("V0"), kap, 255.0, A.mult, 1.0, A.add)
+    scan(V("LS", 0, 24), V("K3", 0, 24), V("LP", 0, 24), A.mult, A.add)
+    ts(W("V1"), k3, 65536.0, A.mult)
+    cp(W("OL"), V("LS", 1, 24, 2))
+    tt(W("VAL"), W("V0"), W("V1"), A.max)
+    pick("L", 0, "A", 0, QEND, W("OL"))
+    half(False, "L", 0, P)
+    flip(V("VT", 0, 32), V("VAL", 0, 32))
+    ts(W("Q0"), kap, -255.0 / 256, A.mult, 1.0, A.add)
+    scan(V("PR", 0, 32), V("RST", 0, 32), V("VT", 0, 32), A.mult, A.add)
+    ts(W("Q1"), k3, -65535.0 / 65536, A.mult, 1.0, A.add)
+    ts(V("PR", 32, 64), V("VT", 0, 32), 0.0, A.mult, V("PR", 15, 16), A.add)
+    tt(W("INV"), W("Q0"), W("Q1"), A.min)
+    flip(V("PT", 0, 64), V("PR", 0, 64))
+    ts(W("V2"), kap, 1.0, A.add)
+    scan(W("EX", 1, 12), W("PT", 32, 43), W("PT", 32, 43), A.add, A.max)
+    ts(W("V3"), k3, 3.0, A.mult)
+    tt(W("CU4"), W("EX"), W("PT"), A.add)
+    tt(W("KI"), W("V2"), W("V3"), A.max)
+    tt(W("D21"), W("CU4"), W("INV"), A.mult)
+    ts(W("PF"), W("PW"), 1.0 / K4, A.mult)
+    ts(W("O3D"), W("D21"), -0.248, A.add)
+    fill(W("C2B", 0, 4), -1.0)
+    cp(W("QI"), W("O3D"))
+    ts(W("C2B", 4, 12), W("PW", 4, 12), float(NEW2), A.add)
+    ts(W("QI2"), W("QI"), 255, A.bitwise_and)
+    tt(W("X1"), o3, W("K2W"), A.is_equal)
+    ts(W("T4W"), W("QI2"), float(CAP), A.is_le)
+    tt(W("X2"), o3, W("C2B"), A.not_equal)
+    tt(W("OF0"), W("T4W"), W("PF"), A.add)
+    tt(W("SPW", 12, 24), W("T4W"), W("KI"), A.mult)
+    tt(W("SPW"), W("X1"), W("X2"), A.add)
+    ts(W("OF"), W("OF0"), float(K4), A.mult)
+    flip(V("SPT", 0, 32), V("SPW", 0, 32))
+    dma("y", T.sp[0:1, P:3 * P], T.SPT[0:24, 0:16], [V("SPT", 0, 32)], [], store=True)
+
+    half(True, "R", 0, P)
+    relu("T4", 0, 0, P, on_v=(1, 3))
+    quant("K", K4, K4 + P, V("T4", 0, 4 * P))
+    pick("O", 0, "K", 0, K4 + P, W("OF"))
+    mm(4, "U", 0, "O", 0, P)
+    dma("y", T.oc[:, :], T.QO[:, 0:P].bitcast(dt.uint8), [V("QO", 0, P)], [], store=True)
+    for k in range(4):
+        dma("s", T.osc[4 * k:4 * k + 4, :], T.SO[32 * k:32 * k + 4, 0:P], [V("SO", 0, P)], [], store=True)
+    cp(V("Y", 2 * P, 3 * P), V("P4", 0, P))
+    dma("y", T.y[:, 2 * P:3 * P], T.Y[:, 2 * P:3 * P], [V("Y", 2 * P, 3 * P)], [], store=True)
+    ops_end = len(ops)
+    fill(V("SP2", 0, CAP, rows=(0, 32)), 1.0)
+    fill(V("SP2", CAP, P, rows=(0, 32)), 0.0)
+    dma("s", T.sp[0:1, 0:P], T.SP2[0:1, 0:P], [V("SP2", 0, P)], [], store=True)
+    at = [i for i, o in enumerate(ops) if o["q"] == "v"][0]
+    ops = ops[:at] + ops[ops_end:] + ops[at:ops_end]
+    _emit(g, T, ops)

@@ -36,14 +36,14 @@ for _n, _c in (("IM", P), ("IM2", P), ("IQ", 2), ("IQ2", 2), ("QI", 12), ("QI2",
 for _n, _c in (("O0", 8), ("O1", 8), ("O3", 12), ("OS", 12), ("OL", 12), ("OF", 12)):
     _buf(_n, _c, "uint16")
 _parts("ROWS", [(_n, P) for _n in ("MASK", "A1R", "S2R", "WM", "WC", "WM3", "WC3")]
-       + [("RST", 3 * P), ("WMX", 3 * P), ("WCX", 3 * P), ("MD", 64), ("S1B", 128), ("MC", 128),
-          ("MCM", 128), ("MCS", 128), ("WG", 128), ("WG0", 128), ("J16", 128), ("A2R", 64), ("AL", 64), ("S2L", 80),
+       + [("RST", 3 * P), ("AR", R2), ("WMX", 3 * P), ("WCX", 3 * P), ("MD", 64), ("S1B", 128), ("MC", 128),
+          ("MCM", 128), ("MCS", 128), ("WG", 128), ("WG0", 128), ("J16", 128), ("AL", 64), ("S2L", 80),
           ("S1A", 80), ("MA", 80), ("MK", 64), ("SC", 64), ("WM1", 64), ("WC1", 64)])
 _parts("LISTS", [(_n, 16) for _n in (
-    "PW0", "PW", "C2B", "K2W", "C1W", "D21", "R12W", "PF", "CW", "EW", "EW2", "MW", "CUW", "AB", "AB2",
-    "OB", "O3F", "O3D", "S3D", "S3", "F0", "F1", "X1", "X2", "L0", "V0", "V1", "V2", "V3", "INV", "Q0", "Q1", "T4W",
+    "PW0", "PW", "C2B", "K2W", "C1W", "D21", "R12W", "PF", "CW", "EW", "EW2", "MW", "CUW",
+    "O3F", "O3D", "S3D", "S3", "F0", "F1", "X1", "X2", "L0", "V0", "V1", "V2", "V3", "INV", "Q0", "Q1", "T4W",
     "Z0", "Z2", "Z3", "Z4", "Z5", "Z6", "Z7", "Z8", "Z9", "KI", "OF0", "ONE", "CU4")]
-    + [(_n, 32) for _n in ("DW", "TD", "F12", "X3", "LP", "LS", "VT", "SH")]
+    + [(_n, 32) for _n in ("AB", "R4", "TD", "F12", "X3", "LP", "LS", "VT", "SH")]
     + [("PR", 64), ("PT", 64), ("ST", 64)])
 _parts("ZERO", [("INJ", 64), ("TW", 32), ("K3D", 32), ("K3", 32), ("VAL", 32), ("SPW", 32), ("SI", 64), ("EX", 16),
                 ("CUM", 144)])
@@ -254,6 +254,9 @@ def rank_program(g, core, T, topo):
     iota(V("IQ", 0, 2), [[0, 2]], 0, 1, False)
     iota(W("PW0"), [[16, 12]], 0, 0, True)
     iota(V("J16", 0, 128), [[0, 8], [1, 16]], 0, 0, True)
+    fill(V("SP2", 0, CAP, rows=(0, 32)), 1.0)
+    fill(V("SP2", CAP, P, rows=(0, 32)), 0.0)
+    dma("s", T.sp[0:1, 0:P], T.SP2[0:1, 0:P], [V("SP2", 0, P)], [], store=True)
     fill(V("O0", 0, 8), 0)
     fill(V("O1", 0, 8), 1)
     fill(V("RST", 0, 3 * P), 1.0)
@@ -278,6 +281,7 @@ def rank_program(g, core, T, topo):
     half(False, "A", C1 - 64, C1 + 64)
     ts(V("MASK", 0, P), V("IM2", 0, P), 0, A.is_equal)
     cp(V("A1R", 0, P), V("P4", 0, P), "s")
+    cp(V("AR", BDUP, BDUP + 128), V("P4", 64, P), "s")
     fill(V("TL", 256, 512), 0.0)
     ts(W("PW"), W("PW0"), V("Z0", 0, 1), A.add)
     ts(V("WG0", 0, 128), V("J16", 0, 128), V("Z0", 0, 1), A.is_le)
@@ -289,23 +293,21 @@ def rank_program(g, core, T, topo):
     ts(W("EW"), W("PW"), float(P - 1), A.is_equal)
     cp(W("UP1"), a1w)
     cp(W("UP1", 16, 24), V("WC", 79, P, 16))
-    ts(W("CW", 0, 8), W("PW", 4, 12), float(1 - CAP), A.add)
-    ts(V("DW", 16, 32, 2), W("PW", 4, 12), float(K2), A.add)
-    for h in (1, 17):
-        ts(V("DW", h, h + 15, 2), W("PW", 4, 12), float(NEW2), A.add)
+    ts(W("CW", 0, 8), W("PW", 4, 12), float(201 - 2 * CAP), A.add)
+    ts(V("TW", 0, 32, 4), W("PW", 4, 12), float(NEW2), A.add)
+    fill(V("R4", 0, 32), 1.0)
+    fill(V("MA", 64 + last, 65 + last), float(200 - CAP))
+    fill(V("R4", 0, 32, 4), 0.0)
     if last:
         ts(V("MD", 0, 63), V("MASK", 0, 63), float(LATE + 1 - K2), A.mult)
         ts(V("MD", 63, 64), V("MASK", 63, 64), float(NEW2 - K2), A.mult)
         cp(V("AL", 0, 1), V("A1R", P - 1, P))
         cp(V("AL", 1, 64), V("A1R", 0, 63))
-        ts(W("Z2", 0, 8), W("EW", 4, 12), float(LATE - (P - 1) - (K1B - 64)), A.mult, float(K1B - 64), A.add)
-        tt(V("DW", 0, 16, 2), W("Z2", 0, 8), W("PW", 4, 12), A.add)
-        for h in (0, 8):
-            ts(W("EW2", h, h + 8), W("EW", 4, 12), -199.0, A.mult)
+        ts(W("Z2", 0, 8), W("EW", 4, 12), -1000.0, A.mult, 1000.0, A.add)
+        ts(W("EW2", 0, 8), W("EW", 4, 12), -199.0, A.mult)
         fill(V("MC", 127, 128), 0.0)
     else:
         ts(V("MD", 0, 64), V("MASK", 0, 64), float(LATE - K2), A.mult)
-        ts(V("DW", 0, 16, 2), W("PW", 4, 12), float(K1B - 64), A.add)
     pd = W("PW")
     if sh:
         ts(W("Z7"), W("EW"), float(-P), A.mult, 1.0, A.add)
@@ -323,10 +325,18 @@ def rank_program(g, core, T, topo):
     ts(W("Z3"), pd, 64.0 - last, A.is_lt, float(N2 + last - RA), A.mult)
     ts(W("Z4"), pd, float(RA), A.add)
     mask("WM1", 0, "P7", 0, 64)
-    cp(V("A2R", 0, 64), V("P7", 0, 64))
+    cp(V("AR", NEW2, NEW2 + 64), V("P7", 0, 64))
     cp(W("UP1", 12, 16), fold("WC1", "WM1", 64))
     send(up, W("LUP1", 0, 24), W("UP1", 0, 24), "up1", "all")
     cp(V("Y", 0, P), V("P4", 0, P), "s")
+    if last:
+        ts(W("Z5"), W("EW"), float(N2 - RA - (P - 1)), A.mult)
+        tt(W("Z6"), W("Z3"), W("Z4"), A.add)
+        tt(W("R12W"), W("Z6"), W("Z5"), A.add)
+    else:
+        tt(W("R12W"), W("Z3"), W("Z4"), A.add)
+    ts(V("F12", 0, 24, 2), pd, float(R2), A.add)
+    fill(V("LUP1", 24, 36), 0.0)
     mm(5, "UB", 0, "A", R1B, R1B + 128)
     half(True, "A", R1B, R1B + 128)
     tt(V("S1B", 0, 128), V("P5", 0, 128), V("A1R", 64, P), A.add)
@@ -341,11 +351,13 @@ def rank_program(g, core, T, topo):
     mm(6, "UB", 0, "A", R2, R2 + P)
     half(True, "A", R2, R2 + P)
     tt(V("S2R", 64, P), V("P6", 64, P), V("A1R", 64, P), A.add)
-    tt(V("S2L", last, 64 + last), V("P6", 0, 64), V("A2R", 0, 64), A.add)
+    tt(V("S2L", last, 64 + last), V("P6", 0, 64), V("AR", NEW2, NEW2 + 64), A.add)
     tt(V("MC", 0, 128 - last), V("S1B", 0, 128 - last), V("S2R", 64, P - last), A.is_ge)
     relu("TK", 0, 0, P)
+    mm(4, "UA", 0, "A", K1B, K1B + 128)
+    cp(V("AR", K1B, K1B + 128), V("P4", 0, 128), "s")
     if last:
-        cp(V("S2L", 0, 1), V("S2R", P - 1, P))
+        cp(V("S2L", 0, 1), V("S2R", P - 1, P), "s")
     tt(V("MCM", 0, 128), V("MC", 0, 128), V("WG", 0, 128), A.mult)
     scan(V("CUM", 16, 144), V("MC", 0, 128), V("MC", 0, 128), A.add, A.max)
     mcs = fold("MCS", "MCM", 128)
@@ -354,77 +366,76 @@ def rank_program(g, core, T, topo):
     quant("A", K2, K2 + P, V("TK", 0, 4 * P))
     tt(W("AB", 0, 8), W("CUW", 0, 8), W("MW", 0, 8), A.subtract)
     tt(W("AB", 8, 16), W("AB", 0, 8), W("CW", 0, 8), A.subtract)
+    if last:
+        tt(W("AB", 16, 24), W("AB", 0, 8), W("Z2", 0, 8), A.add)
+    dma("y", T.y[:, 0:P], T.Y[:, 0:P], [V("Y", 0, P), W("MW", 0, 8)], [], store=True)
     left = L7 if last else C1 - 64
     half(False, "A", left, left + 128)
 
     mm(5, "UB", 0, "A", N2 - 64, N2 + 64)
     half(True, "A", N2 - 64, N2 + 64)
+    mm(4, "UA", 0, "A", K2, K2 + P)
     tt(V("S1A", 0, 64), V("P5", 64, 128), V("AL" if last else "A1R", 0, 64), A.add)
     tt(V("MA", 0, 64 + last), V("S1A", 0, 64 + last), V("S2L", 0, 64 + last), A.is_ge)
-    ma, n1, ab = V("MA", last, 64 + last), V("ONE", 8, 9), "AB"
-    op("v", lambda q: q.tensor_reduce(ap(n1), ap(ma), AxisListType.X, A.add), [ma], [n1])
-    if last:
-        ts(W("Z9", 0, 16), W("EW2", 0, 16), V("MA", 0, 1), A.mult)
-    tt(V("MK", 0, 64), ma, V("MD", 0, 64), A.mult)
-    if last:
-        tt(W("AB2", 0, 16), W("AB", 0, 16), W("Z9", 0, 16), A.add)
-        ab = "AB2"
-    ts(V("TW", 1, 16, 2), W(ab, 0, 8), n1, A.add, float(CAP - 200), A.is_le)
-    ts(V("TW", 17, 32, 2), W(ab, 8, 16), n1, A.add, 0.0, A.is_ge)
-    scan(V("SC", 0, 64), V("INJ", 0, 64), V("MK", 0, 64), A.max, A.add)
+    ma, mn, nn = V("MA", last, 64 + last), V("MA", last, 65 + last), V("ONE", 8, 9)
+    op("v", lambda q: q.tensor_reduce(ap(nn), ap(mn), AxisListType.X, A.add, negate=True), [mn], [nn])
     relu("TL", 0, 64, 128)
-    scan(V("TD", 0, 32), V("TW", 0, 32), V("DW", 0, 32), A.mult, A.max)
-    cp(W("O3", 0, 4), V("SC", 15, 64, 16))
-    tt(W("OB", 0, 8), V("TD", 1, 16, 2), V("TD", 17, 32, 2), A.max)
+    if last:
+        z, e7, m0, a7 = W("Z9", 0, 1), W("EW2", 7, 8), V("MA", 0, 1), V("AB", 7, 24, 8)
+        op("s", lambda q: q.activation(ap(z), ap(e7), ACT.Identity, scale=ap(m0)), [e7, m0], [z])
+        op("s", lambda q: q.activation(ap(a7), ap(a7), ACT.Identity, bias=ap(z)), [a7, z], [a7])
+    tt(V("MK", 0, 64), ma, V("MD", 0, 64), A.mult)
     quant("A", LATE, LATE + 128, V("TL", 0, 512))
-    cp(W("O3", 4, 12), W("OB", 0, 8))
-    pick("K", 0, "A", 0, QEND, W("O3"))
-    mm(4, "UA", 0, "K", 0, P)
-    mm(7, "UB", 0, "K", 0, P)
-    mm(0, "U", 0, "K", 0, P)
+    ts(V("TW", 1, 32, 4), W("AB", 0, 8), nn, A.is_le, float(K1B - 64 - NEW2), A.mult)
+    ts(V("TW", 2, 32, 4), W("AB", 8, 16), nn, A.is_ge, float(K2 - NEW2), A.mult)
+    if last:
+        ts(V("TW", 3, 32, 4), W("AB", 16, 24), nn, A.is_le, float(LATE - (P - 1) - (K1B - 64)), A.mult)
+    mm(7, "UA", 0, "A", LATE, LATE + 128)
+    cp(V("AR", K2, K2 + P), V("P4", 0, P), "s")
+    cp(V("AR", LATE, LATE + 64), V("P7", 0, 64), "s")
+    scan(V("TD", 0, 32), V("R4", 0, 32), V("TW", 0, 32), A.mult, A.add)
+    scan(V("SC", 0, 64), V("INJ", 0, 64), V("MK", 0, 64), A.max, A.add)
+    cp(W("O3", 4, 12), V("TD", 3, 32, 4))
+    cp(W("O3", 0, 4), V("SC", 15, 64, 16))
 
     o3 = W("O3F")
-    turn("WMX", 2 * P, "P6", sh)
-    turn("WM3", 0, "P4", 0)
-    fill(V("LUP1", 24, 36), 0.0)
+    ar, m3, mk = V("AR", 0, R2), V("WM3", 0, P), V("MASK", 0, P)
+    op("v", lambda q: q.tensor_tensor(ap(m3), ap(ar).indirect(ap(W("O3"))), ap(mk), A.mult), [ar, W("O3"), mk], [m3])
     cp(W("UP2"), fold("WC3", "WM3", P))
     send(up, W("LUP2"), W("UP2"), "up2", "all")
-    turn("WMX", 0, "P7", sh)
+    pick("K", 0, "A", 0, QEND, W("O3"))
+    cp(o3, W("O3"))
+    o3d = o3
+    if sh:
+        cp(W("SI"), o3, "s")
+        cp(W("SI", 32, 43), W("O3F", 1, 12), "s")
+        cp(W("SI", 43, 44), W("O3F", 0, 1), "s")
+    mm(7, "UB", 0, "K", 0, P)
+    mm(0, "U", 0, "K", 0, P)
+    turn("WMX", 2 * P, "P6", sh)
     if sh or last:
         mask("WMX", P, "P5", 65, 63)
         mask("WMX", 2 * P - 1, "P5", 64, 1)
     else:
         mask("WMX", P, "P5", 64, 64)
+    turn("WMX", 0, "P7", sh)
+    if sh:
+        flip(V("ST", 0, 64), V("SI", 0, 64))
+        cp(V("SH", 0, 31), V("ST", 1, 32), "s")
+        cp(V("SH", 15, 32, 16), V("ST", 32, 64, 16), "s")
     tt(W("DN2", 0, 36), fold("WCX", "WMX", 3 * P), W("LUP1", 0, 36), A.add)
+    if sh:
+        flip(V("SI", 0, 32), V("SH", 0, 32))
+        o3d = W("SI")
     m12, kd = W("DN2", 36, 48), W("DN2", 48, 60)
+    tt(W("F0"), W("R12W"), o3d, A.subtract)
     tt(m12, W("DN2"), W("DN2", 12, 24), A.max)
     tt(kd, W("DN2", 12, 24), W("DN2"), A.is_gt)
     send(down, W("LDN2", 0, 36), W("DN2", 24, 60), "dn2", "all")
     cp(V("Y", P, 2 * P), V("P0", 0, P), "s")
-    o3d = o3
-    if sh:
-        cp(W("SI"), W("O3"))
-        cp(W("SI", 32, 43), W("O3", 1, 12))
-        cp(W("SI", 43, 44), W("O3", 0, 1))
-        flip(V("ST", 0, 64), V("SI", 0, 64))
-        cp(V("SH", 0, 31), V("ST", 1, 32))
-        cp(V("SH", 15, 32, 16), V("ST", 32, 64, 16))
-        flip(V("SI", 0, 32), V("SH", 0, 32))
-        o3d = W("SI")
-    cp(o3, W("O3"))
-    if last:
-        ts(W("Z5"), W("EW"), float(N2 - RA - (P - 1)), A.mult)
-        tt(W("Z6"), W("Z3"), W("Z4"), A.add)
-        tt(W("R12W"), W("Z6"), W("Z5"), A.add)
-    else:
-        tt(W("R12W"), W("Z3"), W("Z4"), A.add)
-    ts(V("F12", 0, 24, 2), pd, float(R2), A.add)
-    tt(W("F0"), W("R12W"), o3d, A.subtract)
-    ts(W("C1W"), W("PW"), float(C1), A.add)
+    dma("y", T.y[:, P:2 * P], T.Y[:, P:2 * P], [V("Y", P, 2 * P)], [], store=True)
     tt(W("F1"), W("F0"), kd, A.mult)
-    ts(W("K2W"), W("PW"), float(K2), A.add)
     tt(V("F12", 1, 24, 2), W("F1"), o3d, A.add)
-    dma("y", T.y[:, 0:2 * P], T.Y[:, 0:2 * P], [V("Y", 0, 2 * P), W("F0")], [], store=True)
     tt(W("S3D"), W("LUP2"), W("DN2", 24, 36), A.add)
     tt(V("K3D", 1, 24, 2), W("S3D"), m12, A.is_gt)
     scan(V("X3", 0, 24), V("K3D", 0, 24), V("F12", 0, 24), A.mult, A.max)
@@ -432,6 +443,8 @@ def rank_program(g, core, T, topo):
     pick("S", 0, "A", 0, QEND, W("OS"))
     send2(down, "R", 0, "S", 0, P, "f4", "all")
     kap, k3, l12 = W("LDN2", 24, 36), V("K3", 1, 24, 2), V("LP", 1, 24, 2)
+    ts(W("C1W"), W("PW"), float(C1), A.add)
+    ts(W("K2W"), W("PW"), float(K2), A.add)
     ts(W("L0"), kap, float(NEW2 - C1), A.mult)
     tt(W("S3"), W("UP2"), W("LDN2"), A.add)
     tt(l12, W("L0"), W("C1W"), A.add)
@@ -477,16 +490,12 @@ def rank_program(g, core, T, topo):
     relu("T4", 0, 0, P, on_v=(1, 3))
     quant("K", K4, K4 + P, V("T4", 0, 4 * P))
     pick("O", 0, "K", 0, K4 + P, W("OF"))
-    mm(4, "U", 0, "O", 0, P)
+    mm(4, "U", 0, "O", 0, 128)
+    mm(5, "U", 0, "O", 64, P)
     dma("y", T.oc[:, :], T.QO[:, 0:P].bitcast(dt.uint8), [V("QO", 0, P)], [], store=True)
     for k in range(4):
-        dma("s", T.osc[4 * k:4 * k + 4, :], T.SO[32 * k:32 * k + 4, 0:P], [V("SO", 0, P)], [], store=True)
-    cp(V("Y", 2 * P, 3 * P), V("P4", 0, P))
+        dma("ys"[k % 2], T.osc[4 * k:4 * k + 4, :], T.SO[32 * k:32 * k + 4, 0:P], [V("SO", 0, P)], [], store=True)
+    cp(V("Y", 2 * P, 2 * P + 112), V("P4", 0, 112), "s")
+    cp(V("Y", 2 * P + 112, 3 * P), V("P5", 48, 128))
     dma("y", T.y[:, 2 * P:3 * P], T.Y[:, 2 * P:3 * P], [V("Y", 2 * P, 3 * P)], [], store=True)
-    ops_end = len(ops)
-    fill(V("SP2", 0, CAP, rows=(0, 32)), 1.0)
-    fill(V("SP2", CAP, P, rows=(0, 32)), 0.0)
-    dma("s", T.sp[0:1, 0:P], T.SP2[0:1, 0:P], [V("SP2", 0, P)], [], store=True)
-    at = [i for i, o in enumerate(ops) if o["q"] == "v"][0]
-    ops = ops[:at] + ops[ops_end:] + ops[at:ops_end]
     _emit(g, T, ops)

@@ -6,6 +6,8 @@ CODE = "float8_e4m3fn_x4"
 JUNK, NEW2, BDUP, C1, RA, R1B, N2, L7, LATE, K2, K1B, R2, QEND = (
     0, 64, 128, 256, 512, 576, 704, 768, 896, 1024, 1216, 1344, 1536)
 K4 = 256
+HOP, LOAD, WAKE, PEEK, ROW, ISSUE, FIRST, LEAN, LAND, ON, OFF = 1.3, 1.0, 0.14, 0.02, 0.028, 0.35, 1.1, 0.05, 0.3, 30000, 21000
+AHEAD, SLACK = 0.4, 0.06
 
 SCRATCH = {}
 PART = {}
@@ -23,7 +25,7 @@ def _parts(buf, items):
     _buf(buf, at)
 
 
-for _n, _c in (("A", QEND), ("K", 448), ("W", 1024), ("U", 128), ("UA", 128), ("UB", 128), ("L", P), ("S", P),
+for _n, _c in (("A", QEND), ("K", K4 + P), ("W", 1024), ("U", 128), ("UA", 128), ("UB", 128), ("L", P), ("S", P),
                ("R", P), ("O", P)):
     _buf("Q" + _n, _c, CODE)
     _buf("S" + _n, _c, "uint8")
@@ -35,23 +37,23 @@ for _n, _c in (("IM", P), ("IM2", P), ("IQ", 2), ("IQ2", 2), ("QI", 12), ("QI2",
     _buf(_n, _c, "int32")
 for _n, _c in (("O0", 8), ("O1", 8), ("O3", 12), ("OS", 12), ("OL", 12), ("OF", 12)):
     _buf(_n, _c, "uint16")
-_parts("ROWS", [(_n, P) for _n in ("MASK", "A1R", "S2R", "WM", "WC", "WM3", "WC3")]
-       + [("RST", 3 * P), ("AR", R2), ("WMX", 3 * P), ("WCX", 3 * P), ("MD", 64), ("S1B", 128), ("MC", 128),
-          ("MCM", 128), ("MCS", 128), ("WG", 128), ("WG0", 128), ("J16", 128), ("AL", 64), ("S2L", 80),
-          ("S1A", 80), ("MA", 80), ("MK", 64), ("SC", 64), ("WM1", 64), ("WC1", 64)])
+_parts("ROWS", [(_n, P) for _n in ("MASK", "WM", "WC", "WM3", "WC3", "RST")]
+       + [("WMX", 3 * P), ("WCX", 3 * P), ("MD", 64), ("S1B", 144), ("MC", 128),
+          ("MCS", 128), ("WG", 128), ("WG0", 128), ("WG1", 128), ("S2L", 80),
+          ("MA", 80), ("MK", 64), ("SC", 64), ("WM1", 64), ("WC1", 64), ("AR", R2)])
 _parts("LISTS", [(_n, 16) for _n in (
-    "PW0", "PW", "C2B", "K2W", "C1W", "D21", "R12W", "PF", "CW", "EW", "EW2", "MW", "CUW",
-    "O3F", "O3D", "S3D", "S3", "F0", "F1", "X1", "X2", "L0", "V0", "V1", "V2", "V3", "INV", "Q0", "Q1", "T4W",
-    "Z0", "Z2", "Z3", "Z4", "Z5", "Z6", "Z7", "Z8", "Z9", "KI", "OF0", "ONE", "CU4")]
-    + [(_n, 32) for _n in ("AB", "R4", "TD", "F12", "X3", "LP", "LS", "VT", "SH")]
+    "PW0", "PW", "C2B", "K2W", "C1W", "D21", "R12W", "CW", "EW", "EW2", "MW", "CUW",
+    "O3F", "SUF", "S3D", "F0", "F1", "X1", "X2", "L0", "V0", "V1", "V2", "V3", "INV", "Q0", "Q1",
+    "Z0", "Z2", "Z3", "Z4", "Z5", "Z6", "Z7", "Z8", "Z9", "KI", "ONE", "CU4", "S1D", "S2D", "S3")]
+    + [(_n, 32) for _n in ("AB", "R4", "TD", "F12", "XS", "LP", "LS", "VT", "SH", "OFD", "OFS")]
     + [("PR", 64), ("PT", 64), ("ST", 64)])
 _parts("ZERO", [("INJ", 64), ("TW", 32), ("K3D", 32), ("K3", 32), ("VAL", 32), ("SPW", 32), ("SI", 64), ("EX", 16),
-                ("CUM", 144)])
-for _n, _c in (("Y", 3 * P), ("SP2", P), ("SPT", 32), ("UP1", 24), ("LUP1", 36), ("DN2", 60), ("LDN2", 36),
-               ("UP2", 12), ("LUP2", 12)):
+                ("T4I", 32)])
+for _n, _c in (("Y", 3 * P), ("SP2", P), ("SPT", 32), ("UP1", 16), ("LUP1", 16), ("DN2", 36), ("LDN2", 36),
+               ("UP2", 12), ("LUP2", 12), ("CUM", 128)):
     _buf(_n, _c)
-ARRIVE = ["h1c", "h1s", "r1c", "r2c", "r2s", "h2c", "h2s", "up1", "up2", "dn2", "f4c", "f4s"]
-POOL = ["s%d" % _n for _n in range(100)]
+ARRIVE = ["h1c", "h1s", "r2c", "r2s", "h2c", "h2s", "up1", "up2", "dn2", "f4c", "f4s"]
+POOL = ["s%d" % _n for _n in range(130)]
 SEMAPHORES = ARRIVE + ["sent", "st"] + POOL
 
 
@@ -72,6 +74,127 @@ def _meet(a, b):
     if a[2] <= b[1] or b[2] <= a[1]:
         return False
     return not (a[3] == b[3] and a[3] > 1 and (a[1] - b[1]) % a[3] != 0)
+
+
+def _cost(o, q):
+    if q == "g":
+        return ISSUE
+    if o.get("dma"):
+        return 0.05
+    w = o["w"][0]
+    n = len(range(w[1], w[2], w[3]))
+    if q == "t":
+        return 0.0006 * (n + 16)
+    return 0.001 * max(64, n * o.get("k", 1)) + o.get("fix", 0) + (0.02 if q == "s" else 0)
+
+
+def _order(progs):
+    ops = [o for core in progs for o in progs[core]]
+    n = len(ops)
+    pre, soft = [[] for _ in ops], [set() for _ in ops]
+    sent, at, first = {}, 0, set()
+    for core, mine in progs.items():
+        line = {}
+        for x, o in enumerate(mine):
+            i = at + x
+            o["core"], o["x"] = core, x
+            if o.get("sent"):
+                sent[o["dst"], o["name"]] = i
+                if core not in first:
+                    first.add(core)
+                    o["first"] = FIRST
+            if o["q"] == "arr":
+                continue
+            for y in range(x):
+                p = mine[y]
+                hit = any(_meet(a, b) for a in o["r"] + o["w"] for b in p["w"]) or any(_meet(a, b) for a in o["w"] for b in p["r"])
+                if not hit and (p["q"] != o["q"] or "alt" in o or "alt" in p):
+                    hit = any(_bank(a) and _meet(a, b) for a in o["r"] for b in p["r"])
+                if hit or "behind" in o and o["behind"] in p["w"]:
+                    pre[i].append(at + y)
+            if o["q"] == "g" or o.get("dma"):
+                if o["q"] in line and line[o["q"]] not in pre[i]:
+                    pre[i].append(line[o["q"]])
+                    soft[i].add(line[o["q"]])
+                line[o["q"]] = i
+            if o.get("acc"):
+                soft[i] |= {j for j in pre[i] if ops[j]["q"] == "t"}
+        at += len(mine)
+    for i, o in enumerate(ops):
+        if o["q"] == "arr":
+            pre[i] = [sent[o["core"], o["sem"]]]
+    post = [[] for _ in ops]
+    for i in range(n):
+        for j in pre[i]:
+            post[j].append(i)
+
+    def lag(o):
+        return HOP + o["busy"] if o.get("sent") else LOAD + o["busy"] if o.get("dma") else 0.0 if o["q"] == "arr" else WAKE
+    way, left, todo = [0.0] * n, [len(p) for p in post], [i for i in range(n) if not post[i]]
+    while todo:
+        i = todo.pop()
+        o = ops[i]
+        way[i] = (0.0 if o["q"] == "arr" else _cost(o, o["q"])) + max(
+            [way[k] + (0.0 if i in soft[k] else lag(o)) for k in post[i]] + [lag(o)])
+        for j in pre[i]:
+            left[j] -= 1
+            if not left[j]:
+                todo.append(j)
+    left = [len(p) for p in pre]
+    ready = {i: 0.0 for i in range(n) if not left[i]}
+    free, busy, out, can = {}, {}, {core: [] for core in progs}, [0.0] * n
+    while ready:
+        when = {}
+        for i, t in ready.items():
+            for q in [ops[i]["q"]] + (["s"] if "alt" in ops[i] else []):
+                when[i, q] = max(t, free.get((ops[i]["core"], q), 0.0))
+        t0, i0, q0 = min((t, i, q) for (i, q), t in when.items())
+        core = ops[i0]["core"]
+        mine = sorted((k for k, q in when if q == q0 and ops[k]["core"] == core and when[k, q] <= t0 + AHEAD),
+                      key=lambda k: (-way[k], k))
+        for i in mine:
+            if q0 == "arr" or when[i, q0] <= t0 + PEEK and all(
+                    when[i, q0] + _cost(ops[i], q0) + way[k] <= max(when[k, q0] + way[k] + SLACK, when[k, q0] + _cost(ops[k], q0) + way[i])
+                    for k in mine if way[k] > way[i]):
+                break
+        else:
+            i = mine[0]
+        o = ops[i]
+        q = o["q"]
+        if "alt" in o and when[i, "s"] + _cost(o, "s") <= when[i, "v"] + _cost(o, "v") + LEAN:
+            q = "s"
+        end = when[i, q]
+        if q != "arr":
+            end += _cost(o, q) + o.get("first", 0.0)
+            free[core, q] = end
+            out[core].append((o["x"], q))
+        done = end + lag(o)
+        if "busy" in o:
+            done = max([done - o["busy"]] + [busy.get((core, e), 0.0) for e in o["es"]]) + o["busy"]
+            for e in o["es"]:
+                busy[core, e] = done - (LAND if o.get("sent") else 0.0)
+        del ready[i]
+        for k in post[i]:
+            left[k] -= 1
+            can[k] = max(can[k], end if i in soft[k] else done)
+            if not left[k]:
+                ready[k] = can[k]
+    return out
+
+
+ORDER = {}
+
+
+def rank_program(g, core, T, topo):
+    if T.rank_of(core) is None:
+        return
+    if not ORDER:
+        ORDER.update(_order({c: _calls(c, T, topo) for c in T.cores}))
+    ops = _calls(core, T, topo)
+    for x, q in ORDER[core]:
+        if q != ops[x]["q"]:
+            ops[x].update(q=q, fn=ops[x]["alt"])
+    _emit(g, T, [o for o in ops if o["q"] == "arr"] + [ops[x] for x, _ in ORDER[core]])
 
 
 def _emit(g, T, ops):
@@ -122,15 +245,16 @@ def _emit(g, T, ops):
     g.sync.wait_ge(T.sem["st"], total["st"])
 
 
-def rank_program(g, core, T, topo):
+def _calls(core, T, topo):
     r = T.rank_of(core)
-    if r is None:
-        return
     A, ACT = AluOpType, ActivationFunctionType
     ops = []
     up, down, up2, down2 = [T.cores[(r + k) % N] for k in (1, -1, 2, -2)]
     last = int(r == N - 1)
     sh = int(r == 0)
+    near = topo.chip(up) == topo.chip(core)
+    hand = topo.chip(down) == topo.chip(core)
+    direct = topo.chip(down2) != topo.chip(down)
 
     def ap(v):
         rows = slice(None) if v[4] is None else slice(v[4][0], v[4][1])
@@ -142,20 +266,25 @@ def rank_program(g, core, T, topo):
     def val(s):
         return ap(s) if isinstance(s, tuple) else s
 
+    def plain(*vs):
+        return all(SCRATCH[v[0]][2] == "float32" for v in vs)
+
     def tt(o, a, b, f):
-        op("v", lambda q: q.tensor_tensor(ap(o), ap(a), ap(b), f), [a, b], [o])
+        op("v", lambda q: q.tensor_tensor(ap(o), ap(a), ap(b), f), [a, b], [o], k=1 if _bank(a) else 2)
 
     def ts(o, a, s1, f1, s2=None, f2=None):
+        k = {}
+        if plain(o, a) and (f1, f2) in ((A.mult, None), (A.add, None), (A.mult, A.add)):
+            sc, bi = (1.0, s1) if f1 == A.add else (s1, 0.0 if f2 is None else s2)
+            k["alt"] = lambda q: q.activation(ap(o), ap(a), ACT.Identity, bias=val(bi), scale=val(sc))
         if f2 is None:
-            op("v", lambda q: q.tensor_scalar(ap(o), ap(a), val(s1), None, f1), [a, s1], [o])
+            op("v", lambda q: q.tensor_scalar(ap(o), ap(a), val(s1), None, f1), [a, s1], [o], **k)
         else:
-            op("v", lambda q: q.tensor_scalar(ap(o), ap(a), val(s1), val(s2), f1, f2), [a, s1, s2], [o])
+            op("v", lambda q: q.tensor_scalar(ap(o), ap(a), val(s1), val(s2), f1, f2), [a, s1, s2], [o], **k)
 
-    def cp(o, a, q="v"):
-        if q == "v":
-            op("v", lambda e: e.tensor_copy(ap(o), ap(a)), [a], [o])
-        else:
-            op("s", lambda e: e.activation(ap(o), ap(a), ACT.Copy), [a], [o])
+    def cp(o, a):
+        k = {"alt": lambda e: e.activation(ap(o), ap(a), ACT.Copy)} if plain(o, a) else {}
+        op("v", lambda e: e.tensor_copy(ap(o), ap(a)), [a], [o], **k)
 
     def fill(o, c):
         op("v", lambda q: q.memset(ap(o), c), [], [o])
@@ -174,7 +303,7 @@ def rank_program(g, core, T, topo):
 
     def quant(b, lo, hi, tile):
         op("v", lambda q: q.quantize_mx(ap(V("Q" + b, lo, hi)), ap(V("S" + b, lo, hi)), ap(tile)), [tile],
-           [V("Q" + b, lo, hi), V("S" + b, lo, hi)])
+           [V("Q" + b, lo, hi), V("S" + b, lo, hi)], k=1.1)
 
     def mm(bank, sb, slo, mb, lo, hi, start=True, stop=True):
         sides = [V("Q" + sb, slo, slo + 128), V("S" + sb, slo, slo + 128), V("Q" + mb, lo, hi), V("S" + mb, lo, hi)]
@@ -188,37 +317,40 @@ def rank_program(g, core, T, topo):
 
     c05 = float(np.float32(0.05))
 
-    def relu(tile, col, lo, hi, on_v=()):
+    def relu(tile, col, lo, hi, both=True):
         for t in range(4):
             o, a = V(tile, 4 * col + t, 4 * (col + hi - lo), 4), V("P%d" % t, lo, hi)
-            if t in on_v:
-                ts(o, a, 0.0, A.max, c05, A.mult)
-            else:
-                op("s", lambda q, o=o, a=a: q.activation(ap(o), ap(a), ACT.Relu, scale=c05), [a], [o])
+            op("v", lambda q, o=o, a=a: q.tensor_scalar(ap(o), ap(a), 0.0, c05, A.max, A.mult), [a], [o],
+               alt=lambda q, o=o, a=a: q.activation(ap(o), ap(a), ACT.Relu, scale=c05))
+            if not both:
+                ops[-1].update(q="s", fn=ops[-1].pop("alt"))
 
     def pick(ob, olo, wb, wlo, whi, off):
         n = 16 * (off[2] - off[1])
         oq, wq, os_, ws_ = V("Q" + ob, olo, olo + n), V("Q" + wb, wlo, whi), V("S" + ob, olo, olo + n), V("S" + wb, wlo, whi)
-        op("v", lambda q: q.tensor_copy(ap(oq).bitcast(dt.uint32), ap(wq).bitcast(dt.uint32).indirect(ap(off))), [wq, off], [oq])
-        op("s", lambda q: q.activation(ap(os_), ap(ws_).indirect(ap(off)), ACT.Copy), [ws_, off], [os_])
+        op("v", lambda q: q.tensor_copy(ap(oq).bitcast(dt.uint32), ap(wq).bitcast(dt.uint32).indirect(ap(off))),
+           [wq, off], [oq], k=1.5, fix=0.05)
+        op("s", lambda q: q.activation(ap(os_), ap(ws_).indirect(ap(off)), ACT.Copy), [ws_, off], [os_], k=1.5, fix=0.05)
 
     def engines(src, dst, kind):
         es = topo.engines(src, dst)
-        return es[-8:] if kind == "hi" else es[:8] if kind == "lo" else es
+        return es[-8:] if kind == "hi" else es
 
     def send(dst, o, a, sem, kind):
         rid, pid, _ = topo.addr(dst)
         es = engines(core, dst, kind)
         cast = (lambda v: ap(v).bitcast(dt.uint8)) if a[0][0] == "Q" else ap
+        rate = ON if topo.chip(dst) == topo.chip(core) else OFF
         op("g", lambda q: q.remote_dma(cast(o), cast(a), T.sem[sem], T.sem["sent"], pid, rid, sum(1 << e for e in es)),
-           [a], [], sent=len(es))
+           [a], [], sent=len(es), name=sem, dst=dst, es=es,
+           busy=128 // len(es) * (ROW + (a[2] - a[1]) * (1 if a[0][0] == "S" else 4) / rate))
 
     def send2(dst, ob, olo, ab, alo, n, sem, kind):
         send(dst, V("Q" + ob, olo, olo + n), V("Q" + ab, alo, alo + n), sem + "c", kind)
         send(dst, V("S" + ob, olo, olo + n), V("S" + ab, alo, alo + n), sem + "s", kind)
 
-    def dma(q, o, a, r_, w, store=False):
-        op(q, lambda e: e.dma_start(o, a), r_, w, dma=True, store=store)
+    def dma(q, o, a, r_, w, store=False, busy=0.4):
+        op(q, lambda e: e.dma_start(o, a), r_, w, dma=True, store=store, es=range(16), busy=busy)
 
     def mask(m, at, b, lo, n):
         tt(V(m, at, at + n), V(b, lo, lo + n), V("MASK", at % P, at % P + n), A.mult)
@@ -228,46 +360,48 @@ def rank_program(g, core, T, topo):
         if shift:
             mask(m, at + P - 1, b, 0, 1)
 
-    def fold(c, m, n):
-        scan(V(c, 0, n), V("RST", 0, n), V(m, 0, n), A.mult, A.add)
-        return V(c, 15, n, 16)
+    def fold(c, m, n, at=0):
+        scan(V(c, at, at + n), V("RST", 0, n), V(m, at, at + n), A.mult, A.add)
+        return V(c, at + 15, at + n, 16)
 
     def W(name, lo=0, hi=12):
         return V(name, lo, hi)
 
-    for b, lo, n, s, src, kind in (("QA", RA, 64, "h1c", up, "hi"), ("SA", RA, P, "h1s", up, "hi"), ("QA", R1B, 128, "r1c", up, "hi"),
-                                   ("QA", R2, P, "r2c", up2, "lo"), ("SA", R2, P, "r2s", up2, "lo"),
+    def later(v):
+        ops[-1]["behind"] = v
+
+    s2 = up if near else up2
+    for b, lo, n, s, src, kind in (("QA", RA, P, "h1c", up, "all"), ("SA", RA, P, "h1s", up, "all"),
+                                   ("QA", R2, P, "r2c", s2, "all"), ("SA", R2, P, "r2s", s2, "all"),
                                    ("QA", N2, 64, "h2c", up, "all"), ("SA", N2, 64, "h2s", up, "all"),
                                    ("QR", 0, P, "f4c", up, "all"), ("SR", 0, P, "f4s", up, "all"),
-                                   ("LUP1", 0, 24, "up1", down, "all"), ("LUP2", 0, 12, "up2", down, "all"),
+                                   ("LUP1", 0, 16, "up1", down, "hi"), ("LUP2", 0, 12, "up2", down, "hi"),
                                    ("LDN2", 0, 36, "dn2", up, "all")):
         ops.append(dict(q="arr", r=[], w=[V(b, lo, lo + n)], sem=s, val=len(engines(src, core, kind))))
 
-    dma("y", T.XT[:, 0:512], T.x[:, 0:512], [], [V("XT", 0, 512)])
-    dma("s", T.XT[:, 512:768], T.x[:, 512:768], [], [V("XT", 512, 768)])
-    dma("y", T.XT[:, 768:1024], T.x[:, 0:256], [], [V("XT", 768, 1024)])
-    dma("s", T.UT[:], T.u[:], [], [V("UT", 0, 512)])
-    dma("y", T.QW[:, 0:512].bitcast(dt.uint8), T.wc[:, 0:2048], [], [V("QW", 0, 512)])
-    dma("s", T.SW[:], T.ws[:], [], [V("SW", 0, 1024)])
-    dma("y", T.QW[:, 512:1024].bitcast(dt.uint8), T.wc[:, 2048:4096], [], [V("QW", 512, 1024)])
+    wrap = 64 if last else 2 * int(r < 2)
+    dma("y", T.XT[:, 0:768], T.x[:, 0:768], [], [V("XT", 0, 768)], busy=0.6)
+    if wrap:
+        dma("s", T.XT[:, 768:768 + 4 * wrap], T.x[:, 0:4 * wrap], [], [V("XT", 768, 768 + 4 * wrap)], busy=0.2)
+    dma("y", T.UT[:], T.u[:], [], [V("UT", 0, 512)])
+    dma("y", T.QW[:, 0:512].bitcast(dt.uint8), T.wc[:, 0:2048], [], [V("QW", 0, 512)], busy=0.7)
+    dma("y", T.SW[:], T.ws[:], [], [V("SW", 0, 1024)])
+    dma("y", T.QW[:, 512:1024].bitcast(dt.uint8), T.wc[:, 2048:4096], [], [V("QW", 512, 1024)], busy=0.7)
     iota(V("IM", 0, P), [[0, 12], [1, 16]], 128, -1, False)
     iota(V("IQ", 0, 2), [[0, 2]], 0, 1, False)
     iota(W("PW0"), [[16, 12]], 0, 0, True)
-    iota(V("J16", 0, 128), [[0, 8], [1, 16]], 0, 0, True)
     fill(V("SP2", 0, CAP, rows=(0, 32)), 1.0)
     fill(V("SP2", CAP, P, rows=(0, 32)), 0.0)
-    dma("s", T.sp[0:1, 0:P], T.SP2[0:1, 0:P], [V("SP2", 0, P)], [], store=True)
     fill(V("O0", 0, 8), 0)
     fill(V("O1", 0, 8), 1)
-    fill(V("RST", 0, 3 * P), 1.0)
-    fill(V("ZERO", 0, 320), 0.0)
-    fill(V("RST", 0, 3 * P, 16), 0.0)
-    quant("A", C1, C1 + 128, V("XT", 0, 512))
-    send(down, V("QA", RA, RA + 64), V("QA", C1 + sh, C1 + sh + 64), "h1c", "hi")
-    quant("A", C1 + 128, C1 + 256, V("XT", 512, 1024))
-    send(down, V("SA", RA, RA + P), V("SA", C1 + sh, C1 + sh + P), "h1s", "hi")
-    send(down, V("QA", R1B, R1B + 128), V("QA", C1 + sh + 64, C1 + sh + P), "r1c", "hi")
-    send2(down2, "A", R2, "A", C1 + int(r < 2), P, "r2", "lo")
+    fill(V("RST", 0, P), 1.0)
+    fill(V("ZERO", 0, 336), 0.0)
+    fill(V("RST", 0, P, 16), 0.0)
+    n1 = P + 2 * int(r < 2)
+    quant("A", C1, C1 + n1, V("XT", 0, 4 * n1))
+    send2(down, "A", RA, "A", C1 + sh, P, "h1", "all")
+    if direct:
+        send2(down2, "A", R2, "A", C1 + int(r < 2), P, "r2", "all")
     quant("A", BDUP, BDUP + 128, V("XT", 256, 768))
     ts(V("IM2", 0, P), V("IM", 0, P), 15, A.bitwise_and)
     ts(V("IQ2", 0, 2), V("IQ", 0, 2), 15, A.bitwise_and)
@@ -277,32 +411,37 @@ def rank_program(g, core, T, topo):
     pick("UB", 0, "U", 0, 128, V("O1", 0, 8))
     if last:
         quant("A", L7, L7 + 128, V("XT", 508, 1020))
+    wide = 128 if near else P
     mm(4, "UA", 0, "A", C1, C1 + P)
-    half(False, "A", C1 - 64, C1 + 64)
+    half(False, "A", C1, C1 + wide)
     ts(V("MASK", 0, P), V("IM2", 0, P), 0, A.is_equal)
-    cp(V("A1R", 0, P), V("P4", 0, P), "s")
-    cp(V("AR", BDUP, BDUP + 128), V("P4", 64, P), "s")
+    cp(V("AR", BDUP, BDUP + 128), V("P4", 64, P))
     fill(V("TL", 256, 512), 0.0)
     ts(W("PW"), W("PW0"), V("Z0", 0, 1), A.add)
-    ts(V("WG0", 0, 128), V("J16", 0, 128), V("Z0", 0, 1), A.is_le)
-    ts(V("WG", 0, 128), V("MASK", 0, 128), 32.0, A.mult)
-    turn("WM", 0, "A1R", 0)
-    tt(V("WG", 0, 128), V("WG", 0, 128), V("WG0", 0, 128), A.add)
+    ts(V("WG0", 0, 128), V("MASK", 0, 128), -1.0, A.mult, 1.0, A.add)
+    ts(V("WG1", 0, 128), V("MASK", 15, 143), 31.0, A.mult)
+    ts(V("Z2", 8, 9), V("MASK", 15, 16), -31.0, A.mult, 32.0, A.add)
+    ts(V("Z2", 9, 10), V("MASK", 15, 16), -31.0, A.mult, -1.0, A.add)
+    turn("WM", 0, "P4", 0)
+    tt(V("WG", 0, 128), V("WG1", 0, 128), V("WG0", 0, 128), A.add)
     a1w = fold("WC", "WM", P)
     ts(V("INJ", 0, 64, 16), W("PW", 0, 4), float(K2), A.add)
     ts(W("EW"), W("PW"), float(P - 1), A.is_equal)
     cp(W("UP1"), a1w)
-    cp(W("UP1", 16, 24), V("WC", 79, P, 16))
     ts(W("CW", 0, 8), W("PW", 4, 12), float(201 - 2 * CAP), A.add)
     ts(V("TW", 0, 32, 4), W("PW", 4, 12), float(NEW2), A.add)
     fill(V("R4", 0, 32), 1.0)
     fill(V("MA", 64 + last, 65 + last), float(200 - CAP))
     fill(V("R4", 0, 32, 4), 0.0)
+    ts(W("C1W"), W("PW"), float(C1), A.add)
+    ts(W("K2W"), W("PW"), float(K2), A.add)
+    cp(V("OFD", 1, 24, 2), W("PW"))
+    fill(V("OFD", 0, 24, 2), float(K4))
+    fill(W("C2B", 0, 4), -1.0)
+    ts(W("C2B", 4, 12), W("PW", 4, 12), float(NEW2), A.add)
     if last:
         ts(V("MD", 0, 63), V("MASK", 0, 63), float(LATE + 1 - K2), A.mult)
         ts(V("MD", 63, 64), V("MASK", 63, 64), float(NEW2 - K2), A.mult)
-        cp(V("AL", 0, 1), V("A1R", P - 1, P))
-        cp(V("AL", 1, 64), V("A1R", 0, 63))
         ts(W("Z2", 0, 8), W("EW", 4, 12), -1000.0, A.mult, 1000.0, A.add)
         ts(W("EW2", 0, 8), W("EW", 4, 12), -199.0, A.mult)
         fill(V("MC", 127, 128), 0.0)
@@ -313,189 +452,211 @@ def rank_program(g, core, T, topo):
         ts(W("Z7"), W("EW"), float(-P), A.mult, 1.0, A.add)
         tt(W("Z8"), W("Z7"), W("PW"), A.add)
         pd = W("Z8")
-
-    half(True, "A", RA - 64, RA + 64)
-    relu("TL", 128, 64, 128, on_v=(1, 3))
-    quant("A", JUNK, JUNK + 128, V("TL", 256, 768))
-    send2(down, "A", N2, "A", NEW2, 64, "h2", "all")
-
-    mm(7, "UA", 0, "A", NEW2, NEW2 + 128)
-    mm(4, "U", 0, "A", NEW2, NEW2 + P)
-    half(False, "A", C1 + 64, C1 + P)
     ts(W("Z3"), pd, 64.0 - last, A.is_lt, float(N2 + last - RA), A.mult)
     ts(W("Z4"), pd, float(RA), A.add)
-    mask("WM1", 0, "P7", 0, 64)
-    cp(V("AR", NEW2, NEW2 + 64), V("P7", 0, 64))
-    cp(W("UP1", 12, 16), fold("WC1", "WM1", 64))
-    send(up, W("LUP1", 0, 24), W("UP1", 0, 24), "up1", "all")
-    cp(V("Y", 0, P), V("P4", 0, P), "s")
+    ts(V("F12", 0, 24, 2), pd, float(R2), A.add)
     if last:
         ts(W("Z5"), W("EW"), float(N2 - RA - (P - 1)), A.mult)
         tt(W("Z6"), W("Z3"), W("Z4"), A.add)
         tt(W("R12W"), W("Z6"), W("Z5"), A.add)
     else:
         tt(W("R12W"), W("Z3"), W("Z4"), A.add)
-    ts(V("F12", 0, 24, 2), pd, float(R2), A.add)
-    fill(V("LUP1", 24, 36), 0.0)
-    mm(5, "UB", 0, "A", R1B, R1B + 128)
-    half(True, "A", R1B, R1B + 128)
-    tt(V("S1B", 0, 128), V("P5", 0, 128), V("A1R", 64, P), A.add)
-    mask("WMX", P + 64 - sh, "P5", 0, 128 - last)
-    relu("TK", P, 0, 128)
+
+    half(True, "A", RA, RA + wide)
+    relu("TL", 128, 0, 64)
+    quant("A", JUNK, JUNK + 128, V("TL", 256, 768))
+    if hand:
+        send2(down, "A", R2, "A", RA, P, "r2", "all")
+    send2(down, "A", N2, "A", NEW2, 64, "h2", "all")
+
+    mm(4, "UA", 0, "A", NEW2, NEW2 + 128)
+    mask("WM1", 0, "P4", 0, 64)
     if last:
-        mm(7, "UB", 0, "A", RA, RA + 128)
-        mask("WMX", P + 63, "P7", 63, 1)
-        tt(V("S1A", 64, 65), V("P7", 63, 64), V("A1R", 63, 64), A.add)
+        cp(V("AR", NEW2, NEW2 + 64), V("P4", 0, 64))
+    cp(W("UP1", 12, 16), fold("WC1", "WM1", 64))
+    send(up, W("LUP1", 0, 16), W("UP1", 0, 16), "up1", "hi")
+    mm(5, "UB", 0, "A", R1B - 2, R1B + 128)
+    mask("WMX", P + 64 - sh - last, "P5", 2 - last, 128)
+    mm(6, "UA", 0, "A", C1 + 62, C1 + P, stop=False)
+    mm(6, "UB", 0, "A", R1B - 2, R1B + 128, start=False)
+    cp(V("S1B", 0, 130), V("P6", 0, 130))
+    if near:
+        half(False, "A", C1 + 64, C1 + P)
+        half(True, "A", R1B, R1B + 128)
+        relu("TK", P, 0, 128)
+    else:
+        relu("TK", P, 64, P)
     half(False, "A", NEW2, NEW2 + P)
     quant("A", K1B, K1B + 128, V("TK", 4 * P, 1280))
     mm(6, "UB", 0, "A", R2, R2 + P)
     half(True, "A", R2, R2 + P)
-    tt(V("S2R", 64, P), V("P6", 64, P), V("A1R", 64, P), A.add)
-    tt(V("S2L", last, 64 + last), V("P6", 0, 64), V("AR", NEW2, NEW2 + 64), A.add)
-    tt(V("MC", 0, 128 - last), V("S1B", 0, 128 - last), V("S2R", 64, P - last), A.is_ge)
+    mm(7, "UA", 0, "A", NEW2, NEW2 + P, stop=False)
+    mm(7, "UB", 0, "A", R2, R2 + P, start=False)
+    tt(V("MC", 0, 128 - last), V("P7", 64, P - last), V("S1B", 2, 130 - last), A.is_le)
+    cp(V("S2L", last, 64 + last), V("P7", 0, 64))
+    if last:
+        tt(V("MA", 64, 65), V("P7", 63, 64), V("S1B", 1, 2), A.is_le)
     relu("TK", 0, 0, P)
     mm(4, "UA", 0, "A", K1B, K1B + 128)
-    cp(V("AR", K1B, K1B + 128), V("P4", 0, 128), "s")
+    cp(V("AR", K1B, K1B + 128), V("P4", 0, 128))
     if last:
-        cp(V("S2L", 0, 1), V("S2R", P - 1, P), "s")
-    tt(V("MCM", 0, 128), V("MC", 0, 128), V("WG", 0, 128), A.mult)
-    scan(V("CUM", 16, 144), V("MC", 0, 128), V("MC", 0, 128), A.add, A.max)
-    mcs = fold("MCS", "MCM", 128)
-    ts(W("MW", 0, 8), mcs, 32.0, A.is_ge, 232.0, A.mult)
-    tt(W("CUW", 0, 8), mcs, V("CUM", 15, 128, 16), A.add)
+        cp(V("S2L", 0, 1), V("P7", P - 1, P))
+    scan(V("CUM", 0, 128), V("MC", 0, 128), V("MC", 0, 128), A.add, A.max)
+    scan(V("MCS", 0, 128), V("WG", 0, 128), V("MC", 0, 128), A.mult, A.add)
+    mcs = V("MCS", 15, 128, 16)
+    ts(W("MW", 0, 8), mcs, V("Z2", 8, 9), A.is_ge, 168.0, A.mult)
+    ts(W("SUF", 0, 8), mcs, V("Z2", 9, 10), A.mult)
+    tt(W("CUW", 0, 8), W("SUF", 0, 8), V("CUM", 15, 128, 16), A.add)
     quant("A", K2, K2 + P, V("TK", 0, 4 * P))
     tt(W("AB", 0, 8), W("CUW", 0, 8), W("MW", 0, 8), A.subtract)
     tt(W("AB", 8, 16), W("AB", 0, 8), W("CW", 0, 8), A.subtract)
     if last:
         tt(W("AB", 16, 24), W("AB", 0, 8), W("Z2", 0, 8), A.add)
-    dma("y", T.y[:, 0:P], T.Y[:, 0:P], [V("Y", 0, P), W("MW", 0, 8)], [], store=True)
+    mm(4, "UA", 0, "A", K2, K2 + P)
+    cp(V("AR", K2, K2 + P), V("P4", 0, P))
+    turn("WMX", 2 * P, "P6", sh)
+    b3w = fold("WCX", "WMX", P, 2 * P)
     left = L7 if last else C1 - 64
     half(False, "A", left, left + 128)
+    mm(7, "UA", 0, "A", left, left + 128, stop=False)
 
-    mm(5, "UB", 0, "A", N2 - 64, N2 + 64)
+    mm(7, "UB", 0, "A", N2 - 64, N2 + 64, start=False)
     half(True, "A", N2 - 64, N2 + 64)
-    mm(4, "UA", 0, "A", K2, K2 + P)
-    tt(V("S1A", 0, 64), V("P5", 64, 128), V("AL" if last else "A1R", 0, 64), A.add)
-    tt(V("MA", 0, 64 + last), V("S1A", 0, 64 + last), V("S2L", 0, 64 + last), A.is_ge)
+    mm(5, "UB", 0, "A", N2 - 64, N2 + 64)
+    tt(V("MA", 0, 64), V("P7", 64, 128), V("S2L", 0, 64), A.is_ge)
+    later(V("QA", K2, K2 + P))
     ma, mn, nn = V("MA", last, 64 + last), V("MA", last, 65 + last), V("ONE", 8, 9)
     op("v", lambda q: q.tensor_reduce(ap(nn), ap(mn), AxisListType.X, A.add, negate=True), [mn], [nn])
-    relu("TL", 0, 64, 128)
+    relu("TL", 0, 64, 128, False)
     if last:
-        z, e7, m0, a7 = W("Z9", 0, 1), W("EW2", 7, 8), V("MA", 0, 1), V("AB", 7, 24, 8)
-        op("s", lambda q: q.activation(ap(z), ap(e7), ACT.Identity, scale=ap(m0)), [e7, m0], [z])
-        op("s", lambda q: q.activation(ap(a7), ap(a7), ACT.Identity, bias=ap(z)), [a7, z], [a7])
+        z, e7, m0 = W("Z9", 0, 1), W("EW2", 7, 8), V("MA", 0, 1)
+        tt(z, e7, m0, A.mult)
     tt(V("MK", 0, 64), ma, V("MD", 0, 64), A.mult)
-    quant("A", LATE, LATE + 128, V("TL", 0, 512))
+    if last:
+        ts(V("AB", 7, 24, 8), V("AB", 7, 24, 8), z, A.add)
+    scan(V("SC", 0, 64), V("INJ", 0, 64), V("MK", 0, 64), A.max, A.add)
     ts(V("TW", 1, 32, 4), W("AB", 0, 8), nn, A.is_le, float(K1B - 64 - NEW2), A.mult)
     ts(V("TW", 2, 32, 4), W("AB", 8, 16), nn, A.is_ge, float(K2 - NEW2), A.mult)
     if last:
         ts(V("TW", 3, 32, 4), W("AB", 16, 24), nn, A.is_le, float(LATE - (P - 1) - (K1B - 64)), A.mult)
-    mm(7, "UA", 0, "A", LATE, LATE + 128)
-    cp(V("AR", K2, K2 + P), V("P4", 0, P), "s")
-    cp(V("AR", LATE, LATE + 64), V("P7", 0, 64), "s")
-    scan(V("TD", 0, 32), V("R4", 0, 32), V("TW", 0, 32), A.mult, A.add)
-    scan(V("SC", 0, 64), V("INJ", 0, 64), V("MK", 0, 64), A.max, A.add)
-    cp(W("O3", 4, 12), V("TD", 3, 32, 4))
     cp(W("O3", 0, 4), V("SC", 15, 64, 16))
-
-    o3 = W("O3F")
-    ar, m3, mk = V("AR", 0, R2), V("WM3", 0, P), V("MASK", 0, P)
-    op("v", lambda q: q.tensor_tensor(ap(m3), ap(ar).indirect(ap(W("O3"))), ap(mk), A.mult), [ar, W("O3"), mk], [m3])
-    cp(W("UP2"), fold("WC3", "WM3", P))
-    send(up, W("LUP2"), W("UP2"), "up2", "all")
-    pick("K", 0, "A", 0, QEND, W("O3"))
-    cp(o3, W("O3"))
-    o3d = o3
-    if sh:
-        cp(W("SI"), o3, "s")
-        cp(W("SI", 32, 43), W("O3F", 1, 12), "s")
-        cp(W("SI", 43, 44), W("O3F", 0, 1), "s")
-    mm(7, "UB", 0, "K", 0, P)
-    mm(0, "U", 0, "K", 0, P)
-    turn("WMX", 2 * P, "P6", sh)
+    scan(V("TD", 0, 32), V("R4", 0, 32), V("TW", 0, 32), A.mult, A.add)
     if sh or last:
         mask("WMX", P, "P5", 65, 63)
         mask("WMX", 2 * P - 1, "P5", 64, 1)
     else:
         mask("WMX", P, "P5", 64, 64)
+    cp(W("O3", 4, 12), V("TD", 3, 32, 4))
+
+    quant("A", LATE, LATE + 128, V("TL", 0, 512))
+    mm(7, "UA", 0, "A", LATE, LATE + 128)
+    cp(V("AR", LATE, LATE + 64), V("P7", 0, 64))
+    mm(6, "U", 0, "A", NEW2, NEW2 + P)
+    cp(V("Y", 0, P), V("P6", 0, P))
+    dma("y", T.y[:, 0:P], T.Y[:, 0:P], [V("Y", 0, P)], [], store=True)
+    o3 = W("O3F")
+    ar, m3, mk = V("AR", 0, R2), V("WM3", 0, P), V("MASK", 0, P)
+    op("v", lambda q: q.tensor_tensor(ap(m3), ap(ar).indirect(ap(W("O3"))), ap(mk), A.mult), [ar, W("O3"), mk], [m3],
+       k=1.5, fix=0.05)
+    cp(W("UP2"), fold("WC3", "WM3", P))
+    send(up, W("LUP2"), W("UP2"), "up2", "hi")
+    pick("K", 0, "A", 0, R2, W("O3"))
+    cp(o3, W("O3"))
+    o3d = o3
+    if sh:
+        cp(W("SI"), o3)
+        cp(W("SI", 32, 43), W("O3F", 1, 12))
+        cp(W("SI", 43, 44), W("O3F", 0, 1))
+    mm(7, "UB", 0, "K", 0, P)
+    mm(4, "U", 0, "K", 0, P)
     turn("WMX", 0, "P7", sh)
     if sh:
         flip(V("ST", 0, 64), V("SI", 0, 64))
-        cp(V("SH", 0, 31), V("ST", 1, 32), "s")
-        cp(V("SH", 15, 32, 16), V("ST", 32, 64, 16), "s")
-    tt(W("DN2", 0, 36), fold("WCX", "WMX", 3 * P), W("LUP1", 0, 36), A.add)
+        cp(V("SH", 0, 31), V("ST", 1, 32))
+        cp(V("SH", 15, 32, 16), V("ST", 32, 64, 16))
+    if sh or last:
+        fold("WCX", "WMX", P, P)
+    else:
+        fold("WCX", "WMX", 64, P)
+        fold("WCX", "WMX", 128, P + 64)
+    tt(W("S2D", 0, 4), V("WCX", P + 15, P + 64, 16), W("LUP1", 12, 16), A.add)
+    tt(W("S2D", 4, 12), V("WCX", P + 79, 2 * P, 16), W("LUP1", 4, 12), A.add)
+    tt(W("S1D"), fold("WCX", "WMX", P), W("LUP1"), A.add)
+    cp(W("DN2", 0, 12), b3w)
     if sh:
         flip(V("SI", 0, 32), V("SH", 0, 32))
         o3d = W("SI")
-    m12, kd = W("DN2", 36, 48), W("DN2", 48, 60)
+    m12, kd = W("DN2", 12, 24), W("DN2", 24, 36)
     tt(W("F0"), W("R12W"), o3d, A.subtract)
-    tt(m12, W("DN2"), W("DN2", 12, 24), A.max)
-    tt(kd, W("DN2", 12, 24), W("DN2"), A.is_gt)
-    send(down, W("LDN2", 0, 36), W("DN2", 24, 60), "dn2", "all")
-    cp(V("Y", P, 2 * P), V("P0", 0, P), "s")
-    dma("y", T.y[:, P:2 * P], T.Y[:, P:2 * P], [V("Y", P, 2 * P)], [], store=True)
+    tt(m12, W("S1D"), W("S2D"), A.max)
+    tt(kd, W("S2D"), W("S1D"), A.is_gt)
+    send(down, W("LDN2", 0, 36), W("DN2", 0, 36), "dn2", "all")
+    cp(V("Y", P, 2 * P), V("P4", 0, P))
     tt(W("F1"), W("F0"), kd, A.mult)
     tt(V("F12", 1, 24, 2), W("F1"), o3d, A.add)
-    tt(W("S3D"), W("LUP2"), W("DN2", 24, 36), A.add)
+    tt(W("S3D"), W("LUP2"), b3w, A.add)
     tt(V("K3D", 1, 24, 2), W("S3D"), m12, A.is_gt)
-    scan(V("X3", 0, 24), V("K3D", 0, 24), V("F12", 0, 24), A.mult, A.max)
-    cp(W("OS"), V("X3", 1, 24, 2))
+    scan(V("XS", 0, 24), V("K3D", 0, 24), V("F12", 0, 24), A.mult, A.max)
+    cp(W("OS"), V("XS", 1, 24, 2))
     pick("S", 0, "A", 0, QEND, W("OS"))
     send2(down, "R", 0, "S", 0, P, "f4", "all")
+    dma("y", T.y[:, P:2 * P], T.Y[:, P:2 * P], [V("Y", P, 2 * P), V("QR", 0, P)], [], store=True)
+    dma("y", T.sp[0:1, 0:P], T.SP2[0:1, 0:P], [V("SP2", 0, P), V("QR", 0, P)], [], store=True, busy=0.03)
     kap, k3, l12 = W("LDN2", 24, 36), V("K3", 1, 24, 2), V("LP", 1, 24, 2)
-    ts(W("C1W"), W("PW"), float(C1), A.add)
-    ts(W("K2W"), W("PW"), float(K2), A.add)
     ts(W("L0"), kap, float(NEW2 - C1), A.mult)
+    later(W("OS"))
     tt(W("S3"), W("UP2"), W("LDN2"), A.add)
+    later(W("OS"))
     tt(l12, W("L0"), W("C1W"), A.add)
     tt(k3, W("S3"), W("LDN2", 12, 24), A.is_gt)
     tt(V("LP", 0, 24, 2), o3, l12, A.subtract)
     ts(W("V0"), kap, 255.0, A.mult, 1.0, A.add)
+    later(W("OS"))
     scan(V("LS", 0, 24), V("K3", 0, 24), V("LP", 0, 24), A.mult, A.add)
     ts(W("V1"), k3, 65536.0, A.mult)
     cp(W("OL"), V("LS", 1, 24, 2))
     tt(W("VAL"), W("V0"), W("V1"), A.max)
-    pick("L", 0, "A", 0, QEND, W("OL"))
+    pick("L", 0, "A", 0, R2, W("OL"))
     half(False, "L", 0, P)
-    flip(V("VT", 0, 32), V("VAL", 0, 32))
     ts(W("Q0"), kap, -255.0 / 256, A.mult, 1.0, A.add)
-    scan(V("PR", 0, 32), V("RST", 0, 32), V("VT", 0, 32), A.mult, A.add)
-    ts(W("Q1"), k3, -65535.0 / 65536, A.mult, 1.0, A.add)
-    ts(V("PR", 32, 64), V("VT", 0, 32), 0.0, A.mult, V("PR", 15, 16), A.add)
-    tt(W("INV"), W("Q0"), W("Q1"), A.min)
-    flip(V("PT", 0, 64), V("PR", 0, 64))
-    ts(W("V2"), kap, 1.0, A.add)
-    scan(W("EX", 1, 12), W("PT", 32, 43), W("PT", 32, 43), A.add, A.max)
-    ts(W("V3"), k3, 3.0, A.mult)
-    tt(W("CU4"), W("EX"), W("PT"), A.add)
-    tt(W("KI"), W("V2"), W("V3"), A.max)
-    tt(W("D21"), W("CU4"), W("INV"), A.mult)
-    ts(W("PF"), W("PW"), 1.0 / K4, A.mult)
-    ts(W("O3D"), W("D21"), -0.248, A.add)
-    fill(W("C2B", 0, 4), -1.0)
-    cp(W("QI"), W("O3D"))
-    ts(W("C2B", 4, 12), W("PW", 4, 12), float(NEW2), A.add)
-    ts(W("QI2"), W("QI"), 255, A.bitwise_and)
+    later(W("OS"))
     tt(W("X1"), o3, W("K2W"), A.is_equal)
-    ts(W("T4W"), W("QI2"), float(CAP), A.is_le)
     tt(W("X2"), o3, W("C2B"), A.not_equal)
-    tt(W("OF0"), W("T4W"), W("PF"), A.add)
-    tt(W("SPW", 12, 24), W("T4W"), W("KI"), A.mult)
     tt(W("SPW"), W("X1"), W("X2"), A.add)
-    ts(W("OF"), W("OF0"), float(K4), A.mult)
+    ts(W("Q1"), k3, -65535.0 / 65536, A.mult, 1.0, A.add)
+    flip(V("VT", 0, 32), V("VAL", 0, 32))
+    tt(W("INV"), W("Q0"), W("Q1"), A.min)
+    scan(V("PR", 0, 32), V("RST", 0, 32), V("VT", 0, 32), A.mult, A.add)
+    ts(W("V2"), kap, 1.0, A.add)
+    later(W("OS"))
+    ts(V("PR", 32, 64), V("VT", 0, 32), 0.0, A.mult, V("PR", 15, 16), A.add)
+    ts(W("V3"), k3, 3.0, A.mult)
+    flip(V("PT", 0, 64), V("PR", 0, 64))
+    tt(W("KI"), W("V2"), W("V3"), A.max)
+    scan(W("EX", 1, 12), W("PT", 32, 43), W("PT", 32, 43), A.add, A.max)
+    tt(W("CU4"), W("EX"), W("PT"), A.add)
+    tt(W("D21"), W("CU4"), W("INV"), A.mult)
+    ts(W("QI"), W("D21"), -0.248, A.add)
+    ts(W("QI2"), W("QI"), 255, A.bitwise_and)
+    t4 = V("T4I", 1, 24, 2)
+    ts(t4, W("QI2"), float(CAP), A.is_le)
+    scan(V("OFS", 0, 24), V("T4I", 0, 24), V("OFD", 0, 24), A.mult, A.add)
+    tt(W("SPW", 12, 24), t4, W("KI"), A.mult)
+    cp(W("OF"), V("OFS", 1, 24, 2))
     flip(V("SPT", 0, 32), V("SPW", 0, 32))
-    dma("y", T.sp[0:1, P:3 * P], T.SPT[0:24, 0:16], [V("SPT", 0, 32)], [], store=True)
+    dma("y", T.sp[0:1, P:3 * P], T.SPT[0:24, 0:16], [V("SPT", 0, 32)], [], store=True, busy=0.06)
 
     half(True, "R", 0, P)
-    relu("T4", 0, 0, P, on_v=(1, 3))
+    relu("T4", 0, 0, P)
     quant("K", K4, K4 + P, V("T4", 0, 4 * P))
-    pick("O", 0, "K", 0, K4 + P, W("OF"))
-    mm(4, "U", 0, "O", 0, 128)
+    pick("O", 64, "K", 0, K4 + P, W("OF", 4, 12))
+    mm(4, "U", 0, "K", K4, K4 + 128)
     mm(5, "U", 0, "O", 64, P)
+    pick("O", 0, "K", 0, K4 + P, W("OF", 0, 4))
     dma("y", T.oc[:, :], T.QO[:, 0:P].bitcast(dt.uint8), [V("QO", 0, P)], [], store=True)
     for k in range(4):
-        dma("ys"[k % 2], T.osc[4 * k:4 * k + 4, :], T.SO[32 * k:32 * k + 4, 0:P], [V("SO", 0, P)], [], store=True)
-    cp(V("Y", 2 * P, 2 * P + 112), V("P4", 0, 112), "s")
-    cp(V("Y", 2 * P + 112, 3 * P), V("P5", 48, 128))
+        dma("ys"[k % 2], T.osc[4 * k:4 * k + 4, :], T.SO[32 * k:32 * k + 4, 0:P], [V("SO", 0, P)], [], store=True, busy=0.03)
+    cp(V("Y", 2 * P, 2 * P + 64), V("P4", 0, 64))
+    cp(V("Y", 2 * P + 64, 3 * P), V("P5", 0, 128))
     dma("y", T.y[:, 2 * P:3 * P], T.Y[:, 2 * P:3 * P], [V("Y", 2 * P, 3 * P)], [], store=True)
-    _emit(g, T, ops)
+    return ops

@@ -1,13 +1,15 @@
 import numpy as np
+from concourse.bass import DstId, RemoteDMATransfer
 from concourse.mybir import dt, AluOpType, AxisListType, ActivationFunctionType
 
 N, P, CAP = 8, 192, 64
 CODE = "float8_e4m3fn_x4"
-JUNK, NEW2, BDUP, C1, RA, R1B, N2, L7, LATE, K2, K1B, R2, QEND = (
-    0, 64, 128, 256, 512, 576, 704, 768, 896, 1024, 1216, 1344, 1536)
-K4 = 256
-HOP, LOAD, WAKE, PEEK, ROW, ISSUE, FIRST, LEAN, LAND, ON, OFF = 1.3, 1.0, 0.14, 0.02, 0.028, 0.35, 1.1, 0.05, 0.3, 30000, 21000
-AHEAD, SLACK = 0.4, 0.06
+R2, OWN, LATE, K2, K1B, JUNK, NEW2, BDUP, C1, OEND, L7, RA, R1B, N2, QEND = (
+    0, 192, 224, 352, 544, 672, 736, 800, 928, 1152, 1152, 1280, 1344, 1472, 1664)
+K3, CD, KEND = 128, 320, 464
+LO, HI = (0, 64), (64, 128)
+HOP, LOAD, WAKE, PEEK, ROW, ISSUE, FIRST, LEAN, LAND, ON, OFF = 1.0, 1.0, 0.17, 0.02, 0.028, 0.35, 1.1, 0.1, 0.3, 30000, 21000
+AHEAD, SLACK, SLOW, JITTER, SEED = 0.2, 0.1, 1.25, 0.0, 0
 
 SCRATCH = {}
 PART = {}
@@ -25,34 +27,35 @@ def _parts(buf, items):
     _buf(buf, at)
 
 
-for _n, _c in (("A", QEND), ("K", K4 + P), ("W", 1024), ("U", 128), ("UA", 128), ("UB", 128), ("L", P), ("S", P),
-               ("R", P), ("O", P)):
+for _n, _c in (("A", QEND), ("K", KEND), ("W", 1024), ("U", 128), ("UA", 128), ("UB", 128), ("UC", 128), ("L", P),
+               ("S", P), ("R", P), ("O", P)):
     _buf("Q" + _n, _c, CODE)
     _buf("S" + _n, _c, "uint8")
-for _n, _c in (("XT", 1024), ("UT", 512), ("TL", 768), ("TK", 1280), ("T4", 768)):
+for _n, _c in (("XT", 1024), ("UT", 512), ("TL", 768), ("TK", 1536), ("T4", 768), ("T3", 512)):
     _buf(_n, _c, "bfloat16")
 for _n in range(8):
     _buf("P%d" % _n, 512, where="psum")
-for _n, _c in (("IM", P), ("IM2", P), ("IQ", 2), ("IQ2", 2), ("QI", 12), ("QI2", 12)):
+for _n, _c in (("IM", 224), ("IM2", 224), ("IQ", 2), ("IQ2", 2), ("QI", 12), ("QI2", 12)):
     _buf(_n, _c, "int32")
-for _n, _c in (("O0", 8), ("O1", 8), ("O3", 12), ("OS", 12), ("OL", 12), ("OF", 12)):
+for _n, _c in (("O0", 16), ("O3", 14), ("OC", 8), ("OS", 12), ("OL", 12), ("OF", 12)):
     _buf(_n, _c, "uint16")
-_parts("ROWS", [(_n, P) for _n in ("MASK", "WM", "WC", "WM3", "WC3", "RST")]
-       + [("WMX", 3 * P), ("WCX", 3 * P), ("MD", 64), ("S1B", 144), ("MC", 128),
-          ("MCS", 128), ("WG", 128), ("WG0", 128), ("WG1", 128), ("S2L", 80),
-          ("MA", 80), ("MK", 64), ("SC", 64), ("WM1", 64), ("WC1", 64), ("AR", R2)])
+_parts("ROWS", [("MASK", 144), ("M4", 224), ("MG", 208), ("RSG", 208), ("WM3", 208), ("WC3", 208)]
+       + [(_n, P) for _n in ("WM", "WC", "RST", "WMX", "WCX")]
+       + [("MD", 64), ("S1B", 144), ("MC", 128), ("MCS", 128), ("WG", 128), ("WG0", 128), ("WG1", 128), ("S2L", 80),
+          ("MA", 80), ("MK", 64), ("SC", 64), ("WM1", 80), ("WC1", 64), ("CL", 80), ("CUM", 128), ("WMC", 128),
+          ("WCC", 128), ("WM2", 128), ("WC2", 128), ("CS", 80), ("WCY", 80)])
 _parts("LISTS", [(_n, 16) for _n in (
-    "PW0", "PW", "C2B", "K2W", "C1W", "D21", "R12W", "CW", "EW", "EW2", "MW", "CUW",
-    "O3F", "SUF", "S3D", "F0", "F1", "X1", "X2", "L0", "V0", "V1", "V2", "V3", "INV", "Q0", "Q1",
-    "Z0", "Z2", "Z3", "Z4", "Z5", "Z6", "Z7", "Z8", "Z9", "KI", "ONE", "CU4", "S1D", "S2D", "S3")]
-    + [(_n, 32) for _n in ("AB", "R4", "TD", "F12", "XS", "LP", "LS", "VT", "SH", "OFD", "OFS")]
-    + [("PR", 64), ("PT", 64), ("ST", 64)])
-_parts("ZERO", [("INJ", 64), ("TW", 32), ("K3D", 32), ("K3", 32), ("VAL", 32), ("SPW", 32), ("SI", 64), ("EX", 16),
-                ("T4I", 32)])
-for _n, _c in (("Y", 3 * P), ("SP2", P), ("SPT", 32), ("UP1", 16), ("LUP1", 16), ("DN2", 36), ("LDN2", 36),
-               ("UP2", 12), ("LUP2", 12), ("CUM", 128)):
+    "PW0", "PW", "C2B", "K2W", "CW", "EW", "EW2", "SUF", "X1", "X2", "Z0", "Z2", "Z3", "Z4", "Z5", "Z6",
+    "Z7", "Z8", "Z9", "ONE", "CU4", "S2D", "OFS", "T4F", "OCF", "OCG", "RS", "BIG", "NE", "S3X", "PWX", "ZL", "ZM")]
+    + [(_n, 32) for _n in ("AB", "VT")]
+    + [(_n, 36) for _n in ("XD", "XS", "LD", "LS", "TV", "TI", "TS", "IS", "KS")]
+    + [("R4", 48), ("TD", 48), ("SA1", 48), ("SB1", 48), ("PR", 64), ("PT", 64)])
+_parts("ZERO", [("INJ", 64), ("TW", 48), ("TA", 48), ("TB", 48), ("AD", 12), ("WS", 80), ("WMY", 80), ("SPW", 32),
+                ("XF", 36), ("LF", 36), ("VS", 96), ("WL", 80), ("DN", 12), ("U2S", 8)])
+for _n, _c in (("Y", 3 * P), ("SP2", P), ("SPT", 32), ("UP1", 4), ("LUP1", 4), ("LA1", 4), ("A1", 4), ("B3", 4),
+               ("LB3", 4), ("LDN", 12), ("UP2", 12), ("LUP2", 8), ("AR", OEND - OWN), ("AX", OEND - OWN)):
     _buf(_n, _c)
-ARRIVE = ["h1c", "h1s", "r2c", "r2s", "h2c", "h2s", "up1", "up2", "dn2", "f4c", "f4s"]
+ARRIVE = ["h1c", "h1s", "r2c", "r2s", "h2c", "h2s", "c3c", "c3s", "a1", "b3", "up1", "up2", "dn", "f4c", "f4s"]
 POOL = ["s%d" % _n for _n in range(130)]
 SEMAPHORES = ARRIVE + ["sent", "st"] + POOL
 
@@ -73,12 +76,14 @@ def _meet(a, b):
         return True
     if a[2] <= b[1] or b[2] <= a[1]:
         return False
+    if a[4] and b[4] and (a[4][1] <= b[4][0] or b[4][1] <= a[4][0]):
+        return False
     return not (a[3] == b[3] and a[3] > 1 and (a[1] - b[1]) % a[3] != 0)
 
 
 def _cost(o, q):
     if q == "g":
-        return ISSUE
+        return ISSUE if o.get("sent") else 0.15 + 0.002 * (o["w"][0][2] - o["w"][0][1])
     if o.get("dma"):
         return 0.05
     w = o["w"][0]
@@ -99,7 +104,8 @@ def _order(progs):
             i = at + x
             o["core"], o["x"] = core, x
             if o.get("sent"):
-                sent[o["dst"], o["name"]] = i
+                for key in o["to"]:
+                    sent[key] = i
                 if core not in first:
                     first.add(core)
                     o["first"] = FIRST
@@ -110,7 +116,7 @@ def _order(progs):
                 hit = any(_meet(a, b) for a in o["r"] + o["w"] for b in p["w"]) or any(_meet(a, b) for a in o["w"] for b in p["r"])
                 if not hit and (p["q"] != o["q"] or "alt" in o or "alt" in p):
                     hit = any(_bank(a) and _meet(a, b) for a in o["r"] for b in p["r"])
-                if hit or "behind" in o and o["behind"] in p["w"]:
+                if hit:
                     pre[i].append(at + y)
             if o["q"] == "g" or o.get("dma"):
                 if o["q"] in line and line[o["q"]] not in pre[i]:
@@ -128,18 +134,22 @@ def _order(progs):
         for j in pre[i]:
             post[j].append(i)
 
+    def cost(o, q):
+        return _cost(o, q) * (1.0 if q == "g" or o.get("dma") else SLOW)
+
     def lag(o):
         return HOP + o["busy"] if o.get("sent") else LOAD + o["busy"] if o.get("dma") else 0.0 if o["q"] == "arr" else WAKE
     way, left, todo = [0.0] * n, [len(p) for p in post], [i for i in range(n) if not post[i]]
     while todo:
         i = todo.pop()
         o = ops[i]
-        way[i] = (0.0 if o["q"] == "arr" else _cost(o, o["q"])) + max(
+        way[i] = (0.0 if o["q"] == "arr" else cost(o, o["q"])) + max(
             [way[k] + (0.0 if i in soft[k] else lag(o)) for k in post[i]] + [lag(o)])
         for j in pre[i]:
             left[j] -= 1
             if not left[j]:
                 todo.append(j)
+    way = [w + JITTER * ((i * 7919 + SEED * 104729) % 1009 / 1009 - 0.5) for i, w in enumerate(way)]
     left = [len(p) for p in pre]
     ready = {i: 0.0 for i in range(n) if not left[i]}
     free, busy, out, can = {}, {}, {core: [] for core in progs}, [0.0] * n
@@ -154,18 +164,18 @@ def _order(progs):
                       key=lambda k: (-way[k], k))
         for i in mine:
             if q0 == "arr" or when[i, q0] <= t0 + PEEK and all(
-                    when[i, q0] + _cost(ops[i], q0) + way[k] <= max(when[k, q0] + way[k] + SLACK, when[k, q0] + _cost(ops[k], q0) + way[i])
+                    when[i, q0] + cost(ops[i], q0) + way[k] <= max(when[k, q0] + way[k] + SLACK, when[k, q0] + cost(ops[k], q0) + way[i])
                     for k in mine if way[k] > way[i]):
                 break
         else:
             i = mine[0]
         o = ops[i]
         q = o["q"]
-        if "alt" in o and when[i, "s"] + _cost(o, "s") <= when[i, "v"] + _cost(o, "v") + LEAN:
+        if "alt" in o and when[i, "s"] + cost(o, "s") <= when[i, "v"] + cost(o, "v") + LEAN:
             q = "s"
         end = when[i, q]
         if q != "arr":
-            end += _cost(o, q) + o.get("first", 0.0)
+            end += cost(o, q) + o.get("first", 0.0)
             free[core, q] = end
             out[core].append((o["x"], q))
         done = end + lag(o)
@@ -249,7 +259,7 @@ def _calls(core, T, topo):
     r = T.rank_of(core)
     A, ACT = AluOpType, ActivationFunctionType
     ops = []
-    up, down, up2, down2 = [T.cores[(r + k) % N] for k in (1, -1, 2, -2)]
+    up, down, up2, down2, down3 = [T.cores[(r + k) % N] for k in (1, -1, 2, -2, -3)]
     last = int(r == N - 1)
     sh = int(r == 0)
     near = topo.chip(up) == topo.chip(core)
@@ -269,6 +279,9 @@ def _calls(core, T, topo):
     def plain(*vs):
         return all(SCRATCH[v[0]][2] == "float32" for v in vs)
 
+    def on(v, rows):
+        return v[:4] + (rows,)
+
     def tt(o, a, b, f):
         op("v", lambda q: q.tensor_tensor(ap(o), ap(a), ap(b), f), [a, b], [o], k=1 if _bank(a) else 2)
 
@@ -286,11 +299,18 @@ def _calls(core, T, topo):
         k = {"alt": lambda e: e.activation(ap(o), ap(a), ACT.Copy)} if plain(o, a) else {}
         op("v", lambda e: e.tensor_copy(ap(o), ap(a)), [a], [o], **k)
 
-    def fill(o, c):
-        op("v", lambda q: q.memset(ap(o), c), [], [o])
+    def both(o, a):
+        cp(on(o, LO), on(a, LO))
+        cp(on(o, HI), on(a, LO))
 
-    def scan(o, a, b, f0, f1):
-        op("v", lambda q: q.tensor_tensor_scan(ap(o), ap(a), ap(b), 0.0, f0, f1), [a, b], [o])
+    def fill(o, c):
+        op("v", lambda q: q.memset(ap(o), c), [], [o], k=0.5 if SCRATCH[o[0]][2] == "bfloat16" else 1)
+
+    def const(o, c):
+        ts(o, V("MASK", 0, len(range(o[1], o[2], o[3])), 1, o[4]), 0.0, A.mult, c, A.add)
+
+    def scan(o, a, b, f0, f1, init=0.0):
+        op("v", lambda q: q.tensor_tensor_scan(ap(o), ap(a), ap(b), init, f0, f1), [a, b], [o])
 
     def flip(o, a):
         op("v", lambda q: q.transpose(ap(o), ap(a)), [a], [o])
@@ -311,19 +331,17 @@ def _calls(core, T, topo):
         op("t", lambda q: q.matmul_mx(ap(o), ap(sides[0]), ap(sides[1]), ap(sides[2]), ap(sides[3]), start, stop),
            sides, [o], acc=not start)
 
-    def half(right, mb, lo, hi):
+    def half(right, mb, lo, hi, b0=0):
         for t in range(4):
-            mm(t, "W", 128 * t + (512 if right else 0), mb, lo, hi, start=not right, stop=right)
+            mm(b0 + t, "W", 128 * t + (512 if right else 0), mb, lo, hi, start=not right, stop=right)
 
     c05 = float(np.float32(0.05))
 
-    def relu(tile, col, lo, hi, both=True):
-        for t in range(4):
-            o, a = V(tile, 4 * col + t, 4 * (col + hi - lo), 4), V("P%d" % t, lo, hi)
+    def relu(tile, col, lo, hi, b0=0, only=None):
+        for t in range(4) if only is None else [only]:
+            o, a = V(tile, 4 * col + t, 4 * (col + hi - lo), 4), V("P%d" % (b0 + t), lo, hi)
             op("v", lambda q, o=o, a=a: q.tensor_scalar(ap(o), ap(a), 0.0, c05, A.max, A.mult), [a], [o],
                alt=lambda q, o=o, a=a: q.activation(ap(o), ap(a), ACT.Relu, scale=c05))
-            if not both:
-                ops[-1].update(q="s", fn=ops[-1].pop("alt"))
 
     def pick(ob, olo, wb, wlo, whi, off):
         n = 16 * (off[2] - off[1])
@@ -331,6 +349,10 @@ def _calls(core, T, topo):
         op("v", lambda q: q.tensor_copy(ap(oq).bitcast(dt.uint32), ap(wq).bitcast(dt.uint32).indirect(ap(off))),
            [wq, off], [oq], k=1.5, fix=0.05)
         op("s", lambda q: q.activation(ap(os_), ap(ws_).indirect(ap(off)), ACT.Copy), [ws_, off], [os_], k=1.5, fix=0.05)
+
+    def gather(o, win, off, mk):
+        op("v", lambda q: q.tensor_tensor(ap(o), ap(win).indirect(ap(off)), ap(mk), A.mult), [win, off, mk], [o],
+           k=1.5, fix=0.05)
 
     def engines(src, dst, kind):
         es = topo.engines(src, dst)
@@ -342,8 +364,24 @@ def _calls(core, T, topo):
         cast = (lambda v: ap(v).bitcast(dt.uint8)) if a[0][0] == "Q" else ap
         rate = ON if topo.chip(dst) == topo.chip(core) else OFF
         op("g", lambda q: q.remote_dma(cast(o), cast(a), T.sem[sem], T.sem["sent"], pid, rid, sum(1 << e for e in es)),
-           [a], [], sent=len(es), name=sem, dst=dst, es=es,
+           [a], [], sent=len(es), to=[(dst, sem)], es=es,
            busy=128 // len(es) * (ROW + (a[2] - a[1]) * (1 if a[0][0] == "S" else 4) / rate))
+
+    def apart(src, dsts):
+        a, b = [topo.engines(src, d) for d in dsts]
+        if len(a) > len(b):
+            return [e for e in a if e not in b], b
+        return a[:len(a) // 2], a[len(a) // 2:]
+
+    def send_both(dsts, outs, ins, sems):
+        es = apart(core, dsts)
+
+        def transfers():
+            return [RemoteDMATransfer(dst_ids=[DstId(rid=topo.addr(d)[0], pnc=topo.addr(d)[1])], src=ap(a), dst=ap(o),
+                                      dma_engine_mask=sum(1 << e for e in m), remote_sem=T.sem[k])
+                    for d, o, a, m, k in zip(dsts, outs, ins, es, sems)]
+        op("g", lambda q: q.remote_dma_fused(transfers(), local_sem=T.sem["sent"]), ins, [], sent=len(es[0] + es[1]),
+           to=list(zip(dsts, sems)), es=es[0] + es[1], busy=128 // len(es[1]) * ROW)
 
     def send2(dst, ob, olo, ab, alo, n, sem, kind):
         send(dst, V("Q" + ob, olo, olo + n), V("Q" + ab, alo, alo + n), sem + "c", kind)
@@ -352,32 +390,35 @@ def _calls(core, T, topo):
     def dma(q, o, a, r_, w, store=False, busy=0.4):
         op(q, lambda e: e.dma_start(o, a), r_, w, dma=True, store=store, es=range(16), busy=busy)
 
-    def mask(m, at, b, lo, n):
-        tt(V(m, at, at + n), V(b, lo, lo + n), V("MASK", at % P, at % P + n), A.mult)
-
-    def turn(m, at, b, shift):
-        mask(m, at, b, shift, P - shift)
-        if shift:
-            mask(m, at + P - 1, b, 0, 1)
+    def mask(m, at, b, lo, n, rows=None):
+        tt(V(m, at, at + n, 1, rows), V(b, lo, lo + n, 1, rows), V("M4", at, at + n, 1, rows), A.mult)
 
     def fold(c, m, n, at=0):
         scan(V(c, at, at + n), V("RST", 0, n), V(m, at, at + n), A.mult, A.add)
         return V(c, at + 15, at + n, 16)
 
-    def W(name, lo=0, hi=12):
-        return V(name, lo, hi)
+    def W(name, lo=0, hi=12, rows=None):
+        return V(name, lo, hi, 1, rows)
 
-    def later(v):
-        ops[-1]["behind"] = v
+    def third(name, k, rows=None):
+        return V(name, k, 36, 3, rows)
+
+    def ps(b, lo, hi):
+        return V("P%d" % b, lo, hi)
 
     s2 = up if near else up2
+    cc = N2 + 64 + last
     for b, lo, n, s, src, kind in (("QA", RA, P, "h1c", up, "all"), ("SA", RA, P, "h1s", up, "all"),
                                    ("QA", R2, P, "r2c", s2, "all"), ("SA", R2, P, "r2s", s2, "all"),
-                                   ("QA", N2, 64, "h2c", up, "all"), ("SA", N2, 64, "h2s", up, "all"),
+                                   ("QA", N2, 64 + last, "h2c", up, "all"), ("SA", N2, 64 + last, "h2s", up, "all"),
+                                   ("QA", cc, 64 + last, "c3c", up, "all"), ("SA", cc, 64 + last, "c3s", up, "all"),
                                    ("QR", 0, P, "f4c", up, "all"), ("SR", 0, P, "f4s", up, "all"),
-                                   ("LUP1", 0, 16, "up1", down, "hi"), ("LUP2", 0, 12, "up2", down, "hi"),
-                                   ("LDN2", 0, 36, "dn2", up, "all")):
+                                   ("LUP1", 0, 4, "up1", down, "hi"), ("LUP2", 0, 8, "up2", down, "all"),
+                                   ("LDN", 0, 12, "dn", up, "all")):
         ops.append(dict(q="arr", r=[], w=[V(b, lo, lo + n)], sem=s, val=len(engines(src, core, kind))))
+    for b, s, src, k in (("LA1", "a1", r - 1, 0), ("LB3", "b3", r + 3, 1)):
+        es = apart(T.cores[src % N], [T.cores[(src + 1) % N], T.cores[(src - 3) % N]])
+        ops.append(dict(q="arr", r=[], w=[V(b, 0, 4)], sem=s, val=len(es[k])))
 
     wrap = 64 if last else 2 * int(r < 2)
     dma("y", T.XT[:, 0:768], T.x[:, 0:768], [], [V("XT", 0, 768)], busy=0.6)
@@ -387,276 +428,393 @@ def _calls(core, T, topo):
     dma("y", T.QW[:, 0:512].bitcast(dt.uint8), T.wc[:, 0:2048], [], [V("QW", 0, 512)], busy=0.7)
     dma("y", T.SW[:], T.ws[:], [], [V("SW", 0, 1024)])
     dma("y", T.QW[:, 512:1024].bitcast(dt.uint8), T.wc[:, 2048:4096], [], [V("QW", 512, 1024)], busy=0.7)
-    iota(V("IM", 0, P), [[0, 12], [1, 16]], 128, -1, False)
+    iota(V("IM", 0, 224), [[0, 14], [1, 16]], 128, -1, False)
     iota(V("IQ", 0, 2), [[0, 2]], 0, 1, False)
     iota(W("PW0"), [[16, 12]], 0, 0, True)
+    if sh:
+        iota(V("AX", 0, 368, 1, LO), [[1, 368]], OWN, 0, True)
     fill(V("SP2", 0, CAP, rows=(0, 32)), 1.0)
     fill(V("SP2", CAP, P, rows=(0, 32)), 0.0)
     fill(V("O0", 0, 8), 0)
-    fill(V("O1", 0, 8), 1)
+    fill(V("O0", 8, 16), 1)
     fill(V("RST", 0, P), 1.0)
-    fill(V("ZERO", 0, 336), 0.0)
+    cuts = [PART[k][1] for k in ("INJ", "AD", "XF", "WL")] + [SCRATCH["ZERO"][1][1]]
+    for k in range(4):
+        fill(V("ZERO", cuts[k], cuts[k + 1]), 0.0)
     fill(V("RST", 0, P, 16), 0.0)
     n1 = P + 2 * int(r < 2)
     quant("A", C1, C1 + n1, V("XT", 0, 4 * n1))
     send2(down, "A", RA, "A", C1 + sh, P, "h1", "all")
+    if sh:
+        iota(V("AX", 368, 736, 1, LO), [[1, 368]], OWN + 368, 0, True)
     if direct:
         send2(down2, "A", R2, "A", C1 + int(r < 2), P, "r2", "all")
     quant("A", BDUP, BDUP + 128, V("XT", 256, 768))
-    ts(V("IM2", 0, P), V("IM", 0, P), 15, A.bitwise_and)
+    ts(V("IM2", 0, 224), V("IM", 0, 224), 15, A.bitwise_and)
     ts(V("IQ2", 0, 2), V("IQ", 0, 2), 15, A.bitwise_and)
     quant("U", 0, 128, V("UT", 0, 512))
     cp(V("Z0", 0, 2), V("IQ2", 0, 2))
+    pick("UC", 0, "U", 0, 128, V("O0", 4, 12))
     pick("UA", 0, "U", 0, 128, V("O0", 0, 8))
-    pick("UB", 0, "U", 0, 128, V("O1", 0, 8))
+    pick("UB", 0, "U", 0, 128, V("O0", 8, 16))
     if last:
         quant("A", L7, L7 + 128, V("XT", 508, 1020))
     wide = 128 if near else P
-    mm(4, "UA", 0, "A", C1, C1 + P)
+    mm(4, "UC", 0, "A", C1, C1 + P)
     half(False, "A", C1, C1 + wide)
-    ts(V("MASK", 0, P), V("IM2", 0, P), 0, A.is_equal)
-    cp(V("AR", BDUP, BDUP + 128), V("P4", 64, P))
+    S = float(LATE - K2)
+    ts(V("MASK", 0, 144), V("IM2", 0, 144), 0, A.is_equal)
+    ts(V("M4", 0, 224), V("IM2", 0, 224), 0, A.is_equal, S, A.mult)
+
+    def ar(lo, hi):
+        return V("AR", lo - OWN, hi - OWN)
+
+    def keep(lo, hi, p):
+        cp(ar(lo, hi), p)
+        if sh:
+            cp(V("AX", lo - OWN, hi - OWN, 1, HI), on(p, HI))
+    keep(BDUP, BDUP + 128, V("P4", 64, P))
+    const(ar(LATE - 2, LATE + 64), 0.0)
     fill(V("TL", 256, 512), 0.0)
     ts(W("PW"), W("PW0"), V("Z0", 0, 1), A.add)
     ts(V("WG0", 0, 128), V("MASK", 0, 128), -1.0, A.mult, 1.0, A.add)
-    ts(V("WG1", 0, 128), V("MASK", 15, 143), 31.0, A.mult)
-    ts(V("Z2", 8, 9), V("MASK", 15, 16), -31.0, A.mult, 32.0, A.add)
-    ts(V("Z2", 9, 10), V("MASK", 15, 16), -31.0, A.mult, -1.0, A.add)
-    turn("WM", 0, "P4", 0)
+    ts(V("WG1", 0, 128), V("MASK", 15, 143), 199.0, A.mult)
+    ts(V("Z2", 9, 10), V("MASK", 15, 16), -199.0, A.mult, -1.0, A.add)
+    if r < 3:
+        mask("WM", 0, "P4", 0, P, LO)
+        mask("WM", 0, "P4", 1, P - 1, HI)
+        mask("WM", P - 1, "P4", 0, 1, HI)
+    else:
+        mask("WM", 0, "P4", 0, P)
     tt(V("WG", 0, 128), V("WG1", 0, 128), V("WG0", 0, 128), A.add)
-    a1w = fold("WC", "WM", P)
-    ts(V("INJ", 0, 64, 16), W("PW", 0, 4), float(K2), A.add)
+    fold("WC", "WM", P)
+    for b, rows in (("A1", LO), ("B3", HI)):
+        cp(W(b, 0, 4, LO), V("WC", 79, 128, 16, rows))
+        cp(W(b, 0, 4, HI), V("WC", 143, P, 16, rows))
+    send_both([up, down3], [W("LA1", 0, 4), W("LB3", 0, 4)], [W("A1", 0, 4), W("B3", 0, 4)], ["a1", "b3"])
+    cp(W("UP1", 0, 4, LO), V("WC", 15, 64, 16, LO))
+    w1 = V("WC", 79, P, 16)
+    if r in (1, 2):
+        mask("WM2", 0, "P4", 64, 128)
+        w1 = fold("WC2", "WM2", 128)
+    fill(V("T3", 256, 512), 0.0)
+    if not last:
+        pick("K", K3 - 64, "A", C1, C1 + 64, V("O0", 0, 4))
+    const(V("XF", 2, 12, 3, LO), 1.0)
+    ts(V("INJ", 0, 64, 16), W("PW", 0, 4), float(K2 - OWN), A.add)
     ts(W("EW"), W("PW"), float(P - 1), A.is_equal)
-    cp(W("UP1"), a1w)
-    ts(W("CW", 0, 8), W("PW", 4, 12), float(201 - 2 * CAP), A.add)
-    ts(V("TW", 0, 32, 4), W("PW", 4, 12), float(NEW2), A.add)
-    fill(V("R4", 0, 32), 1.0)
-    fill(V("MA", 64 + last, 65 + last), float(200 - CAP))
-    fill(V("R4", 0, 32, 4), 0.0)
-    ts(W("C1W"), W("PW"), float(C1), A.add)
-    ts(W("K2W"), W("PW"), float(K2), A.add)
-    cp(V("OFD", 1, 24, 2), W("PW"))
-    fill(V("OFD", 0, 24, 2), float(K4))
-    fill(W("C2B", 0, 4), -1.0)
-    ts(W("C2B", 4, 12), W("PW", 4, 12), float(NEW2), A.add)
+    ts(W("CW", 0, 8), W("PW", 4, 12), float(200 - 2 * CAP), A.add)
+    d1, d2, d3 = (K1B - 64 - NEW2) / 2, (NEW2 - K2) / 2, (LATE - 1 - (P - 1) - (K1B - 64)) / 2 if last else 1.0
+    ts(V("TW", 4, 48, 6), W("PW", 4, 12), NEW2 - OWN + d1 - d2 + d3 * last + d3, A.add)
+    const(V("TW", 2, 48, 6), -1.0)
+    const(V("TA", 0, 48, 6), -1.0)
+    const(V("TA", 1, 48, 6), 0.5)
+    const(V("TB", 0, 48, 6), -1.0)
+    const(V("MA", 64 + last, 65 + last), 199.5 - CAP)
+    for k, c in enumerate((d1 / d2, d2 / d3, 1.0, d3, 1.0, 0.0)):
+        const(V("R4", k, 48, 6), c)
+    ts(third("LD", 0), W("PW"), float(C1 - OWN), A.add)
+    ts(third("LD", 1), W("PW"), float(NEW2 - OWN), A.add)
+    ts(W("K2W"), W("PW"), float(K2 - OWN), A.add)
+    const(W("C2B", 0, 4), -1.0)
+    ts(W("C2B", 4, 12), W("PW", 4, 12), float(NEW2 - OWN), A.add)
+    for name, xyz in (("TV", (255.0, 65280.0, -65536.0)), ("TI", (1 - 2.0 ** -8, 2.0 ** -8 - 2.0 ** -16, 2.0 ** -16)),
+                      ("TS", (-1.0, -1.0, 3.0))):
+        for k in range(3):
+            const(third(name, k, LO), xyz[k])
+    md, mg, rsg = V("M4", 0, 64), V("M4", 0, P), "RST"
     if last:
-        ts(V("MD", 0, 63), V("MASK", 0, 63), float(LATE + 1 - K2), A.mult)
+        md = V("MD", 0, 64)
+        cp(V("MD", 0, 63), V("M4", 0, 63))
         ts(V("MD", 63, 64), V("MASK", 63, 64), float(NEW2 - K2), A.mult)
         ts(W("Z2", 0, 8), W("EW", 4, 12), -1000.0, A.mult, 1000.0, A.add)
         ts(W("EW2", 0, 8), W("EW", 4, 12), -199.0, A.mult)
         fill(V("MC", 127, 128), 0.0)
-    else:
-        ts(V("MD", 0, 64), V("MASK", 0, 64), float(LATE - K2), A.mult)
+        fill(V("TL", 0, 4), 0.0)
+        ts(W("BIG", 0, 1), W("EW", 11, 12), 1e29, A.mult)
+        ts(W("NE", 0, 1), W("EW", 11, 12), -1.0, A.mult, 1.0, A.add)
+        cp(W("PWX", 4, 11), W("PW", 4, 11))
+    if sh or last:
+        const(V("WMX", 48, 63), 0.0)
+        const(V("WMX", P - 1, P), 0.0)
     pd = W("PW")
     if sh:
         ts(W("Z7"), W("EW"), float(-P), A.mult, 1.0, A.add)
         tt(W("Z8"), W("Z7"), W("PW"), A.add)
         pd = W("Z8")
+        md, mg, rsg = V("MD", 0, 64), V("MG", 0, 208), "RSG"
+        cp(V("MD", 0, 64, 1, LO), V("M4", 0, 64, 1, LO))
+        cp(V("MD", 0, 64, 1, HI), V("M4", 15, 79, 1, HI))
+        ts(V("MG", 0, 208, 1, LO), V("M4", 15, 223, 1, LO), 1 / S, A.mult)
+        cp(V("MG", 0, 208, 1, HI), V("M4", 15, 223, 1, HI))
+        const(V("AX", LATE - OWN, LATE - OWN + 64, 1, HI), 0.0)
+        fill(V("RSG", 0, 208), 1.0)
+        fill(V("RSG", 1, 208, 16), 0.0)
     ts(W("Z3"), pd, 64.0 - last, A.is_lt, float(N2 + last - RA), A.mult)
     ts(W("Z4"), pd, float(RA), A.add)
-    ts(V("F12", 0, 24, 2), pd, float(R2), A.add)
+    ts(third("XD", 2), pd, float(R2), A.add)
     if last:
         ts(W("Z5"), W("EW"), float(N2 - RA - (P - 1)), A.mult)
         tt(W("Z6"), W("Z3"), W("Z4"), A.add)
-        tt(W("R12W"), W("Z6"), W("Z5"), A.add)
+        tt(third("XD", 0), W("Z6"), W("Z5"), A.add)
     else:
-        tt(W("R12W"), W("Z3"), W("Z4"), A.add)
+        tt(third("XD", 0), W("Z3"), W("Z4"), A.add)
 
     half(True, "A", RA, RA + wide)
     relu("TL", 128, 0, 64)
     quant("A", JUNK, JUNK + 128, V("TL", 256, 768))
     if hand:
         send2(down, "A", R2, "A", RA, P, "r2", "all")
-    send2(down, "A", N2, "A", NEW2, 64, "h2", "all")
-
-    mm(4, "UA", 0, "A", NEW2, NEW2 + 128)
-    mask("WM1", 0, "P4", 0, 64)
+    send2(down, "A", N2, "A", NEW2, 64 + sh, "h2", "all")
+    if hand:
+        send2(down, "A", N2 + 64 + sh, "A", R2, 64 + sh, "c3", "all")
+    cp(W("AD", 4, 8, LO), W("LB3", 0, 4, LO))
+    cp(W("AD", 8, 12, LO), W("LB3", 0, 4, HI))
+    cp(W("AD", 4, 8, HI), W("LA1", 0, 4, LO))
+    cp(W("AD", 8, 12, HI), W("LA1", 0, 4, HI))
+    cp(W("AD", 0, 4, HI), W("LUP1", 0, 4, LO))
     if last:
-        cp(V("AR", NEW2, NEW2 + 64), V("P4", 0, 64))
-    cp(W("UP1", 12, 16), fold("WC1", "WM1", 64))
-    send(up, W("LUP1", 0, 16), W("UP1", 0, 16), "up1", "hi")
-    mm(5, "UB", 0, "A", R1B - 2, R1B + 128)
-    mask("WMX", P + 64 - sh - last, "P5", 2 - last, 128)
-    mm(6, "UA", 0, "A", C1 + 62, C1 + P, stop=False)
-    mm(6, "UB", 0, "A", R1B - 2, R1B + 128, start=False)
-    cp(V("S1B", 0, 130), V("P6", 0, 130))
+        tt(W("AD", 11, 12, LO), W("AD", 11, 12, LO), W("BIG", 0, 1, LO), A.add)
+    tt(W("RS", 0, 8), w1, W("AD", 4, 12), A.add)
+    ts(V("TB", 1, 48, 6), W("RS", 0, 8), 0.5, A.mult)
+
+    if not near:
+        half(False, "A", C1 + 64, C1 + P, 4)
+        fill(V("TK", 0, 256), 0.0)
+        half(True, "A", R2 + 64, R2 + P, 4)
+        relu("TK", 256, 64, P)
+        relu("TK", 128, 0, 128, 4)
+        quant("A", K2 + 64, K1B + 128, V("TK", 512, 1536))
+    b1, b2, b3, b4, bl = (4, 5, 6, 7, 0) if near else (0, 1, 2, 3, 4)
+    mm(b3, "UA", 0, "A", C1 + 62, C1 + P, stop=False)
+    mm(b3, "UB", 0, "A", R1B - 2, R1B + 128, start=False)
+    cp(V("S1B", 0, 130), ps(b3, 0, 130))
+    if near:
+        mm(b2, "UB", 0, "A", R1B - 2, R1B + 128)
+        mask("WMX", 64 - sh, "P%d" % b2, 2, 128)
+    mm(b1, "UC", 0, "A", NEW2, NEW2 + 128)
+    mask("WM1", 0, "P%d" % b1, 0, 64)
+    if last:
+        cp(ar(NEW2, NEW2 + 64), ps(b1, 0, 64))
+    cp(W("UP1", 0, 4, HI), on(fold("WC1", "WM1", 64), LO))
+    send(up, W("LUP1", 0, 4), W("UP1", 0, 4), "up1", "hi")
+    if not hand:
+        send2(down, "A", N2 + 64 + sh, "A", R2, 64 + sh, "c3", "all")
     if near:
         half(False, "A", C1 + 64, C1 + P)
         half(True, "A", R1B, R1B + 128)
-        relu("TK", P, 0, 128)
+        relu("TK", 256, 0, 128)
+        half(False, "A", NEW2, NEW2 + P)
+        quant("A", K1B, K1B + 128, V("TK", 1024, 1536))
+        half(True, "A", R2, R2 + P)
+        mm(7, "UA", 0, "A", NEW2, NEW2 + P, stop=False)
+        mm(7, "UB", 0, "A", R2, R2 + P, start=False)
+        tt(V("MC", 0, 128), V("P7", 64, P), V("S1B", 2, 130), A.is_le)
+        cp(V("S2L", 0, 64), V("P7", 0, 64))
+        relu("TK", 64, 0, P)
+        mm(4, "UC", 0, "A", K1B, K1B + 128)
+        keep(K1B, K1B + 128, V("P4", 0, 128))
+        quant("A", K2, K2 + P, V("TK", 256, 1024))
+        mm(4, "UC", 0, "A", K2, K2 + P)
+        keep(K2, K2 + P, V("P4", 0, P))
     else:
-        relu("TK", P, 64, P)
-    half(False, "A", NEW2, NEW2 + P)
-    quant("A", K1B, K1B + 128, V("TK", 4 * P, 1280))
-    mm(6, "UB", 0, "A", R2, R2 + P)
-    half(True, "A", R2, R2 + P)
-    mm(7, "UA", 0, "A", NEW2, NEW2 + P, stop=False)
-    mm(7, "UB", 0, "A", R2, R2 + P, start=False)
-    tt(V("MC", 0, 128 - last), V("P7", 64, P - last), V("S1B", 2, 130 - last), A.is_le)
-    cp(V("S2L", last, 64 + last), V("P7", 0, 64))
-    if last:
-        tt(V("MA", 64, 65), V("P7", 63, 64), V("S1B", 1, 2), A.is_le)
-    relu("TK", 0, 0, P)
-    mm(4, "UA", 0, "A", K1B, K1B + 128)
-    cp(V("AR", K1B, K1B + 128), V("P4", 0, 128))
-    if last:
-        cp(V("S2L", 0, 1), V("P7", P - 1, P))
+        mm(b2, "UA", 0, "A", C1 + 64, C1 + P, stop=False)
+        mm(b2, "UB", 0, "A", R2 + 64, R2 + P, start=False)
+        tt(V("MC", 0, 128 - last), ps(b2, 0, 128 - last), V("S1B", 2, 130 - last), A.is_le)
+        if last:
+            cp(V("S2L", 0, 1), ps(b2, 127, 128))
+        mm(b3, "UA", 0, "A", NEW2, NEW2 + 128, stop=False)
+        mm(b3, "UB", 0, "A", R2, R2 + 128, start=False)
+        cp(V("S2L", last, 64 + last), ps(b3, 0, 64))
+        if last:
+            tt(V("MA", 64, 65), ps(b3, 63, 64), V("S1B", 1, 2), A.is_le)
+        mm(b2, "UC", 0, "A", K2 + 64, K1B + 128)
+        cp(ar(K2 + 64, K1B + 128), ps(b2, 0, 256))
+        for t in range(4):
+            mm(t % 3, "W", 128 * t, "A", NEW2, NEW2 + 128, stop=False)
+            mm(t % 3, "W", 128 * t + 512, "A", R2, R2 + 128, start=False)
+            relu("TK", 64, 0, 64, t % 3 - t, t)
+        quant("A", K2 - 64, K2 + 64, V("TK", 0, 512))
+        mm(b2, "UC", 0, "A", K2, K2 + 128)
+        cp(ar(K2, K2 + 64), ps(b2, 0, 64))
+        mm(b3, "UB", 0, "A", R1B - 2, R1B + 128)
+        mask("WMX", 64 - last, "P%d" % b3, 2 - last, 128)
     scan(V("CUM", 0, 128), V("MC", 0, 128), V("MC", 0, 128), A.add, A.max)
     scan(V("MCS", 0, 128), V("WG", 0, 128), V("MC", 0, 128), A.mult, A.add)
-    mcs = V("MCS", 15, 128, 16)
-    ts(W("MW", 0, 8), mcs, V("Z2", 8, 9), A.is_ge, 168.0, A.mult)
-    ts(W("SUF", 0, 8), mcs, V("Z2", 9, 10), A.mult)
-    tt(W("CUW", 0, 8), W("SUF", 0, 8), V("CUM", 15, 128, 16), A.add)
-    quant("A", K2, K2 + P, V("TK", 0, 4 * P))
-    tt(W("AB", 0, 8), W("CUW", 0, 8), W("MW", 0, 8), A.subtract)
+    ts(W("SUF", 0, 8), V("MCS", 15, 128, 16), V("Z2", 9, 10), A.mult)
+    tt(W("AB", 0, 8), W("SUF", 0, 8), V("CUM", 15, 128, 16), A.add)
     tt(W("AB", 8, 16), W("AB", 0, 8), W("CW", 0, 8), A.subtract)
     if last:
         tt(W("AB", 16, 24), W("AB", 0, 8), W("Z2", 0, 8), A.add)
-    mm(4, "UA", 0, "A", K2, K2 + P)
-    cp(V("AR", K2, K2 + P), V("P4", 0, P))
-    turn("WMX", 2 * P, "P6", sh)
-    b3w = fold("WCX", "WMX", P, 2 * P)
+    ts(W("OCF", 0, 8), W("SUF", 0, 8), -200.0, A.is_le, float(K1B - 64 - K2), A.mult)
+    tt(W("OCG", 0, 8), W("OCF", 0, 8), W("PW", 0, 8), A.add)
+    cp(W("OC", 0, 8), W("OCG", 0, 8))
+    gather(V("WMC", 0, 128), ar(K2 + 64, K1B + 128), W("OC", 0, 8), V("M4", 0, 128))
+    tt(V("TA", 2, 48, 6), fold("WCC", "WMC", 128), W("AD", 4, 12), A.add)
     left = L7 if last else C1 - 64
-    half(False, "A", left, left + 128)
-    mm(7, "UA", 0, "A", left, left + 128, stop=False)
+    half(False, "A", left, left + 128, bl)
+    mm(b4, "UA", 0, "A", left, left + 128, stop=False)
 
-    mm(7, "UB", 0, "A", N2 - 64, N2 + 64, start=False)
-    half(True, "A", N2 - 64, N2 + 64)
-    mm(5, "UB", 0, "A", N2 - 64, N2 + 64)
-    tt(V("MA", 0, 64), V("P7", 64, 128), V("S2L", 0, 64), A.is_ge)
-    later(V("QA", K2, K2 + P))
+    mm(b4, "UB", 0, "A", N2 - 64, N2 + 64, start=False)
+    half(True, "A", N2 - 64, N2 + 64, bl)
+    bn = b2 if near else b3
+    mm(bn, "UB", 0, "A", N2 - 64, N2 + 64)
+    tt(V("MA", 0, 64), ps(b4, 64, 128), V("S2L", 0, 64), A.is_ge)
     ma, mn, nn = V("MA", last, 64 + last), V("MA", last, 65 + last), V("ONE", 8, 9)
-    op("v", lambda q: q.tensor_reduce(ap(nn), ap(mn), AxisListType.X, A.add, negate=True), [mn], [nn])
-    relu("TL", 0, 64, 128, False)
+    op("v", lambda q: q.tensor_reduce(ap(nn), ap(mn), AxisListType.X, A.add, negate=True), [mn], [nn, W("WM1", 0, 65)],
+       alt=lambda q: q.activation(ap(W("WM1", 0, 65)), ap(mn), ACT.Identity, scale=-1.0, accum_out=ap(nn)))
+    relu("TL", last, 64, 128, bl)
     if last:
-        z, e7, m0 = W("Z9", 0, 1), W("EW2", 7, 8), V("MA", 0, 1)
-        tt(z, e7, m0, A.mult)
-    tt(V("MK", 0, 64), ma, V("MD", 0, 64), A.mult)
+        z = W("Z9", 0, 1)
+        ts(z, W("EW2", 7, 8), V("MA", 0, 1), A.mult)
+    tt(V("MK", 0, 64), ma, md, A.mult)
     if last:
         ts(V("AB", 7, 24, 8), V("AB", 7, 24, 8), z, A.add)
     scan(V("SC", 0, 64), V("INJ", 0, 64), V("MK", 0, 64), A.max, A.add)
-    ts(V("TW", 1, 32, 4), W("AB", 0, 8), nn, A.is_le, float(K1B - 64 - NEW2), A.mult)
-    ts(V("TW", 2, 32, 4), W("AB", 8, 16), nn, A.is_ge, float(K2 - NEW2), A.mult)
+    for k in range(2 + last):
+        o, a = V("TW", k + k // 2, 48, 6), W("AB", 8 * k, 8 * k + 8)
+        op("s", lambda q, o=o, a=a: q.activation(ap(o), ap(a), ACT.Sign, bias=ap(nn), scale=-1.0), [a, nn], [o])
     if last:
-        ts(V("TW", 3, 32, 4), W("AB", 16, 24), nn, A.is_le, float(LATE - (P - 1) - (K1B - 64)), A.mult)
-    cp(W("O3", 0, 4), V("SC", 15, 64, 16))
-    scan(V("TD", 0, 32), V("R4", 0, 32), V("TW", 0, 32), A.mult, A.add)
-    if sh or last:
-        mask("WMX", P, "P5", 65, 63)
-        mask("WMX", 2 * P - 1, "P5", 64, 1)
+        ts(W("Z9", 2, 3), W("TW", 45, 46), S / 2, A.mult, S / 2, A.add)
+    if sh:
+        both(W("O3", 0, 4), V("SC", 15, 64, 16))
+        cp(W("O3", 12, 13), W("O3", 0, 1))
     else:
-        mask("WMX", P, "P5", 64, 64)
-    cp(W("O3", 4, 12), V("TD", 3, 32, 4))
+        cp(W("O3", 0, 4), V("SC", 15, 64, 16))
 
-    quant("A", LATE, LATE + 128, V("TL", 0, 512))
-    mm(7, "UA", 0, "A", LATE, LATE + 128)
-    cp(V("AR", LATE, LATE + 64), V("P7", 0, 64))
+    rows = LO if sh or last else None
+    scan(W("SA1", 0, 48, rows), W("TW", 0, 48, rows), W("TA", 0, 48, rows), A.add, A.mult)
+    scan(W("SB1", 0, 48, rows), W("TW", 0, 48, rows), W("TB", 0, 48, rows), A.add, A.mult)
+    tt(W("UP2", 4, 12, rows), V("SB1", 1, 48, 6, rows), V("SA1", 2, 48, 6, rows), A.subtract)
+    if rows:
+        tt(W("U2S", 0, 8, rows), V("SB1", 1, 48, 6, rows), V("SA1", 2, 48, 6, rows), A.subtract)
+        send(up, W("LUP2", 0, 8), W("U2S", 0, 8), "up2", "all")
+    else:
+        send(up, W("LUP2", 0, 8), W("UP2", 4, 12), "up2", "all")
+    scan(V("TD", 0, 48), V("TW", 0, 48), V("R4", 0, 48), A.add, A.mult)
+    if sh or last:
+        mask("WMY", 0, "P%d" % bn, 65, 63)
+        mask("WMY", 79, "P%d" % bn, 64, 1)
+    else:
+        mask("WMX", 0, "P%d" % bn, 64, 64)
+    cp(W("O3", 4, 12), V("TD", 4, 48, 6))
+    lq = LATE - 2 * last
+    quant("A", lq, lq + 128, V("TL", 0, 512))
+    mm(b4, "UC", 0, "A", lq, lq + 128)
+    tt(V("WL", 0, 64 - last), ps(b4, 2 * last, 64 + last), V("MK", 0, 64 - last), A.mult)
+    if last:
+        ts(W("Z9", 4, 5), ps(b4, 1, 2), W("Z9", 2, 3), A.mult)
+    scan(V("CL", 0, 64 + sh), V(rsg, 0, 64 + sh), V("WL", 0, 64 + sh), A.mult, A.add)
     mm(6, "U", 0, "A", NEW2, NEW2 + P)
     cp(V("Y", 0, P), V("P6", 0, P))
     dma("y", T.y[:, 0:P], T.Y[:, 0:P], [V("Y", 0, P)], [], store=True)
-    o3 = W("O3F")
-    ar, m3, mk = V("AR", 0, R2), V("WM3", 0, P), V("MASK", 0, P)
-    op("v", lambda q: q.tensor_tensor(ap(m3), ap(ar).indirect(ap(W("O3"))), ap(mk), A.mult), [ar, W("O3"), mk], [m3],
-       k=1.5, fix=0.05)
-    cp(W("UP2"), fold("WC3", "WM3", P))
-    send(up, W("LUP2"), W("UP2"), "up2", "hi")
-    pick("K", 0, "A", 0, R2, W("O3"))
-    cp(o3, W("O3"))
-    o3d = o3
-    if sh:
-        cp(W("SI"), o3)
-        cp(W("SI", 32, 43), W("O3F", 1, 12))
-        cp(W("SI", 43, 44), W("O3F", 0, 1))
-    mm(7, "UB", 0, "K", 0, P)
-    mm(4, "U", 0, "K", 0, P)
-    turn("WMX", 0, "P7", sh)
-    if sh:
-        flip(V("ST", 0, 64), V("SI", 0, 64))
-        cp(V("SH", 0, 31), V("ST", 1, 32))
-        cp(V("SH", 15, 32, 16), V("ST", 32, 64, 16))
+    ng = 13 if sh else 12 if last else 4
+    end = min(16 * ng, P + 1)
+    gather(V("WM3", 0, 16 * ng), V("AX" if sh else "AR", 0, OEND - OWN), W("O3", 0, ng), mg[:2] + (mg[1] + 16 * ng, 1, None))
+    scan(V("WC3", 0, end), V(rsg, 0, end), V("WM3", 0, end), A.mult, A.add)
+    tt(W("UP2", 0, min(ng, 12), HI), V("WC3", 15 + sh, end, 16, HI), W("AD", 0, min(ng, 12), HI), A.add)
+    tt(W("UP2", 0, 4, HI), W("UP2", 0, 4, HI), V("CL", 15 + sh, 64 + sh, 16, HI), A.add)
     if sh or last:
-        fold("WCX", "WMX", P, P)
-    else:
-        fold("WCX", "WMX", 64, P)
-        fold("WCX", "WMX", 128, P + 64)
-    tt(W("S2D", 0, 4), V("WCX", P + 15, P + 64, 16), W("LUP1", 12, 16), A.add)
-    tt(W("S2D", 4, 12), V("WCX", P + 79, 2 * P, 16), W("LUP1", 4, 12), A.add)
-    tt(W("S1D"), fold("WCX", "WMX", P), W("LUP1"), A.add)
-    cp(W("DN2", 0, 12), b3w)
+        ts(W("UP2", 11, 12, HI), W("UP2", 11, 12, HI), W("CL", 0, 1, HI) if sh else W("Z9", 4, 5, HI), A.add)
+    o3 = third("LD", 2)
+    cp(o3, W("O3"))
     if sh:
-        flip(V("SI", 0, 32), V("SH", 0, 32))
-        o3d = W("SI")
-    m12, kd = W("DN2", 12, 24), W("DN2", 24, 36)
-    tt(W("F0"), W("R12W"), o3d, A.subtract)
-    tt(m12, W("S1D"), W("S2D"), A.max)
-    tt(kd, W("S2D"), W("S1D"), A.is_gt)
-    send(down, W("LDN2", 0, 36), W("DN2", 0, 36), "dn2", "all")
-    cp(V("Y", P, 2 * P), V("P4", 0, P))
-    tt(W("F1"), W("F0"), kd, A.mult)
-    tt(V("F12", 1, 24, 2), W("F1"), o3d, A.add)
-    tt(W("S3D"), W("LUP2"), b3w, A.add)
-    tt(V("K3D", 1, 24, 2), W("S3D"), m12, A.is_gt)
-    scan(V("XS", 0, 24), V("K3D", 0, 24), V("F12", 0, 24), A.mult, A.max)
-    cp(W("OS"), V("XS", 1, 24, 2))
-    pick("S", 0, "A", 0, QEND, W("OS"))
+        cp(third("XD", 1, LO), V("WC3", 16, P + 1, 16, LO))
+    else:
+        ts(third("XD", 1), W("O3"), float(OWN), A.add)
+    if sh or last:
+        fold("WCX", "WMX", 144, 48)
+        fold("WCY", "WMY", 80)
+        cp(W("S2D", 0, 3, HI), W("LUP1", 0, 3, HI))
+        tt(W("S2D", 3, 4, HI), V("WCX", 63, 64, 1, HI), W("LUP1", 3, 4, HI), A.add)
+        tt(W("S2D", 4, 12, HI), V("WCX", 79, P, 16, HI), W("AD", 4, 12, HI), A.add)
+        tt(W("S2D", 0, 4, HI), W("S2D", 0, 4, HI), V("WCY", 15, 64, 16, HI), A.add)
+        ts(W("S2D", 11, 12, HI), W("S2D", 11, 12, HI), V("WCY", 79, 80, 1, HI), A.add)
+    else:
+        fold("WCX", "WMX", 64)
+        fold("WCX", "WMX", 128, 64)
+        tt(W("S2D", 0, 4, HI), V("WCX", 15, 64, 16, HI), W("LUP1", 0, 4, HI), A.add)
+        tt(W("S2D", 4, 12, HI), V("WCX", 79, P, 16, HI), W("AD", 4, 12, HI), A.add)
+    s1d, s2d = W("UP2", rows=HI), W("S2D", rows=HI)
+    tt(W("DN", rows=LO), s1d, s2d, A.min)
+    tt(W("DN", rows=HI), s2d, s1d, A.is_ge)
+    send(down, W("LDN"), W("DN"), "dn", "all")
+    tt(third("XF", 1, LO), s2d, s1d, A.is_lt)
+    tt(V("XF", 14, 36, 3, LO), W("LUP2", 0, 8, LO), W("DN", 4, 12, LO), A.is_ge)
+    scan(W("XS", 0, 36, LO), W("XF", 0, 36, LO), W("XD", 0, 36, LO), A.mult, A.max)
+    both(W("OS"), third("XS", 2))
+    pick("S", 0, "A", 0, N2 + 64, W("OS"))
     send2(down, "R", 0, "S", 0, P, "f4", "all")
-    dma("y", T.y[:, P:2 * P], T.Y[:, P:2 * P], [V("Y", P, 2 * P), V("QR", 0, P)], [], store=True)
+    pick("K", K3, "A", OWN, OEND, W("O3", 0, 4))
     dma("y", T.sp[0:1, 0:P], T.SP2[0:1, 0:P], [V("SP2", 0, P), V("QR", 0, P)], [], store=True, busy=0.03)
-    kap, k3, l12 = W("LDN2", 24, 36), V("K3", 1, 24, 2), V("LP", 1, 24, 2)
-    ts(W("L0"), kap, float(NEW2 - C1), A.mult)
-    later(W("OS"))
-    tt(W("S3"), W("UP2"), W("LDN2"), A.add)
-    later(W("OS"))
-    tt(l12, W("L0"), W("C1W"), A.add)
-    tt(k3, W("S3"), W("LDN2", 12, 24), A.is_gt)
-    tt(V("LP", 0, 24, 2), o3, l12, A.subtract)
-    ts(W("V0"), kap, 255.0, A.mult, 1.0, A.add)
-    later(W("OS"))
-    scan(V("LS", 0, 24), V("K3", 0, 24), V("LP", 0, 24), A.mult, A.add)
-    ts(W("V1"), k3, 65536.0, A.mult)
-    cp(W("OL"), V("LS", 1, 24, 2))
-    tt(W("VAL"), W("V0"), W("V1"), A.max)
-    pick("L", 0, "A", 0, R2, W("OL"))
+    lv, cv = K3 - 64, N2 + 2 * last
+    if last:
+        pick("K", lv, "A", OWN, OEND, W("O3", 8, 12))
+    mm(6, "UA", 0, "K", lv, lv + 128, stop=False)
+    mm(6, "UB", 0, "A", cv, cv + 128, start=False)
+    mask("WS", 0, "P6", 64, 64)
+    if last:
+        mask("WS", 79, "P6", 63, 1)
+    fold("CS", "WS", 64 + 16 * last)
+    half(False, "K", lv, lv + 128, 4)
+    half(True, "A", cv, cv + 128, 4)
+    relu("T3", 0, 64 - last, 128, 4)
+    quant("K", CD, CD + 128, V("T3", 0, 512))
+    if last:
+        pick("K", CD + 97, "A", OWN, OEND, W("O3", 10, 12))
+        ts(W("S3X", 0, 1, LO), W("UP2", 11, 12, LO), W("NE", 0, 1, LO), A.mult, V("CS", 79, 80, 1, LO), A.add)
+    pick("K", K3 + 64, "A", OWN, OEND, W("O3", 4, 12))
+    mm(4, "U", 0, "K", K3, K3 + P)
+    cp(V("Y", P, 2 * P), V("P4", 0, P))
+    dma("y", T.y[:, P:2 * P], T.Y[:, P:2 * P], [V("Y", P, 2 * P), V("QR", 0, P)], [], store=True)
+    lf = W("LF", 0, 36, LO)
+    cp(third("LF", 1, LO), W("LDN", rows=HI))
+    tt(V("LF", 2, 12, 3, LO), V("CS", 15, 64, 16, LO), W("LDN", 0, 4, LO), A.is_ge)
+    tt(V("LF", 14, 36 - 3 * last, 3, LO), W("UP2", 4, 12 - last, LO), W("LDN", 4, 12 - last, LO), A.is_ge)
+    pw = "PW"
+    if last:
+        pw = "PWX"
+        tt(W("LF", 35, 36, LO), W("S3X", 0, 1, LO), W("LDN", 11, 12, LO), A.is_ge)
+        ts(W("ZM", 0, 1, LO), W("LF", 35, 36, LO), float(P - 1 - CD), A.mult, float(CD - P + 1), A.add)
+        ts(W("PWX", 11, 12, LO), W("ZM", 0, 1, LO), W("EW", 11, 12, LO), A.mult, W("PW", 11, 12, LO), A.add)
+    ts(W("ZL", 0, 4, LO), V("LF", 2, 12, 3, LO), -float(CD + last), A.mult, float(CD + last), A.add)
+    tt(W("OFS", 0, 4, LO), W("ZL", 0, 4, LO), W("PW", 0, 4, LO), A.add)
+    both(W("OF", 0, 4), W("OFS", 0, 4))
+    scan(W("VS", 0, 36, LO), lf, W("TV", 0, 36, LO), A.mult, A.add)
+    scan(W("LS", 0, 36, LO), lf, W("LD", 0, 36, LO), A.mult, A.max)
+    both(W("OL"), third("LS", 2))
+    pick("L", 0, "A", OWN, OEND, W("OL"))
     half(False, "L", 0, P)
-    ts(W("Q0"), kap, -255.0 / 256, A.mult, 1.0, A.add)
-    later(W("OS"))
+    scan(W("IS", 0, 36, LO), lf, W("TI", 0, 36, LO), A.mult, A.add)
+    scan(W("KS", 0, 36, LO), lf, W("TS", 0, 36, LO), A.mult, A.add)
     tt(W("X1"), o3, W("K2W"), A.is_equal)
     tt(W("X2"), o3, W("C2B"), A.not_equal)
     tt(W("SPW"), W("X1"), W("X2"), A.add)
-    ts(W("Q1"), k3, -65535.0 / 65536, A.mult, 1.0, A.add)
-    flip(V("VT", 0, 32), V("VAL", 0, 32))
-    tt(W("INV"), W("Q0"), W("Q1"), A.min)
-    scan(V("PR", 0, 32), V("RST", 0, 32), V("VT", 0, 32), A.mult, A.add)
-    ts(W("V2"), kap, 1.0, A.add)
-    later(W("OS"))
-    ts(V("PR", 32, 64), V("VT", 0, 32), 0.0, A.mult, V("PR", 15, 16), A.add)
-    ts(W("V3"), k3, 3.0, A.mult)
-    flip(V("PT", 0, 64), V("PR", 0, 64))
-    tt(W("KI"), W("V2"), W("V3"), A.max)
-    scan(W("EX", 1, 12), W("PT", 32, 43), W("PT", 32, 43), A.add, A.max)
-    tt(W("CU4"), W("EX"), W("PT"), A.add)
-    tt(W("D21"), W("CU4"), W("INV"), A.mult)
-    ts(W("QI"), W("D21"), -0.248, A.add)
-    ts(W("QI2"), W("QI"), 255, A.bitwise_and)
-    t4 = V("T4I", 1, 24, 2)
-    ts(t4, W("QI2"), float(CAP), A.is_le)
-    scan(V("OFS", 0, 24), V("T4I", 0, 24), V("OFD", 0, 24), A.mult, A.add)
-    tt(W("SPW", 12, 24), t4, W("KI"), A.mult)
-    cp(W("OF"), V("OFS", 1, 24, 2))
-    flip(V("SPT", 0, 32), V("SPW", 0, 32))
-    dma("y", T.sp[0:1, P:3 * P], T.SPT[0:24, 0:16], [V("SPT", 0, 32)], [], store=True, busy=0.06)
+    flip(W("VT", 0, 32, LO), V("VS", 2, 96, 3, LO))
+    scan(W("PR", 0, 32, LO), W("RST", 0, 32, LO), W("VT", 0, 32, LO), A.mult, A.add)
+    ts(W("PR", 32, 64, LO), W("PR", 0, 32, LO), -1.0, A.mult, W("PR", 15, 16, LO), A.add)
+    flip(W("PT", 0, 64, LO), W("PR", 0, 64, LO))
+    scan(W("CU4", rows=LO), W("PT", 31, 43, LO), W("PT", rows=LO), A.add, A.add, float(CAP * 65793))
+    tt(W("QI", rows=LO), W("CU4", rows=LO), third("IS", 2, LO), A.mult)
+    ts(W("QI2", rows=LO), W("QI", rows=LO), K3, A.bitwise_and)
+    tt(W("OFS", 4, 12, LO), W("QI2", 4, 12, LO), W(pw, 4, 12, LO), A.add)
+    both(W("OF", 4, 12), W("OFS", 4, 12))
+    ts(W("T4F", rows=LO), W("QI2", rows=LO), -1.0 / K3, A.mult, 1.0, A.add)
+    tt(W("SPW", 12, 24, LO), W("T4F", rows=LO), third("KS", 2, LO), A.mult)
+    flip(W("SPT", 0, 32, (0, 32)), W("SPW", 0, 32, (0, 32)))
 
     half(True, "R", 0, P)
     relu("T4", 0, 0, P)
-    quant("K", K4, K4 + P, V("T4", 0, 4 * P))
-    pick("O", 64, "K", 0, K4 + P, W("OF", 4, 12))
-    mm(4, "U", 0, "K", K4, K4 + 128)
+    quant("K", 0, P, V("T4", 0, 4 * P))
+    pick("O", 64, "K", 0, KEND, W("OF", 4, 12))
     mm(5, "U", 0, "O", 64, P)
-    pick("O", 0, "K", 0, K4 + P, W("OF", 0, 4))
+    pick("O", 0, "K", 0, KEND, W("OF", 0, 4))
+    mm(4, "U", 0, "O", 0, 128)
     dma("y", T.oc[:, :], T.QO[:, 0:P].bitcast(dt.uint8), [V("QO", 0, P)], [], store=True)
     for k in range(4):
         dma("ys"[k % 2], T.osc[4 * k:4 * k + 4, :], T.SO[32 * k:32 * k + 4, 0:P], [V("SO", 0, P)], [], store=True, busy=0.03)
     cp(V("Y", 2 * P, 2 * P + 64), V("P4", 0, 64))
     cp(V("Y", 2 * P + 64, 3 * P), V("P5", 0, 128))
     dma("y", T.y[:, 2 * P:3 * P], T.Y[:, 2 * P:3 * P], [V("Y", 2 * P, 3 * P)], [], store=True)
+    dma("s", T.sp[0:1, P:3 * P], T.SPT[0:24, 0:16], [V("SPT", 0, 32)], [], store=True, busy=0.06)
     return ops

import numpy as np
from concourse.bass import DstId, RemoteDMATransfer
from concourse.mybir import dt, AluOpType, AxisListType, ActivationFunctionType

N, P, CAP = 8, 192, 64
CODE = "float8_e4m3fn_x4"
R2, OWN, LATE, K2, K1B, JUNK, NEW2, BDUP, C1, OEND, L7, RA, R1B, N2, QEND = (
    0, 192, 224, 352, 544, 672, 736, 800, 928, 1152, 1152, 1280, 1344, 1472, 1664)
K3, CD, KEND = 128, 320, 464
LO, HI = (0, 64), (64, 128)
HOP, LOAD, WAKE, PEEK, ROW, ISSUE, FIRST, LEAN, LAND, ON, OFF = 1.0, 1.0, 0.17, 0.02, 0.028, 0.35, 1.1, 0.1, 0.3, 30000, 21000
AHEAD, SLACK, SLOW, JITTER, SEED = 0.2, 0.1, 1.25, 0.0, 0

SCRATCH = {}
PART = {}


def _buf(name, cols, dtype="float32", where="sbuf"):
    SCRATCH[name] = (where, [128, cols], dtype)


def _parts(buf, items):
    at = 0
    for name, cols in items:
        PART[name] = (buf, at)
        at += cols
    _buf(buf, at)


for _n, _c in (("A", QEND), ("K", KEND), ("W", 1024), ("U", 128), ("UA", 128), ("UB", 128), ("UC", 128), ("L", P),
               ("S", P), ("R", P), ("O", P)):
    _buf("Q" + _n, _c, CODE)
    _buf("S" + _n, _c, "uint8")
for _n, _c in (("XT", 1024), ("UT", 512), ("TL", 768), ("TK", 1536), ("T4", 768), ("T3", 512)):
    _buf(_n, _c, "bfloat16")
for _n in range(8):
    _buf("P%d" % _n, 512, where="psum")
for _n, _c in (("IM", 224), ("IM2", 224), ("IQ", 2), ("IQ2", 2), ("QI", 12), ("QI2", 12)):
    _buf(_n, _c, "int32")
for _n, _c in (("O0", 16), ("O3", 14), ("OC", 8), ("OS", 12), ("OL", 12), ("OF", 12)):
    _buf(_n, _c, "uint16")
_parts("ROWS", [("MASK", 144), ("M4", 224), ("MG", 208), ("RSG", 208), ("WM3", 208), ("WC3", 208)]
       + [(_n, P) for _n in ("WM", "WC", "RST", "WMX", "WCX")]
       + [("MD", 64), ("S1B", 144), ("MC", 128), ("MCS", 128), ("WG", 128), ("WG0", 128), ("WG1", 128), ("S2L", 80),
          ("MA", 80), ("MK", 64), ("SC", 64), ("WM1", 80), ("WC1", 64), ("CL", 80), ("CUM", 128), ("WMC", 128),
          ("WCC", 128), ("WM2", 128), ("WC2", 128), ("CS", 80), ("WCY", 80)])
_parts("LISTS", [(_n, 16) for _n in (
    "PW0", "PW", "C2B", "K2W", "CW", "EW", "EW2", "SUF", "X1", "X2", "Z0", "Z2", "Z3", "Z4", "Z5", "Z6",
    "Z7", "Z8", "Z9", "ONE", "CU4", "S2D", "OFS", "T4F", "OCF", "OCG", "RS", "BIG", "NE", "S3X", "PWX", "ZL", "ZM")]
    + [(_n, 32) for _n in ("AB", "VT")]
    + [(_n, 36) for _n in ("XD", "XS", "LD", "LS", "TV", "TI", "TS", "IS", "KS")]
    + [("R4", 48), ("TD", 48), ("SA1", 48), ("SB1", 48), ("PR", 64), ("PT", 64)])
_parts("ZERO", [("INJ", 64), ("TW", 48), ("TA", 48), ("TB", 48), ("AD", 12), ("WS", 80), ("WMY", 80), ("SPW", 32),
                ("XF", 36), ("LF", 36), ("VS", 96), ("WL", 80), ("DN", 12), ("U2S", 8)])
for _n, _c in (("Y", 3 * P), ("SP2", P), ("SPT", 32), ("UP1", 4), ("LUP1", 4), ("LA1", 4), ("A1", 4), ("B3", 4),
               ("LB3", 4), ("LDN", 12), ("UP2", 12), ("LUP2", 8), ("AR", OEND - OWN), ("AX", OEND - OWN)):
    _buf(_n, _c)
ARRIVE = ["h1c", "h1s", "r2c", "r2s", "h2c", "h2s", "c3c", "c3s", "a1", "b3", "up1", "up2", "dn", "f4c", "f4s"]
POOL = ["s%d" % _n for _n in range(130)]
SEMAPHORES = ARRIVE + ["sent", "st"] + POOL


def V(name, lo, hi, step=1, rows=None):
    name, at = PART.get(name, (name, 0))
    return (name, at + lo, at + hi, step, rows)


def _bank(a):
    return a[0][0] == "P" and a[0][1:].isdigit()


def _meet(a, b):
    if a[0] != b[0]:
        return False
    if _bank(a):
        return True
    if a[2] <= b[1] or b[2] <= a[1]:
        return False
    if a[4] and b[4] and (a[4][1] <= b[4][0] or b[4][1] <= a[4][0]):
        return False
    return not (a[3] == b[3] and a[3] > 1 and (a[1] - b[1]) % a[3] != 0)


def _cost(o, q):
    if q == "g":
        return ISSUE if o.get("sent") else 0.15 + 0.002 * (o["w"][0][2] - o["w"][0][1])
    if o.get("dma"):
        return 0.05
    w = o["w"][0]
    n = len(range(w[1], w[2], w[3]))
    if q == "t":
        return 0.0006 * (n + 16)
    return 0.001 * max(64, n * o.get("k", 1)) + o.get("fix", 0) + (0.02 if q == "s" else 0)


def _order(progs):
    ops = [o for core in progs for o in progs[core]]
    n = len(ops)
    pre, soft = [[] for _ in ops], [set() for _ in ops]
    sent, at, first = {}, 0, set()
    for core, mine in progs.items():
        line = {}
        for x, o in enumerate(mine):
            i = at + x
            o["core"], o["x"] = core, x
            if o.get("sent"):
                for key in o["to"]:
                    sent[key] = i
                if core not in first:
                    first.add(core)
                    o["first"] = FIRST
            if o["q"] == "arr":
                continue
            for y in range(x):
                p = mine[y]
                hit = any(_meet(a, b) for a in o["r"] + o["w"] for b in p["w"]) or any(_meet(a, b) for a in o["w"] for b in p["r"])
                if not hit and (p["q"] != o["q"] or "alt" in o or "alt" in p):
                    hit = any(_bank(a) and _meet(a, b) for a in o["r"] for b in p["r"])
                if hit:
                    pre[i].append(at + y)
            if o["q"] == "g" or o.get("dma"):
                if o["q"] in line and line[o["q"]] not in pre[i]:
                    pre[i].append(line[o["q"]])
                    soft[i].add(line[o["q"]])
                line[o["q"]] = i
            if o.get("acc"):
                soft[i] |= {j for j in pre[i] if ops[j]["q"] == "t"}
        at += len(mine)
    for i, o in enumerate(ops):
        if o["q"] == "arr":
            pre[i] = [sent[o["core"], o["sem"]]]
    post = [[] for _ in ops]
    for i in range(n):
        for j in pre[i]:
            post[j].append(i)

    def cost(o, q):
        return _cost(o, q) * (1.0 if q == "g" or o.get("dma") else SLOW)

    def lag(o):
        return HOP + o["busy"] if o.get("sent") else LOAD + o["busy"] if o.get("dma") else 0.0 if o["q"] == "arr" else WAKE
    way, left, todo = [0.0] * n, [len(p) for p in post], [i for i in range(n) if not post[i]]
    while todo:
        i = todo.pop()
        o = ops[i]
        way[i] = (0.0 if o["q"] == "arr" else cost(o, o["q"])) + max(
            [way[k] + (0.0 if i in soft[k] else lag(o)) for k in post[i]] + [lag(o)])
        for j in pre[i]:
            left[j] -= 1
            if not left[j]:
                todo.append(j)
    way = [w + JITTER * ((i * 7919 + SEED * 104729) % 1009 / 1009 - 0.5) for i, w in enumerate(way)]
    left = [len(p) for p in pre]
    ready = {i: 0.0 for i in range(n) if not left[i]}
    free, busy, out, can = {}, {}, {core: [] for core in progs}, [0.0] * n
    while ready:
        when = {}
        for i, t in ready.items():
            for q in [ops[i]["q"]] + (["s"] if "alt" in ops[i] else []):
                when[i, q] = max(t, free.get((ops[i]["core"], q), 0.0))
        t0, i0, q0 = min((t, i, q) for (i, q), t in when.items())
        core = ops[i0]["core"]
        mine = sorted((k for k, q in when if q == q0 and ops[k]["core"] == core and when[k, q] <= t0 + AHEAD),
                      key=lambda k: (-way[k], k))
        for i in mine:
            if q0 == "arr" or when[i, q0] <= t0 + PEEK and all(
                    when[i, q0] + cost(ops[i], q0) + way[k] <= max(when[k, q0] + way[k] + SLACK, when[k, q0] + cost(ops[k], q0) + way[i])
                    for k in mine if way[k] > way[i]):
                break
        else:
            i = mine[0]
        o = ops[i]
        q = o["q"]
        if "alt" in o and when[i, "s"] + cost(o, "s") <= when[i, "v"] + cost(o, "v") + LEAN:
            q = "s"
        end = when[i, q]
        if q != "arr":
            end += cost(o, q) + o.get("first", 0.0)
            free[core, q] = end
            out[core].append((o["x"], q))
        done = end + lag(o)
        if "busy" in o:
            done = max([done - o["busy"]] + [busy.get((core, e), 0.0) for e in o["es"]]) + o["busy"]
            for e in o["es"]:
                busy[core, e] = done - (LAND if o.get("sent") else 0.0)
        del ready[i]
        for k in post[i]:
            left[k] -= 1
            can[k] = max(can[k], end if i in soft[k] else done)
            if not left[k]:
                ready[k] = can[k]
    return out


ORDER = {}


def rank_program(g, core, T, topo):
    if T.rank_of(core) is None:
        return
    if not ORDER:
        ORDER.update(_order({c: _calls(c, T, topo) for c in T.cores}))
    ops = _calls(core, T, topo)
    for x, q in ORDER[core]:
        if q != ops[x]["q"]:
            ops[x].update(q=q, fn=ops[x]["alt"])
    _emit(g, T, [o for o in ops if o["q"] == "arr"] + [ops[x] for x, _ in ORDER[core]])


def _emit(g, T, ops):
    queues = {"g": g, "v": g.vector, "s": g.scalar, "t": g.tensor, "y": g.sync}
    known = {q: set() for q in queues}
    for i, o in enumerate(ops):
        if o["q"] == "arr":
            o["known"] = set()
            continue
        deps = []
        for j in range(i - 1, -1, -1):
            p = ops[j]
            if j in known[o["q"]]:
                continue
            hit = any(_meet(a, b) for a in o["r"] + o["w"] for b in p["w"]) or any(_meet(a, b) for a in o["w"] for b in p["r"])
            if o.get("acc") and p["q"] == "t":
                hit = False
            if not hit and p["q"] != o["q"]:
                hit = any(_bank(a) and _meet(a, b) for a in o["r"] for b in p["r"])
            if hit:
                deps.append(j)
                known[o["q"]] |= {j} | p["known"]
        o["deps"] = deps[::-1]
        o["known"] = set(known[o["q"]])
        for j in deps:
            ops[j]["used"] = True
    last, count, total = {}, {}, {"st": 0, "sent": 0}
    for i, o in enumerate(ops):
        if o["q"] == "arr":
            continue
        q = queues[o["q"]]
        for j in o["deps"]:
            q.wait_ge(T.sem[ops[j]["sem"]], ops[j]["val"])
        ins = o["fn"](q)
        if o.get("sent"):
            total["sent"] += o["sent"]
        elif o.get("store"):
            ins.then_inc(T.sem["st"], 16)
            total["st"] += 16
        elif o.get("used"):
            s = [s for s in POOL if s not in last or last[s] in o["known"]][0]
            step = 16 if o.get("dma") else 1
            last[s] = i
            count[s] = count.get(s, 0) + step
            o["sem"], o["val"] = s, count[s]
            ins.then_inc(T.sem[s], step)
    g.wait_ge(T.sem["sent"], total["sent"])
    g.sync.wait_ge(T.sem["st"], total["st"])


def _calls(core, T, topo):
    r = T.rank_of(core)
    A, ACT = AluOpType, ActivationFunctionType
    ops = []
    up, down, up2, down2, down3 = [T.cores[(r + k) % N] for k in (1, -1, 2, -2, -3)]
    last = int(r == N - 1)
    sh = int(r == 0)
    near = topo.chip(up) == topo.chip(core)
    hand = topo.chip(down) == topo.chip(core)
    direct = topo.chip(down2) != topo.chip(down)

    def ap(v):
        rows = slice(None) if v[4] is None else slice(v[4][0], v[4][1])
        return T[v[0]][rows, v[1]:v[2]] if v[3] == 1 else T[v[0]][rows, v[1]:v[2]:v[3]]

    def op(q, fn, r_, w, **k):
        ops.append(dict(q=q, fn=fn, r=[v for v in r_ if isinstance(v, tuple)], w=w, **k))

    def val(s):
        return ap(s) if isinstance(s, tuple) else s

    def plain(*vs):
        return all(SCRATCH[v[0]][2] == "float32" for v in vs)

    def on(v, rows):
        return v[:4] + (rows,)

    def tt(o, a, b, f):
        op("v", lambda q: q.tensor_tensor(ap(o), ap(a), ap(b), f), [a, b], [o], k=1 if _bank(a) else 2)

    def ts(o, a, s1, f1, s2=None, f2=None):
        k = {}
        if plain(o, a) and (f1, f2) in ((A.mult, None), (A.add, None), (A.mult, A.add)):
            sc, bi = (1.0, s1) if f1 == A.add else (s1, 0.0 if f2 is None else s2)
            k["alt"] = lambda q: q.activation(ap(o), ap(a), ACT.Identity, bias=val(bi), scale=val(sc))
        if f2 is None:
            op("v", lambda q: q.tensor_scalar(ap(o), ap(a), val(s1), None, f1), [a, s1], [o], **k)
        else:
            op("v", lambda q: q.tensor_scalar(ap(o), ap(a), val(s1), val(s2), f1, f2), [a, s1, s2], [o], **k)

    def cp(o, a):
        k = {"alt": lambda e: e.activation(ap(o), ap(a), ACT.Copy)} if plain(o, a) else {}
        op("v", lambda e: e.tensor_copy(ap(o), ap(a)), [a], [o], **k)

    def both(o, a):
        cp(on(o, LO), on(a, LO))
        cp(on(o, HI), on(a, LO))

    def fill(o, c):
        op("v", lambda q: q.memset(ap(o), c), [], [o], k=0.5 if SCRATCH[o[0]][2] == "bfloat16" else 1)

    def const(o, c):
        ts(o, V("MASK", 0, len(range(o[1], o[2], o[3])), 1, o[4]), 0.0, A.mult, c, A.add)

    def scan(o, a, b, f0, f1, init=0.0):
        op("v", lambda q: q.tensor_tensor_scan(ap(o), ap(a), ap(b), init, f0, f1), [a, b], [o])

    def flip(o, a):
        op("v", lambda q: q.transpose(ap(o), ap(a)), [a], [o])

    def iota(o, pat, base, cm, small):
        if small:
            op("g", lambda q: q.iota(ap(o), pat, base, cm, allow_small_or_imprecise_dtypes=True), [], [o])
        else:
            op("g", lambda q: q.iota(ap(o), pat, base, cm), [], [o])

    def quant(b, lo, hi, tile):
        op("v", lambda q: q.quantize_mx(ap(V("Q" + b, lo, hi)), ap(V("S" + b, lo, hi)), ap(tile)), [tile],
           [V("Q" + b, lo, hi), V("S" + b, lo, hi)], k=1.1)

    def mm(bank, sb, slo, mb, lo, hi, start=True, stop=True):
        sides = [V("Q" + sb, slo, slo + 128), V("S" + sb, slo, slo + 128), V("Q" + mb, lo, hi), V("S" + mb, lo, hi)]
        o = V("P%d" % bank, 0, hi - lo)
        op("t", lambda q: q.matmul_mx(ap(o), ap(sides[0]), ap(sides[1]), ap(sides[2]), ap(sides[3]), start, stop),
           sides, [o], acc=not start)

    def half(right, mb, lo, hi, b0=0):
        for t in range(4):
            mm(b0 + t, "W", 128 * t + (512 if right else 0), mb, lo, hi, start=not right, stop=right)

    c05 = float(np.float32(0.05))

    def relu(tile, col, lo, hi, b0=0, only=None):
        for t in range(4) if only is None else [only]:
            o, a = V(tile, 4 * col + t, 4 * (col + hi - lo), 4), V("P%d" % (b0 + t), lo, hi)
            op("v", lambda q, o=o, a=a: q.tensor_scalar(ap(o), ap(a), 0.0, c05, A.max, A.mult), [a], [o],
               alt=lambda q, o=o, a=a: q.activation(ap(o), ap(a), ACT.Relu, scale=c05))

    def pick(ob, olo, wb, wlo, whi, off):
        n = 16 * (off[2] - off[1])
        oq, wq, os_, ws_ = V("Q" + ob, olo, olo + n), V("Q" + wb, wlo, whi), V("S" + ob, olo, olo + n), V("S" + wb, wlo, whi)
        op("v", lambda q: q.tensor_copy(ap(oq).bitcast(dt.uint32), ap(wq).bitcast(dt.uint32).indirect(ap(off))),
           [wq, off], [oq], k=1.5, fix=0.05)
        op("s", lambda q: q.activation(ap(os_), ap(ws_).indirect(ap(off)), ACT.Copy), [ws_, off], [os_], k=1.5, fix=0.05)

    def gather(o, win, off, mk):
        op("v", lambda q: q.tensor_tensor(ap(o), ap(win).indirect(ap(off)), ap(mk), A.mult), [win, off, mk], [o],
           k=1.5, fix=0.05)

    def engines(src, dst, kind):
        es = topo.engines(src, dst)
        return es[-8:] if kind == "hi" else es

    def send(dst, o, a, sem, kind):
        rid, pid, _ = topo.addr(dst)
        es = engines(core, dst, kind)
        cast = (lambda v: ap(v).bitcast(dt.uint8)) if a[0][0] == "Q" else ap
        rate = ON if topo.chip(dst) == topo.chip(core) else OFF
        op("g", lambda q: q.remote_dma(cast(o), cast(a), T.sem[sem], T.sem["sent"], pid, rid, sum(1 << e for e in es)),
           [a], [], sent=len(es), to=[(dst, sem)], es=es,
           busy=128 // len(es) * (ROW + (a[2] - a[1]) * (1 if a[0][0] == "S" else 4) / rate))

    def apart(src, dsts):
        a, b = [topo.engines(src, d) for d in dsts]
        if len(a) > len(b):
            return [e for e in a if e not in b], b
        return a[:len(a) // 2], a[len(a) // 2:]

    def send_both(dsts, outs, ins, sems):
        es = apart(core, dsts)

        def transfers():
            return [RemoteDMATransfer(dst_ids=[DstId(rid=topo.addr(d)[0], pnc=topo.addr(d)[1])], src=ap(a), dst=ap(o),
                                      dma_engine_mask=sum(1 << e for e in m), remote_sem=T.sem[k])
                    for d, o, a, m, k in zip(dsts, outs, ins, es, sems)]
        op("g", lambda q: q.remote_dma_fused(transfers(), local_sem=T.sem["sent"]), ins, [], sent=len(es[0] + es[1]),
           to=list(zip(dsts, sems)), es=es[0] + es[1], busy=128 // len(es[1]) * ROW)

    def send2(dst, ob, olo, ab, alo, n, sem, kind):
        send(dst, V("Q" + ob, olo, olo + n), V("Q" + ab, alo, alo + n), sem + "c", kind)
        send(dst, V("S" + ob, olo, olo + n), V("S" + ab, alo, alo + n), sem + "s", kind)

    def dma(q, o, a, r_, w, store=False, busy=0.4):
        op(q, lambda e: e.dma_start(o, a), r_, w, dma=True, store=store, es=range(16), busy=busy)

    def mask(m, at, b, lo, n, rows=None):
        tt(V(m, at, at + n, 1, rows), V(b, lo, lo + n, 1, rows), V("M4", at, at + n, 1, rows), A.mult)

    def fold(c, m, n, at=0):
        scan(V(c, at, at + n), V("RST", 0, n), V(m, at, at + n), A.mult, A.add)
        return V(c, at + 15, at + n, 16)

    def W(name, lo=0, hi=12, rows=None):
        return V(name, lo, hi, 1, rows)

    def third(name, k, rows=None):
        return V(name, k, 36, 3, rows)

    def ps(b, lo, hi):
        return V("P%d" % b, lo, hi)

    s2 = up if near else up2
    cc = N2 + 64 + last
    for b, lo, n, s, src, kind in (("QA", RA, P, "h1c", up, "all"), ("SA", RA, P, "h1s", up, "all"),
                                   ("QA", R2, P, "r2c", s2, "all"), ("SA", R2, P, "r2s", s2, "all"),
                                   ("QA", N2, 64 + last, "h2c", up, "all"), ("SA", N2, 64 + last, "h2s", up, "all"),
                                   ("QA", cc, 64 + last, "c3c", up, "all"), ("SA", cc, 64 + last, "c3s", up, "all"),
                                   ("QR", 0, P, "f4c", up, "all"), ("SR", 0, P, "f4s", up, "all"),
                                   ("LUP1", 0, 4, "up1", down, "hi"), ("LUP2", 0, 8, "up2", down, "all"),
                                   ("LDN", 0, 12, "dn", up, "all")):
        ops.append(dict(q="arr", r=[], w=[V(b, lo, lo + n)], sem=s, val=len(engines(src, core, kind))))
    for b, s, src, k in (("LA1", "a1", r - 1, 0), ("LB3", "b3", r + 3, 1)):
        es = apart(T.cores[src % N], [T.cores[(src + 1) % N], T.cores[(src - 3) % N]])
        ops.append(dict(q="arr", r=[], w=[V(b, 0, 4)], sem=s, val=len(es[k])))

    wrap = 64 if last else 2 * int(r < 2)
    dma("y", T.XT[:, 0:768], T.x[:, 0:768], [], [V("XT", 0, 768)], busy=0.6)
    if wrap:
        dma("s", T.XT[:, 768:768 + 4 * wrap], T.x[:, 0:4 * wrap], [], [V("XT", 768, 768 + 4 * wrap)], busy=0.2)
    dma("y", T.UT[:], T.u[:], [], [V("UT", 0, 512)])
    dma("y", T.QW[:, 0:512].bitcast(dt.uint8), T.wc[:, 0:2048], [], [V("QW", 0, 512)], busy=0.7)
    dma("y", T.SW[:], T.ws[:], [], [V("SW", 0, 1024)])
    dma("y", T.QW[:, 512:1024].bitcast(dt.uint8), T.wc[:, 2048:4096], [], [V("QW", 512, 1024)], busy=0.7)
    iota(V("IM", 0, 224), [[0, 14], [1, 16]], 128, -1, False)
    iota(V("IQ", 0, 2), [[0, 2]], 0, 1, False)
    iota(W("PW0"), [[16, 12]], 0, 0, True)
    if sh:
        iota(V("AX", 0, 368, 1, LO), [[1, 368]], OWN, 0, True)
    fill(V("SP2", 0, CAP, rows=(0, 32)), 1.0)
    fill(V("SP2", CAP, P, rows=(0, 32)), 0.0)
    fill(V("O0", 0, 8), 0)
    fill(V("O0", 8, 16), 1)
    fill(V("RST", 0, P), 1.0)
    cuts = [PART[k][1] for k in ("INJ", "AD", "XF", "WL")] + [SCRATCH["ZERO"][1][1]]
    for k in range(4):
        fill(V("ZERO", cuts[k], cuts[k + 1]), 0.0)
    fill(V("RST", 0, P, 16), 0.0)
    n1 = P + 2 * int(r < 2)
    quant("A", C1, C1 + n1, V("XT", 0, 4 * n1))
    send2(down, "A", RA, "A", C1 + sh, P, "h1", "all")
    if sh:
        iota(V("AX", 368, 736, 1, LO), [[1, 368]], OWN + 368, 0, True)
    if direct:
        send2(down2, "A", R2, "A", C1 + int(r < 2), P, "r2", "all")
    quant("A", BDUP, BDUP + 128, V("XT", 256, 768))
    ts(V("IM2", 0, 224), V("IM", 0, 224), 15, A.bitwise_and)
    ts(V("IQ2", 0, 2), V("IQ", 0, 2), 15, A.bitwise_and)
    quant("U", 0, 128, V("UT", 0, 512))
    cp(V("Z0", 0, 2), V("IQ2", 0, 2))
    pick("UC", 0, "U", 0, 128, V("O0", 4, 12))
    pick("UA", 0, "U", 0, 128, V("O0", 0, 8))
    pick("UB", 0, "U", 0, 128, V("O0", 8, 16))
    if last:
        quant("A", L7, L7 + 128, V("XT", 508, 1020))
    wide = 128 if near else P
    mm(4, "UC", 0, "A", C1, C1 + P)
    half(False, "A", C1, C1 + wide)
    S = float(LATE - K2)
    ts(V("MASK", 0, 144), V("IM2", 0, 144), 0, A.is_equal)
    ts(V("M4", 0, 224), V("IM2", 0, 224), 0, A.is_equal, S, A.mult)

    def ar(lo, hi):
        return V("AR", lo - OWN, hi - OWN)

    def keep(lo, hi, p):
        cp(ar(lo, hi), p)
        if sh:
            cp(V("AX", lo - OWN, hi - OWN, 1, HI), on(p, HI))
    keep(BDUP, BDUP + 128, V("P4", 64, P))
    const(ar(LATE - 2, LATE + 64), 0.0)
    fill(V("TL", 256, 512), 0.0)
    ts(W("PW"), W("PW0"), V("Z0", 0, 1), A.add)
    ts(V("WG0", 0, 128), V("MASK", 0, 128), -1.0, A.mult, 1.0, A.add)
    ts(V("WG1", 0, 128), V("MASK", 15, 143), 199.0, A.mult)
    ts(V("Z2", 9, 10), V("MASK", 15, 16), -199.0, A.mult, -1.0, A.add)
    if r < 3:
        mask("WM", 0, "P4", 0, P, LO)
        mask("WM", 0, "P4", 1, P - 1, HI)
        mask("WM", P - 1, "P4", 0, 1, HI)
    else:
        mask("WM", 0, "P4", 0, P)
    tt(V("WG", 0, 128), V("WG1", 0, 128), V("WG0", 0, 128), A.add)
    fold("WC", "WM", P)
    for b, rows in (("A1", LO), ("B3", HI)):
        cp(W(b, 0, 4, LO), V("WC", 79, 128, 16, rows))
        cp(W(b, 0, 4, HI), V("WC", 143, P, 16, rows))
    send_both([up, down3], [W("LA1", 0, 4), W("LB3", 0, 4)], [W("A1", 0, 4), W("B3", 0, 4)], ["a1", "b3"])
    cp(W("UP1", 0, 4, LO), V("WC", 15, 64, 16, LO))
    w1 = V("WC", 79, P, 16)
    if r in (1, 2):
        mask("WM2", 0, "P4", 64, 128)
        w1 = fold("WC2", "WM2", 128)
    fill(V("T3", 256, 512), 0.0)
    if not last:
        pick("K", K3 - 64, "A", C1, C1 + 64, V("O0", 0, 4))
    const(V("XF", 2, 12, 3, LO), 1.0)
    ts(V("INJ", 0, 64, 16), W("PW", 0, 4), float(K2 - OWN), A.add)
    ts(W("EW"), W("PW"), float(P - 1), A.is_equal)
    ts(W("CW", 0, 8), W("PW", 4, 12), float(200 - 2 * CAP), A.add)
    d1, d2, d3 = (K1B - 64 - NEW2) / 2, (NEW2 - K2) / 2, (LATE - 1 - (P - 1) - (K1B - 64)) / 2 if last else 1.0
    ts(V("TW", 4, 48, 6), W("PW", 4, 12), NEW2 - OWN + d1 - d2 + d3 * last + d3, A.add)
    const(V("TW", 2, 48, 6), -1.0)
    const(V("TA", 0, 48, 6), -1.0)
    const(V("TA", 1, 48, 6), 0.5)
    const(V("TB", 0, 48, 6), -1.0)
    const(V("MA", 64 + last, 65 + last), 199.5 - CAP)
    for k, c in enumerate((d1 / d2, d2 / d3, 1.0, d3, 1.0, 0.0)):
        const(V("R4", k, 48, 6), c)
    ts(third("LD", 0), W("PW"), float(C1 - OWN), A.add)
    ts(third("LD", 1), W("PW"), float(NEW2 - OWN), A.add)
    ts(W("K2W"), W("PW"), float(K2 - OWN), A.add)
    const(W("C2B", 0, 4), -1.0)
    ts(W("C2B", 4, 12), W("PW", 4, 12), float(NEW2 - OWN), A.add)
    for name, xyz in (("TV", (255.0, 65280.0, -65536.0)), ("TI", (1 - 2.0 ** -8, 2.0 ** -8 - 2.0 ** -16, 2.0 ** -16)),
                      ("TS", (-1.0, -1.0, 3.0))):
        for k in range(3):
            const(third(name, k, LO), xyz[k])
    md, mg, rsg = V("M4", 0, 64), V("M4", 0, P), "RST"
    if last:
        md = V("MD", 0, 64)
        cp(V("MD", 0, 63), V("M4", 0, 63))
        ts(V("MD", 63, 64), V("MASK", 63, 64), float(NEW2 - K2), A.mult)
        ts(W("Z2", 0, 8), W("EW", 4, 12), -1000.0, A.mult, 1000.0, A.add)
        ts(W("EW2", 0, 8), W("EW", 4, 12), -199.0, A.mult)
        fill(V("MC", 127, 128), 0.0)
        fill(V("TL", 0, 4), 0.0)
        ts(W("BIG", 0, 1), W("EW", 11, 12), 1e29, A.mult)
        ts(W("NE", 0, 1), W("EW", 11, 12), -1.0, A.mult, 1.0, A.add)
        cp(W("PWX", 4, 11), W("PW", 4, 11))
    if sh or last:
        const(V("WMX", 48, 63), 0.0)
        const(V("WMX", P - 1, P), 0.0)
    pd = W("PW")
    if sh:
        ts(W("Z7"), W("EW"), float(-P), A.mult, 1.0, A.add)
        tt(W("Z8"), W("Z7"), W("PW"), A.add)
        pd = W("Z8")
        md, mg, rsg = V("MD", 0, 64), V("MG", 0, 208), "RSG"
        cp(V("MD", 0, 64, 1, LO), V("M4", 0, 64, 1, LO))
        cp(V("MD", 0, 64, 1, HI), V("M4", 15, 79, 1, HI))
        ts(V("MG", 0, 208, 1, LO), V("M4", 15, 223, 1, LO), 1 / S, A.mult)
        cp(V("MG", 0, 208, 1, HI), V("M4", 15, 223, 1, HI))
        const(V("AX", LATE - OWN, LATE - OWN + 64, 1, HI), 0.0)
        fill(V("RSG", 0, 208), 1.0)
        fill(V("RSG", 1, 208, 16), 0.0)
    ts(W("Z3"), pd, 64.0 - last, A.is_lt, float(N2 + last - RA), A.mult)
    ts(W("Z4"), pd, float(RA), A.add)
    ts(third("XD", 2), pd, float(R2), A.add)
    if last:
        ts(W("Z5"), W("EW"), float(N2 - RA - (P - 1)), A.mult)
        tt(W("Z6"), W("Z3"), W("Z4"), A.add)
        tt(third("XD", 0), W("Z6"), W("Z5"), A.add)
    else:
        tt(third("XD", 0), W("Z3"), W("Z4"), A.add)

    half(True, "A", RA, RA + wide)
    relu("TL", 128, 0, 64)
    quant("A", JUNK, JUNK + 128, V("TL", 256, 768))
    if hand:
        send2(down, "A", R2, "A", RA, P, "r2", "all")
    send2(down, "A", N2, "A", NEW2, 64 + sh, "h2", "all")
    if hand:
        send2(down, "A", N2 + 64 + sh, "A", R2, 64 + sh, "c3", "all")
    cp(W("AD", 4, 8, LO), W("LB3", 0, 4, LO))
    cp(W("AD", 8, 12, LO), W("LB3", 0, 4, HI))
    cp(W("AD", 4, 8, HI), W("LA1", 0, 4, LO))
    cp(W("AD", 8, 12, HI), W("LA1", 0, 4, HI))
    cp(W("AD", 0, 4, HI), W("LUP1", 0, 4, LO))
    if last:
        tt(W("AD", 11, 12, LO), W("AD", 11, 12, LO), W("BIG", 0, 1, LO), A.add)
    tt(W("RS", 0, 8), w1, W("AD", 4, 12), A.add)
    ts(V("TB", 1, 48, 6), W("RS", 0, 8), 0.5, A.mult)

    if not near:
        half(False, "A", C1 + 64, C1 + P, 4)
        fill(V("TK", 0, 256), 0.0)
        half(True, "A", R2 + 64, R2 + P, 4)
        relu("TK", 256, 64, P)
        relu("TK", 128, 0, 128, 4)
        quant("A", K2 + 64, K1B + 128, V("TK", 512, 1536))
    b1, b2, b3, b4, bl = (4, 5, 6, 7, 0) if near else (0, 1, 2, 3, 4)
    mm(b3, "UA", 0, "A", C1 + 62, C1 + P, stop=False)
    mm(b3, "UB", 0, "A", R1B - 2, R1B + 128, start=False)
    cp(V("S1B", 0, 130), ps(b3, 0, 130))
    if near:
        mm(b2, "UB", 0, "A", R1B - 2, R1B + 128)
        mask("WMX", 64 - sh, "P%d" % b2, 2, 128)
    mm(b1, "UC", 0, "A", NEW2, NEW2 + 128)
    mask("WM1", 0, "P%d" % b1, 0, 64)
    if last:
        cp(ar(NEW2, NEW2 + 64), ps(b1, 0, 64))
    cp(W("UP1", 0, 4, HI), on(fold("WC1", "WM1", 64), LO))
    send(up, W("LUP1", 0, 4), W("UP1", 0, 4), "up1", "hi")
    if not hand:
        send2(down, "A", N2 + 64 + sh, "A", R2, 64 + sh, "c3", "all")
    if near:
        half(False, "A", C1 + 64, C1 + P)
        half(True, "A", R1B, R1B + 128)
        relu("TK", 256, 0, 128)
        half(False, "A", NEW2, NEW2 + P)
        quant("A", K1B, K1B + 128, V("TK", 1024, 1536))
        half(True, "A", R2, R2 + P)
        mm(7, "UA", 0, "A", NEW2, NEW2 + P, stop=False)
        mm(7, "UB", 0, "A", R2, R2 + P, start=False)
        tt(V("MC", 0, 128), V("P7", 64, P), V("S1B", 2, 130), A.is_le)
        cp(V("S2L", 0, 64), V("P7", 0, 64))
        relu("TK", 64, 0, P)
        mm(4, "UC", 0, "A", K1B, K1B + 128)
        keep(K1B, K1B + 128, V("P4", 0, 128))
        quant("A", K2, K2 + P, V("TK", 256, 1024))
        mm(4, "UC", 0, "A", K2, K2 + P)
        keep(K2, K2 + P, V("P4", 0, P))
    else:
        mm(b2, "UA", 0, "A", C1 + 64, C1 + P, stop=False)
        mm(b2, "UB", 0, "A", R2 + 64, R2 + P, start=False)
        tt(V("MC", 0, 128 - last), ps(b2, 0, 128 - last), V("S1B", 2, 130 - last), A.is_le)
        if last:
            cp(V("S2L", 0, 1), ps(b2, 127, 128))
        mm(b3, "UA", 0, "A", NEW2, NEW2 + 128, stop=False)
        mm(b3, "UB", 0, "A", R2, R2 + 128, start=False)
        cp(V("S2L", last, 64 + last), ps(b3, 0, 64))
        if last:
            tt(V("MA", 64, 65), ps(b3, 63, 64), V("S1B", 1, 2), A.is_le)
        mm(b2, "UC", 0, "A", K2 + 64, K1B + 128)
        cp(ar(K2 + 64, K1B + 128), ps(b2, 0, 256))
        for t in range(4):
            mm(t % 3, "W", 128 * t, "A", NEW2, NEW2 + 128, stop=False)
            mm(t % 3, "W", 128 * t + 512, "A", R2, R2 + 128, start=False)
            relu("TK", 64, 0, 64, t % 3 - t, t)
        quant("A", K2 - 64, K2 + 64, V("TK", 0, 512))
        mm(b2, "UC", 0, "A", K2, K2 + 128)
        cp(ar(K2, K2 + 64), ps(b2, 0, 64))
        mm(b3, "UB", 0, "A", R1B - 2, R1B + 128)
        mask("WMX", 64 - last, "P%d" % b3, 2 - last, 128)
    scan(V("CUM", 0, 128), V("MC", 0, 128), V("MC", 0, 128), A.add, A.max)
    scan(V("MCS", 0, 128), V("WG", 0, 128), V("MC", 0, 128), A.mult, A.add)
    ts(W("SUF", 0, 8), V("MCS", 15, 128, 16), V("Z2", 9, 10), A.mult)
    tt(W("AB", 0, 8), W("SUF", 0, 8), V("CUM", 15, 128, 16), A.add)
    tt(W("AB", 8, 16), W("AB", 0, 8), W("CW", 0, 8), A.subtract)
    if last:
        tt(W("AB", 16, 24), W("AB", 0, 8), W("Z2", 0, 8), A.add)
    ts(W("OCF", 0, 8), W("SUF", 0, 8), -200.0, A.is_le, float(K1B - 64 - K2), A.mult)
    tt(W("OCG", 0, 8), W("OCF", 0, 8), W("PW", 0, 8), A.add)
    cp(W("OC", 0, 8), W("OCG", 0, 8))
    gather(V("WMC", 0, 128), ar(K2 + 64, K1B + 128), W("OC", 0, 8), V("M4", 0, 128))
    tt(V("TA", 2, 48, 6), fold("WCC", "WMC", 128), W("AD", 4, 12), A.add)
    left = L7 if last else C1 - 64
    half(False, "A", left, left + 128, bl)
    mm(b4, "UA", 0, "A", left, left + 128, stop=False)

    mm(b4, "UB", 0, "A", N2 - 64, N2 + 64, start=False)
    half(True, "A", N2 - 64, N2 + 64, bl)
    bn = b2 if near else b3
    mm(bn, "UB", 0, "A", N2 - 64, N2 + 64)
    tt(V("MA", 0, 64), ps(b4, 64, 128), V("S2L", 0, 64), A.is_ge)
    ma, mn, nn = V("MA", last, 64 + last), V("MA", last, 65 + last), V("ONE", 8, 9)
    op("v", lambda q: q.tensor_reduce(ap(nn), ap(mn), AxisListType.X, A.add, negate=True), [mn], [nn, W("WM1", 0, 65)],
       alt=lambda q: q.activation(ap(W("WM1", 0, 65)), ap(mn), ACT.Identity, scale=-1.0, accum_out=ap(nn)))
    relu("TL", last, 64, 128, bl)
    if last:
        z = W("Z9", 0, 1)
        ts(z, W("EW2", 7, 8), V("MA", 0, 1), A.mult)
    tt(V("MK", 0, 64), ma, md, A.mult)
    if last:
        ts(V("AB", 7, 24, 8), V("AB", 7, 24, 8), z, A.add)
    scan(V("SC", 0, 64), V("INJ", 0, 64), V("MK", 0, 64), A.max, A.add)
    for k in range(2 + last):
        o, a = V("TW", k + k // 2, 48, 6), W("AB", 8 * k, 8 * k + 8)
        op("s", lambda q, o=o, a=a: q.activation(ap(o), ap(a), ACT.Sign, bias=ap(nn), scale=-1.0), [a, nn], [o])
    if last:
        ts(W("Z9", 2, 3), W("TW", 45, 46), S / 2, A.mult, S / 2, A.add)
    if sh:
        both(W("O3", 0, 4), V("SC", 15, 64, 16))
        cp(W("O3", 12, 13), W("O3", 0, 1))
    else:
        cp(W("O3", 0, 4), V("SC", 15, 64, 16))

    rows = LO if sh or last else None
    scan(W("SA1", 0, 48, rows), W("TW", 0, 48, rows), W("TA", 0, 48, rows), A.add, A.mult)
    scan(W("SB1", 0, 48, rows), W("TW", 0, 48, rows), W("TB", 0, 48, rows), A.add, A.mult)
    tt(W("UP2", 4, 12, rows), V("SB1", 1, 48, 6, rows), V("SA1", 2, 48, 6, rows), A.subtract)
    if rows:
        tt(W("U2S", 0, 8, rows), V("SB1", 1, 48, 6, rows), V("SA1", 2, 48, 6, rows), A.subtract)
        send(up, W("LUP2", 0, 8), W("U2S", 0, 8), "up2", "all")
    else:
        send(up, W("LUP2", 0, 8), W("UP2", 4, 12), "up2", "all")
    scan(V("TD", 0, 48), V("TW", 0, 48), V("R4", 0, 48), A.add, A.mult)
    if sh or last:
        mask("WMY", 0, "P%d" % bn, 65, 63)
        mask("WMY", 79, "P%d" % bn, 64, 1)
    else:
        mask("WMX", 0, "P%d" % bn, 64, 64)
    cp(W("O3", 4, 12), V("TD", 4, 48, 6))
    lq = LATE - 2 * last
    quant("A", lq, lq + 128, V("TL", 0, 512))
    mm(b4, "UC", 0, "A", lq, lq + 128)
    tt(V("WL", 0, 64 - last), ps(b4, 2 * last, 64 + last), V("MK", 0, 64 - last), A.mult)
    if last:
        ts(W("Z9", 4, 5), ps(b4, 1, 2), W("Z9", 2, 3), A.mult)
    scan(V("CL", 0, 64 + sh), V(rsg, 0, 64 + sh), V("WL", 0, 64 + sh), A.mult, A.add)
    mm(6, "U", 0, "A", NEW2, NEW2 + P)
    cp(V("Y", 0, P), V("P6", 0, P))
    dma("y", T.y[:, 0:P], T.Y[:, 0:P], [V("Y", 0, P)], [], store=True)
    ng = 13 if sh else 12 if last else 4
    end = min(16 * ng, P + 1)
    gather(V("WM3", 0, 16 * ng), V("AX" if sh else "AR", 0, OEND - OWN), W("O3", 0, ng), mg[:2] + (mg[1] + 16 * ng, 1, None))
    scan(V("WC3", 0, end), V(rsg, 0, end), V("WM3", 0, end), A.mult, A.add)
    tt(W("UP2", 0, min(ng, 12), HI), V("WC3", 15 + sh, end, 16, HI), W("AD", 0, min(ng, 12), HI), A.add)
    tt(W("UP2", 0, 4, HI), W("UP2", 0, 4, HI), V("CL", 15 + sh, 64 + sh, 16, HI), A.add)
    if sh or last:
        ts(W("UP2", 11, 12, HI), W("UP2", 11, 12, HI), W("CL", 0, 1, HI) if sh else W("Z9", 4, 5, HI), A.add)
    o3 = third("LD", 2)
    cp(o3, W("O3"))
    if sh:
        cp(third("XD", 1, LO), V("WC3", 16, P + 1, 16, LO))
    else:
        ts(third("XD", 1), W("O3"), float(OWN), A.add)
    if sh or last:
        fold("WCX", "WMX", 144, 48)
        fold("WCY", "WMY", 80)
        cp(W("S2D", 0, 3, HI), W("LUP1", 0, 3, HI))
        tt(W("S2D", 3, 4, HI), V("WCX", 63, 64, 1, HI), W("LUP1", 3, 4, HI), A.add)
        tt(W("S2D", 4, 12, HI), V("WCX", 79, P, 16, HI), W("AD", 4, 12, HI), A.add)
        tt(W("S2D", 0, 4, HI), W("S2D", 0, 4, HI), V("WCY", 15, 64, 16, HI), A.add)
        ts(W("S2D", 11, 12, HI), W("S2D", 11, 12, HI), V("WCY", 79, 80, 1, HI), A.add)
    else:
        fold("WCX", "WMX", 64)
        fold("WCX", "WMX", 128, 64)
        tt(W("S2D", 0, 4, HI), V("WCX", 15, 64, 16, HI), W("LUP1", 0, 4, HI), A.add)
        tt(W("S2D", 4, 12, HI), V("WCX", 79, P, 16, HI), W("AD", 4, 12, HI), A.add)
    s1d, s2d = W("UP2", rows=HI), W("S2D", rows=HI)
    tt(W("DN", rows=LO), s1d, s2d, A.min)
    tt(W("DN", rows=HI), s2d, s1d, A.is_ge)
    send(down, W("LDN"), W("DN"), "dn", "all")
    tt(third("XF", 1, LO), s2d, s1d, A.is_lt)
    tt(V("XF", 14, 36, 3, LO), W("LUP2", 0, 8, LO), W("DN", 4, 12, LO), A.is_ge)
    scan(W("XS", 0, 36, LO), W("XF", 0, 36, LO), W("XD", 0, 36, LO), A.mult, A.max)
    both(W("OS"), third("XS", 2))
    pick("S", 0, "A", 0, N2 + 64, W("OS"))
    send2(down, "R", 0, "S", 0, P, "f4", "all")
    pick("K", K3, "A", OWN, OEND, W("O3", 0, 4))
    dma("y", T.sp[0:1, 0:P], T.SP2[0:1, 0:P], [V("SP2", 0, P), V("QR", 0, P)], [], store=True, busy=0.03)
    lv, cv = K3 - 64, N2 + 2 * last
    if last:
        pick("K", lv, "A", OWN, OEND, W("O3", 8, 12))
    mm(6, "UA", 0, "K", lv, lv + 128, stop=False)
    mm(6, "UB", 0, "A", cv, cv + 128, start=False)
    mask("WS", 0, "P6", 64, 64)
    if last:
        mask("WS", 79, "P6", 63, 1)
    fold("CS", "WS", 64 + 16 * last)
    half(False, "K", lv, lv + 128, 4)
    half(True, "A", cv, cv + 128, 4)
    relu("T3", 0, 64 - last, 128, 4)
    quant("K", CD, CD + 128, V("T3", 0, 512))
    if last:
        pick("K", CD + 97, "A", OWN, OEND, W("O3", 10, 12))
        ts(W("S3X", 0, 1, LO), W("UP2", 11, 12, LO), W("NE", 0, 1, LO), A.mult, V("CS", 79, 80, 1, LO), A.add)
    pick("K", K3 + 64, "A", OWN, OEND, W("O3", 4, 12))
    mm(4, "U", 0, "K", K3, K3 + P)
    cp(V("Y", P, 2 * P), V("P4", 0, P))
    dma("y", T.y[:, P:2 * P], T.Y[:, P:2 * P], [V("Y", P, 2 * P), V("QR", 0, P)], [], store=True)
    lf = W("LF", 0, 36, LO)
    cp(third("LF", 1, LO), W("LDN", rows=HI))
    tt(V("LF", 2, 12, 3, LO), V("CS", 15, 64, 16, LO), W("LDN", 0, 4, LO), A.is_ge)
    tt(V("LF", 14, 36 - 3 * last, 3, LO), W("UP2", 4, 12 - last, LO), W("LDN", 4, 12 - last, LO), A.is_ge)
    pw = "PW"
    if last:
        pw = "PWX"
        tt(W("LF", 35, 36, LO), W("S3X", 0, 1, LO), W("LDN", 11, 12, LO), A.is_ge)
        ts(W("ZM", 0, 1, LO), W("LF", 35, 36, LO), float(P - 1 - CD), A.mult, float(CD - P + 1), A.add)
        ts(W("PWX", 11, 12, LO), W("ZM", 0, 1, LO), W("EW", 11, 12, LO), A.mult, W("PW", 11, 12, LO), A.add)
    ts(W("ZL", 0, 4, LO), V("LF", 2, 12, 3, LO), -float(CD + last), A.mult, float(CD + last), A.add)
    tt(W("OFS", 0, 4, LO), W("ZL", 0, 4, LO), W("PW", 0, 4, LO), A.add)
    both(W("OF", 0, 4), W("OFS", 0, 4))
    scan(W("VS", 0, 36, LO), lf, W("TV", 0, 36, LO), A.mult, A.add)
    scan(W("LS", 0, 36, LO), lf, W("LD", 0, 36, LO), A.mult, A.max)
    both(W("OL"), third("LS", 2))
    pick("L", 0, "A", OWN, OEND, W("OL"))
    half(False, "L", 0, P)
    scan(W("IS", 0, 36, LO), lf, W("TI", 0, 36, LO), A.mult, A.add)
    scan(W("KS", 0, 36, LO), lf, W("TS", 0, 36, LO), A.mult, A.add)
    tt(W("X1"), o3, W("K2W"), A.is_equal)
    tt(W("X2"), o3, W("C2B"), A.not_equal)
    tt(W("SPW"), W("X1"), W("X2"), A.add)
    flip(W("VT", 0, 32, LO), V("VS", 2, 96, 3, LO))
    scan(W("PR", 0, 32, LO), W("RST", 0, 32, LO), W("VT", 0, 32, LO), A.mult, A.add)
    ts(W("PR", 32, 64, LO), W("PR", 0, 32, LO), -1.0, A.mult, W("PR", 15, 16, LO), A.add)
    flip(W("PT", 0, 64, LO), W("PR", 0, 64, LO))
    scan(W("CU4", rows=LO), W("PT", 31, 43, LO), W("PT", rows=LO), A.add, A.add, float(CAP * 65793))
    tt(W("QI", rows=LO), W("CU4", rows=LO), third("IS", 2, LO), A.mult)
    ts(W("QI2", rows=LO), W("QI", rows=LO), K3, A.bitwise_and)
    tt(W("OFS", 4, 12, LO), W("QI2", 4, 12, LO), W(pw, 4, 12, LO), A.add)
    both(W("OF", 4, 12), W("OFS", 4, 12))
    ts(W("T4F", rows=LO), W("QI2", rows=LO), -1.0 / K3, A.mult, 1.0, A.add)
    tt(W("SPW", 12, 24, LO), W("T4F", rows=LO), third("KS", 2, LO), A.mult)
    flip(W("SPT", 0, 32, (0, 32)), W("SPW", 0, 32, (0, 32)))

    half(True, "R", 0, P)
    relu("T4", 0, 0, P)
    quant("K", 0, P, V("T4", 0, 4 * P))
    pick("O", 64, "K", 0, KEND, W("OF", 4, 12))
    mm(5, "U", 0, "O", 64, P)
    pick("O", 0, "K", 0, KEND, W("OF", 0, 4))
    mm(4, "U", 0, "O", 0, 128)
    dma("y", T.oc[:, :], T.QO[:, 0:P].bitcast(dt.uint8), [V("QO", 0, P)], [], store=True)
    for k in range(4):
        dma("ys"[k % 2], T.osc[4 * k:4 * k + 4, :], T.SO[32 * k:32 * k + 4, 0:P], [V("SO", 0, P)], [], store=True, busy=0.03)
    cp(V("Y", 2 * P, 2 * P + 64), V("P4", 0, 64))
    cp(V("Y", 2 * P + 64, 3 * P), V("P5", 0, 128))
    dma("y", T.y[:, 2 * P:3 * P], T.Y[:, 2 * P:3 * P], [V("Y", 2 * P, 3 * P)], [], store=True)
    dma("s", T.sp[0:1, P:3 * P], T.SPT[0:24, 0:16], [V("SPT", 0, 32)], [], store=True, busy=0.06)
    return ops
